import numpy as np, ml_dtypes
CORES = [23,119,17,113]
N = 4
BF = ml_dtypes.bfloat16
def gentries(a):
    return np.ascontiguousarray(a.reshape(8, 16, -1).transpose(0, 2, 1)).reshape(8, -1)
def gtable(e):
    e = np.asarray(e); return np.ascontiguousarray(e.reshape(8, -1, 16).transpose(0, 2, 1)).reshape(128, -1).astype(np.int32)
B, L, S, T, TH = 2560, 256, 128, 4, 1240
W = B + 2 * S * T
def pack(kb, ch, q, hv):
    return {"kb": np.ascontiguousarray(kb.reshape(N, 128, B)).astype(np.float32).astype(BF), "ch": np.ascontiguousarray(ch.reshape(N, 128, B)).astype(np.int32),
            "qs": np.ascontiguousarray(q.reshape(N, 128, L)).astype(np.float32).astype(BF), "hv": np.stack([gtable(a.reshape(8, -1)) for a in hv])}
def nodes(rng, pop, n):
    often = np.take_along_axis(pop, rng.integers(0, pop.shape[2], (N, 8, n)), 2)
    return np.where(rng.random((N, 8, n)) < 0.5, often, rng.integers(1, B, (N, 8, n)))
def abroad(h):
    return np.stack([np.roll(h[:, :, t], -t, axis=0) for t in range(T)], axis=2)
def setup_inputs(rng):
    pop = rng.integers(1, B, (N, 8, B // 4)); kb = rng.integers(0, 256, (N, 8, 16, B))
    ch = nodes(rng, pop, 16 * B).reshape(N, 8, 16, B)
    none = rng.choice(np.array([0.03, 0.1, 0.2, 0.3]), (N, 8, 1, 1)); none = np.where(rng.random((N, 8, 1, B)) < 0.02, 1.0, none)
    ch = np.where(rng.random(ch.shape) < none, 0, ch)
    q = rng.integers(0, 256, (N, 8, 16, L)); edge = rng.integers(0, 41, q.shape); edge = np.where(rng.random(q.shape) < 0.5, edge, 255 - edge)
    q = np.where(rng.random((N, 8, 1, L)) < 0.125, edge, q)
    return pack(kb, ch, q, abroad(nodes(rng, pop, T * L).reshape(N, 8, T, L)))
def setup_inputs_spread(rng):
    kb = (np.exp2(8 * rng.random((N, 8, 1, B))) * rng.random((N, 8, 16, B))).astype(np.int64)
    q = (np.exp2(8 * rng.random((N, 8, 1, L))) * rng.random((N, 8, 16, L))).astype(np.int64)
    ch = 1 + ((B - 1) * rng.random((N, 8, 16, B)) ** 2).astype(np.int64)
    ch = np.where(rng.random(ch.shape) < rng.random((N, 8, 1, B)) ** 2, 0, ch)
    hv = 1 + ((B - 1) * rng.random((N, 8, T, L)) ** 2).astype(np.int64)
    return pack(np.minimum(kb, 255), np.minimum(ch, B - 1), np.minimum(q, 255), np.minimum(hv, B - 1))
def setup_inputs_ends(rng):
    d = rng.choice(np.array([0.08, 0.15, 0.5, 0.9]), (N, 8, 1, B), p=np.array([0.4, 0.3, 0.1, 0.2])); kb = 255 * (rng.random((N, 8, 16, B)) < d).astype(np.int64)
    d = rng.choice(np.array([0.08, 0.2, 0.5, 0.9]), (N, 8, 1, L), p=np.array([0.4, 0.3, 0.15, 0.15])); q = 255 * (rng.random((N, 8, 16, L)) < d).astype(np.int64)
    u = rng.random((N, 8, 16, B)); ch = np.where(u < 0.42, 0, np.where(u < 0.64, B - 1, rng.integers(2, B - 1, u.shape)))
    end = rng.random((N, 8, T, L)) < np.where(np.arange(L) < S, 0.35, 0.95)
    hv = np.where(end, np.where(rng.random(end.shape) < 0.5, 1, B - 1), rng.integers(2, B - 1, end.shape))
    kb[..., 1] = 255; kb[..., B - 1] = 255; kb[..., 2] = 0; kb[..., B - 2] = 0; row = np.arange(16)
    ch[..., 1] = np.where(row == 0, 0, np.where(row % 2 == 1, B - 1, 1)); ch[..., 2] = np.where(row % 2 == 1, B - 2, 2)
    q[..., 0] = 0; q[..., L - 1] = 255; q[..., L - 2] = 0; q[..., L - 3] = 0; q[..., L - 4] = 255
    hv[:, :, 0, 0] = 1; hv[:, :, 0, L - 2:] = 1; hv[:, :, 0, L - 4:L - 2] = 2
    return pack(kb, ch, q, hv)
def setup_inputs_corners(rng):
    kb = rng.integers(0, 61, (N, 8, 16, B)); q = rng.integers(0, 61, (N, 8, 16, L)); ch = np.zeros((N, 8, 16, B), np.int64)
    hv = rng.integers(1, B, (N, 8, T, L)); hv[..., 0] = 1; hv[..., L - 1] = B - 1; v = np.arange(B)
    for r in range(N):
        for g in range(8):
            k = (g + r) % 8; c = ch[r, g]; some = rng.integers(1, B, (16, B))
            if k == 0: c[:] = v
            elif k == 2: c[15] = some[15]
            elif k == 3: c[14] = some[14]
            elif k == 4: c[0] = some[0]
            elif k == 5: c[:] = np.where(some % 2 == 0, 1, B - 1)
            elif k == 6: c[rng.integers(0, 16, B), v] = np.where(v < B - 1, v + 1, 1)
            elif k == 7:
                c[:] = some; kb[r, g] = rng.integers(0, 256, (16, B)); q[r, g] = rng.integers(0, 256, (16, L))
    return pack(kb, ch, q, hv)
def setup_inputs_crowd(rng):
    kb = rng.integers(200, 256, (N, 8, 16, B)); q = rng.integers(0, 61, (N, 8, 16, L)); hv = rng.integers(1, B, (N, 8, T, L))
    ch = np.where(rng.random((N, 8, 16, B)) < 0.5, 0, rng.integers(1, B, (N, 8, 16, B)))
    plan = np.zeros((N, 8, 4 * S + 3), np.int64); cuts = np.zeros(N, np.int64); i = np.arange(S)
    for r in range(N):
        for g in range(8):
            o = rng.permutation(np.arange(1, B))
            for place, node in ((2 * S - 1, B - 1), (3 * S - 2, 1)):
                w = int(np.argmax(o == node)); o[w] = o[place]; o[place] = node
            ring = o[:4 * S]; z, y, w = [int(a) for a in o[4 * S:4 * S + 3]]; far = o[4 * S + 3:]; plan[r, g] = o[:4 * S + 3]
            kg = kb[r, g]; cg = ch[r, g]
            kg[:, ring] = rng.integers(0, 61, (16, 4 * S)); kg[:, y] = 5
            cg[:, ring] = np.where(rng.random((16, 4 * S)) < 0.5, 0, far[rng.integers(0, far.size, (16, 4 * S))])
            row = rng.integers(0, 15, 4 * S); row[S] = 0; row[S + 1] = 14; row[2 * S] = 14; row[2 * S + 1] = 0
            cg[row, ring] = np.roll(ring, -S)
            cg[:, [z, y, w]] = 0; cg[int(rng.integers(0, 16)), z] = y
            m = 0 if r == 0 else (1 if g == 7 else 0) if r == 1 else (g + r) % 8
            chain = i + 0; stage = 0 * i; n = S
            if m == 1: chain[1] = 0; n = S - 2
            elif m == 2: chain = 0 * i + S - 1; n = 0
            elif m == 3: chain = 0 * i; chain[S - 1] = S - 1; n = 0
            elif m == 4: chain = 0 * i; chain[S - 2] = S - 2; chain[S - 1] = S - 1; n = 2
            elif m == 5: chain = i % 4; n = 4
            elif m == 6: chain = i - i % 2; stage = 2 * (i % 2)
            elif m == 7: chain = i - i % 2; stage = 3 * (i % 2); n = 0
            hv[r, g, 0, :S] = ring[stage * S + chain]; hv[r, g, 0, S:] = ring[rng.integers(0, 4 * S, L - S)]
            cuts[r] += n
    for t in range(1, T):
        near = np.take_along_axis(np.roll(plan, -t, axis=0), rng.integers(0, 4 * S, (N, 8, L)), 2)
        hv[:, :, t] = np.where(rng.random((N, 8, L)) < 0.75, near, hv[:, :, t])
    then = np.roll(plan, -1, axis=0)
    for e in range(3):
        hv[:, :, 0, L - 6 + e] = plan[:, :, 4 * S]; hv[:, :, 0, L - 3 + e] = plan[:, :, 4 * S + 2]; hv[:, :, 1, L - 3 + e] = then[:, :, 4 * S]
        for r in range(N):
            for lane, s in ((L - 6 + e, TH + e - 1), (L - 3 + e, TH + (int(cuts[(r + 1) % N]) & 63) + e - 1)):
                q[r, :, :, lane] = 5 + s // 16 + (np.arange(16) < s % 16).astype(np.int64)
    return pack(kb, ch, q, hv)
def check_inputs(d):
    bad = []
    for k, lo, hi in (("kb", 0, 255), ("ch", 0, B - 1), ("qs", 0, 255), ("hv", 1, B - 1)):
        v = np.asarray(d[k]).astype(np.float32)
        if not np.all((v >= lo) & (v <= hi)): bad.append("range of " + k)
        elif np.any(v != np.floor(v)): bad.append("whole numbers in " + k)
    return bad
def reference(kb, ch, qs, hv):
    c = np.zeros((N, 8, 16, W), np.int64); c[..., :B] = ch.reshape(N, 8, 16, B)
    K = np.zeros((N, 8, 16, W), np.int32); K[..., :B] = kb.astype(np.float32).astype(np.int32).reshape(N, 8, 16, B)
    q = qs.astype(np.float32).astype(np.int32).reshape(N, 8, 16, L); p = np.zeros((N, 8, 16, L), np.int32)
    h = np.stack([gentries(a) for a in hv]).astype(np.int64).reshape(N, 8, T, L)
    A = [0] * N; row = np.arange(16)[None, :]; lower = np.tril(np.ones((S, S), bool), -1); twin = np.arange(S) ^ 1
    for t in range(T):
        for x in range(N):
            o = (x - t) % N; C = c[x]; Kx = K[x]; Q = q[o][:, :, None, :]; P = p[o]; v = h[o, :, t]
            never = np.ones((8, L), bool); at = [v]; by = []
            for step in range(3):
                kids = np.take_along_axis(C, v[:, None, :], 2)
                key = np.take_along_axis(Kx, kids.reshape(8, 1, 16 * L), 2).reshape(8, 16, 16, L)
                y = np.abs(P[:, :, None, :] - key)
                s = np.where(kids == 0, 2 ** 20, np.add.reduce(np.abs(y - Q), axis=1))
                k = np.argmin(s, axis=1)
                go = np.take_along_axis(s, k[:, None, :], 1)[:, 0] <= TH + A[x]
                v = np.where(go, np.take_along_axis(kids, k[:, None, :], 1)[:, 0], v)
                P = np.where(go[:, None, :], np.take_along_axis(y, k[:, None, None, :], 2)[:, :, 0], P)
                never = never & go; at.append(v); by.append(k)
            p[o] = P
            a, b, j, k = at[1][:, :S], at[2][:, :S], by[1][:, :S], by[2][:, :S]
            can = never[:, :S] & (a != b) & (j < 15)
            two = np.stack([a, b], axis=-1)
            meet = np.any(two[:, :, None, :, None] == two[:, None, :, None, :], axis=(3, 4))
            stand = can & ~np.any(meet & lower & can[:, None, :], axis=2)
            g, i = np.nonzero(stand & stand[:, twin])
            a, b, j, k = a[g, i], b[g, i], j[g, i], k[g, i]; every = np.arange(len(g))
            m = B + 2 * S * t + 2 * i; n = m + 1; other = B + 2 * S * t + 2 * (i ^ 1)
            ra = C[g, :, a]; rb = C[g, :, b]
            ua = row > j[:, None]; ub = row > k[:, None]
            rm = np.where(ua, ra, 0); rm[every, j] = n
            na = np.where(ua, 0, ra); na[every, j + 1] = other
            C[g, :, a] = na; C[g, :, b] = np.where(ub, 0, rb); C[g, :, m] = rm; C[g, :, n] = np.where(ub, rb, 0)
            if t < T - 1:
                Kx[g, :, m] = Kx[g, :, a]; Kx[g, :, n] = Kx[g, :, b]
            A[x] = len(g) & 63
    return {"yc": c.reshape(N, 128, W).astype(np.float32), "yp": p.reshape(N, 128, L).astype(np.float32).astype(BF)}

@@ -1,0 +1,621 @@
+import math
+from concourse.bass import DstId, RemoteDMATransfer
+from concourse.mybir import AluOpType, ActivationFunctionType
+
+N, B, L, NT, TH = 4, 2560, 256, 4, 1240
+W = B + 256 * NT
+WD = W + 256
+KNONE = 640.0
+BASE = 3.5
+TYPES = "SRXX XSRX SXRX SRXX XSRX SXRX"
+ORDER = "A0 B0 A1 B1 e A2 m B2 l"
+ORDERL = "A0 B0 A1 e B1 A2 m l B2"
+TYPES0 = "ZYZY"
+DIRECT = 2
+NLOAD = 4
+NS = 2
+H = L // NS
+Y = 16 * H
+GF, PEF = 1.56, 0.5
+
+f32, bf, f16, i32, u16 = "float32", "bfloat16", "float16", "int32", "uint16"
+SCRATCH = {}
+for _n, _c, _d in [
+    ("chi", B, i32), ("chf", WD, f32), ("cho", WD, f32), ("key", W, bf), ("ch0", 4, f32), ("qraw", L, bf), ("hvi", 64, i32), ("hvu", 64, u16),
+    ("qT0", L, bf), ("qT1", L, bf), ("qT2", L, bf), ("qT3", L, bf), ("hl1", 16, u16), ("hl2", 16, u16), ("hl3", 16, u16),
+    ("tab", Y + 2048, bf), ("eq", 2048, bf), ("mask", 512, bf), ("pe0", 512, bf), ("pe1", 512, bf), ("pe2", 512, bf),
+    ("rl0", 512, bf), ("rl1", 512, bf), ("rl2", 512, bf), ("rl3", 512, bf), ("kr0", 512, bf), ("kr1", 512, bf), ("kr2", 512, bf),
+    ("ku", 256, u16), ("kc", 256, f32), ("vl0", 16, u16), ("vl1", 16, u16),
+    ("sc", 256, f32), ("oi", 16, i32), ("oj", 16, i32), ("ou", 16, u16), ("sela", 384, f16), ("selb", 128, f16), ("rst0", 128, f32), ("rst1", 128, f32),
+    ("ps", 1024, bf), ("pl", 1024, bf),
+    ("ones", 128, bf), ("idb", 128, bf), ("nid", 128, bf), ("two", 128, bf), ("idh", 128, f16), ("six", 128, bf),
+    ("bgb", 144, bf), ("bgh", 144, f16), ("og", 240, bf), ("gp", 1024, f16), ("gn", 1024, f16), ("bsh", 24, f16), ("boh", 128, f16),
+    ("tle", 128, bf), ("tgt", 128, bf), ("tsh", 128, bf), ("sth", 128, f16),
+    ("ci", 8, i32), ("cf", 12, f32), ("w1", 144, f32), ("w2", 144, f32), ("w3", 128, f32), ("wi", 128, i32),
+    ("whi", 128, f32), ("wlo", 128, f32), ("mt", 512, f32), ("ni", 512, f32), ("dum", 16, f32), ("rb", 8, f32),
+    ("uh", 256, f16), ("db", 4096, bf), ("eqw", 4096, bf), ("oh", 256, bf), ("rr", 256, f32), ("t1", 256, f32), ("t4", 256, f32),
+    ("t2", 128, f32), ("t3", 128, f32), ("pre", 24, f32), ("wc", 16, f32), ("hi", 128, bf), ("lo", 128, bf), ("st", 128, bf),
+    ("fl", 128, bf), ("ab", 16, f32), ("da", 16, f32), ("of", 16, f32), ("og2", 16, f32), ("so", 16, u16),
+    ("zj", 128, f32), ("zc", 4, f32), ("zi", 4, i32), ("zk", 4, i32), ("za", 4, f32),
+]:
+    SCRATCH[_n] = ("sbuf", [128, _c], _d)
+SCRATCH["fa"] = ("sbuf", [128, 16, 16, 16], bf)
+for _n in range(NS):
+    SCRATCH["wd%d0" % _n] = ("sbuf", [128, 2 * Y], bf)
+    SCRATCH["wd%d1" % _n] = ("sbuf", [128, 2 * Y], bf)
+PSUM = ["E0", "E1", "E2", "E3", "W0", "W1", "XB", "FB"]
+POOL = {"E": ["E0", "E1", "E2", "E3"], "W": ["W0", "W1"], "pe": ["pe0", "pe1", "pe2"], "rl": ["rl0", "rl1", "rl2", "rl3"], "kr": ["kr0", "kr1", "kr2"]}
+SLACK = 40
+BETA = 1000
+SEED, NOISE = 816, 1000
+
+
+def isps(nm):
+    return nm in PSUM or nm[:2] in ("E#", "W#")
+
+
+for _n in PSUM:
+    SCRATCH[_n] = ("psum", [128, 512], f32)
+SEMAPHORES = (["sV", "sS", "sP", "sG", "ls"] + ["d%d" % k for k in range(24)] + ["aq%d" % t for t in range(1, 4)]
+              + ["ap%d" % k for k in range(4 * NS)])
+OP = AluOpType
+FN = ActivationFunctionType
+
+
+def build(g, core, T, topo, rank, phys):
+    nodes = []
+    V, S, P = g.vector, g.scalar, g.tensor
+
+    def A(name, lo=0, hi=None, step=1):
+        b = phys.get(name, name.split("#")[0] + "0") if "#" in name else name
+        if hi is None:
+            hi = SCRATCH[b][1][1]
+        ap = T[b][:, lo:hi] if step == 1 else T[b][:, lo:hi:step]
+        n = (hi - lo + step - 1) // step
+        return (ap, [(name, lo, lo + (n - 1) * step + 1)], n, SCRATCH[b][2], 0)
+
+    def IND(win, off):
+        return (win[0].indirect(off[0]), win[1] + off[1], 16 * off[2], win[3], 1)
+
+    def F4(a, b, ilo=None):
+        name = "fa"
+        ap = T[name][:, a:b, :, :] if ilo is None else T[name][:, a:b, ilo, :]
+        return (ap, [(name, 256 * a, 256 * b)], (b - a) * (256 if ilo is None else 16), bf, 0)
+
+    def node(eng, emit, rd, wr, cost, **kw):
+        d = {"eng": eng, "emit": emit, "rd": [r for x in rd for r in x[1]], "wr": [r for x in wr for r in x[1]], "cost": cost}
+        d.update(kw)
+        nodes.append(d)
+        return len(nodes) - 1
+
+    def two_b(*xs):
+        return all(x[3] in (bf, f16, u16) for x in xs)
+
+    def rate(o, i, base):
+        if o[4]:
+            return 3.5
+        return GF if i[4] else base
+
+    def split_out(o):
+        return ((None, o[1][:1]), (None, o[1][1:])) if o[4] else (o, (None, []))
+
+    def val(x):
+        return x[0] if isinstance(x, tuple) else x
+
+    def cols(*xs):
+        return [x for x in xs if isinstance(x, tuple)]
+
+    def cp(o, i):
+        w, r = split_out(o)
+        node("V", lambda: V.tensor_copy(o[0], i[0]), [i, r], [w], 60 + i[2] * rate(o, i, .5 if two_b(o, i) else 1))
+
+    def ts(o, i, s1, op0, s2=None, op1=None):
+        if op1 is None:
+            em = lambda: V.tensor_scalar(o[0], i[0], val(s1), None, op0)
+        else:
+            em = lambda: V.tensor_scalar(o[0], i[0], val(s1), val(s2), op0, op1)
+        node("V", em, [i] + cols(s1, s2), [o], 60 + i[2] * rate(o, i, .5 if two_b(o, i) else 1))
+
+    def tt(o, a, b, op):
+        w, r = split_out(o)
+        ps = isps(a[1][0][0]) or isps(b[1][0][0])
+        node("V", lambda: V.tensor_tensor(o[0], a[0], b[0], op), [a, b, r], [w], 60 + a[2] * rate(o, a, 1 if ps else 2))
+
+    def ms(o, c):
+        node("V", lambda: V.memset(o[0], c), [], [o], 60 + o[2] * (.5 if two_b(o) else 1))
+
+    def scan(o, d0, d1, op0, op1):
+        node("V", lambda: V.tensor_tensor_scan(o[0], d0[0], d1[0], 0.0, op0, op1), [d0, d1], [o],
+             60 + o[2] * (.5 if two_b(o, d0, d1) else 1))
+
+    def act(o, i, fn, scale=1.0, acc=None, bias=None):
+        if bias is not None:
+            node("S", lambda: S.activation(o[0], i[0], fn, bias=bias[0]), [i, bias], [o], 75 + i[2] * rate(o, i, 1))
+            return
+        if acc is None:
+            em = lambda: S.activation(o[0], i[0], fn, scale=scale)
+        else:
+            em = lambda: S.activation(o[0], i[0], fn, scale=scale, accum_out=acc[0])
+        node("S", em, [i], [o] + cols(acc), 75 + i[2] * rate(o, i, 1))
+
+    def mm(lst):
+        def em():
+            r = None
+            for o, l, x, a, b in lst:
+                r = P.matmul(o[0], l[0], x[0], a, b)
+            return r
+        node("P", em, [e[1] for e in lst] + [e[2] for e in lst], [e[0] for e in lst], 30 + PEF * sum(max(64, e[2][2]) for e in lst))
+
+    def acc(o, pairs):
+        return [(o, l, x, k == 0, k == len(pairs) - 1) for k, (l, x) in enumerate(pairs)]
+
+    def iota(o, pat, base, cm):
+        if o[3] == i32:
+            em = lambda: g.iota(o[0], pat, base, cm)
+        else:
+            em = lambda: g.iota(o[0], pat, base, cm, allow_small_or_imprecise_dtypes=True)
+        node("G", em, [], [o], 160 + 2 * o[2])
+
+    def asel(o, i, pat, op, base, cm):
+        node("G", lambda: g.affine_select(o[0], i[0], pat, op, 0.0, base, cm), [i], [o], 200 + 2 * o[2])
+
+    ndma = [0]
+
+    def dma(q, o, i, rd, wr, lat):
+        sem = T.sem["d%d" % ndma[0]]
+        ndma[0] += 1
+        e = g.sync if q == "Y" else g.scalar
+        node(q, lambda: e.dma_start(o, i).then_inc(sem, 16), rd, wr, 60, sem=sem, cnt=16, lat=lat)
+
+    sent = [0]
+
+    def peer(k):
+        return T.cores[(rank + k) % N]
+
+    dma("Y", T.hvi[:], T.hv[:], [], [A("hvi")], 2500)
+    dma("S", T.qraw[:], T.qs[:], [], [A("qraw")], 2500)
+    cw = B // NLOAD
+    for k in range(NLOAD):
+        dma("Y", T.chi[:, k * cw:(k + 1) * cw], T.ch[:, k * cw:(k + 1) * cw], [], [A("chi", k * cw, (k + 1) * cw)], 3000 + 1300 * (k + 1))
+    dma("S", T.key[:, 0:B], T.kb[:], [], [A("key", 0, B)], 9500)
+    cp(A("hvu"), A("hvi"))
+    for k in range(NLOAD):
+        cp(A("chf", k * cw, (k + 1) * cw), A("chi", k * cw, (k + 1) * cw))
+        if k == 0:
+            cp(A("ch0", 0, 1), A("chi", 0, 1))
+            ms(A("chf", 0, 1), 0.0)
+    ms(A("key", 0, 1), KNONE)
+
+    ms(A("ones"), 1.0)
+    iota(A("ci", 0, 1), [[0, 1]], 0, 1)
+    asel(A("idb"), A("ones"), [[-1, 128]], OP.is_equal, 0, 1)
+    ts(A("ci", 1, 2), A("ci", 0, 1), 15, OP.bitwise_and)
+    ts(A("ci", 2, 3), A("ci", 0, 1), 112, OP.bitwise_and)
+    cp(A("cf", 0, 3), A("ci", 0, 3))
+    pc, rowc, g16 = A("cf", 0, 1), A("cf", 1, 2), A("cf", 2, 3)
+    ms(A("cf", 7, 8), -2048.0)
+    ms(A("cf", 8, 9), 2048.0)
+    ms(A("tab", Y, Y + 2048), -2048.0)
+    for k in range(2):
+        asel(A("eq", 1024 * k, 1024 * k + 1024), A("tab", Y, Y + 1024), [[1, 64], [0, 16]], OP.is_equal, 64 * k, -1)
+    iota(A("w1"), [[1, 144]], 0, 0)
+    ts(A("w2"), A("w1"), g16, OP.subtract)
+    ts(A("bgb"), A("w2"), 15.0, OP.is_equal, 4096.0, OP.mult)
+    cp(A("bgh"), A("bgb"))
+    ts(A("w3", 0, 16), A("w1", 0, 16), rowc, OP.is_equal, 6144.0, OP.mult)
+    ts(A("tab", 0, 16), A("w3", 0, 16), -2048.0, OP.add)
+    n = 16
+    while n < Y:
+        cp(A("tab", n, 2 * n), A("tab", 0, n))
+        n *= 2
+    act(A("nid"), A("idb"), FN.Copy, -1.0)
+    act(A("two"), A("idb"), FN.Copy, 2.0)
+    act(A("six"), A("ones"), FN.Copy, 1.0 / 16)
+    cp(A("idh"), A("idb"))
+    ms(A("mask"), 1.0)
+    ms(A("mask", 0, 512, 16), 0.0)
+    ms(A("wd00", Y, 2 * Y), 0.0)
+    for k in range(1, 2 * NS):
+        act(A("wd%d%d" % (k % NS, k // NS), Y, 2 * Y), A("wd00", Y, 2 * Y), FN.Copy)
+    iota(A("wi"), [[256, 8], [1, 16]], 0, 16)
+    ts(A("cf", 3, 4), g16, 16.0, OP.mult)
+    ts(A("sth"), A("wi"), A("cf", 3, 4), OP.subtract)
+    ts(A("rb"), A("sth", 0, 128, 16), float(4096 * TH + Y), OP.add)
+    ms(A("rst0"), 0.0)
+    ms(A("rst1"), 0.0)
+    cp(A("rst0", 0, 128, 16), A("rb"))
+    ts(A("dum", 0, 8), A("sth", 0, 128, 16), 1.0 / 16, OP.mult, float(W), OP.add)
+    ts(A("dum", 8, 16), A("dum", 0, 8), 128.0, OP.add)
+    for h in range(2):
+        mm([(A("XB", 128 * h, 128 * h + 128), A("qraw", 128 * h, 128 * h + 128), A("idb"), True, True)])
+    act(A("qT0"), A("XB", 0, 256), FN.Copy, 1.0 / 2048)
+    ts(A("w3"), A("w2", 0, 128), 0.0, OP.is_ge)
+    ts(A("zj"), A("w2", 0, 128), 16.0, OP.is_lt)
+    tt(A("boh"), A("w3"), A("zj"), OP.mult)
+    ts(A("zj"), A("w1", 0, 128), pc, OP.is_le)
+    tt(A("tle"), A("w3"), A("zj"), OP.mult)
+    tt(A("tgt"), A("boh"), A("tle"), OP.subtract)
+    ts(A("zj"), A("w1", 0, 128), -1.0, OP.add, pc, OP.is_equal)
+    tt(A("tsh"), A("boh"), A("zj"), OP.mult)
+    cp(A("bsh", 0, 8), A("boh", 0, 128, 16))
+    ts(A("bsh", 8, 16), A("boh", 0, 128, 16), -1.0, OP.mult)
+    ts(A("cf", 4, 5), rowc, 15.0, OP.is_equal)
+    ts(A("bsh", 16, 24), A("boh", 0, 128, 16), A("cf", 4, 5), OP.mult)
+    ts(A("pre", 0, 8), A("boh", 0, 128, 16), 1.0 / 16, OP.mult)
+    for q in range(8):
+        ts(A("gp", 128 * q, 128 * q + 128), A("ones"), A("pre", q, q + 1), OP.mult)
+    ts(A("gn"), A("gp"), -1.0, OP.mult)
+    ms(A("og"), 0.0)
+    ms(A("og", 112, 128), 1.0)
+    iota(A("w3"), [[-1, 128]], 64, 0)
+    iota(A("cf", 5, 6), [[0, 1]], 64, -1)
+    act(A("zj"), A("w3"), FN.Exp, math.log(BASE))
+    act(A("cf", 6, 7), A("cf", 5, 6), FN.Exp, math.log(BASE))
+    wcol = A("cf", 6, 7)
+    ts(A("whi"), A("zj"), 3.15, OP.mult)
+    ts(A("wlo"), A("zj"), 1.4, OP.mult)
+    iota(A("mt"), [[256, 4], [4, 64], [-2, 2]], B + 2, 0)
+    iota(A("ni"), [[256, 4], [2, 128]], B + 1, 0)
+
+    def masks():
+        used, out = [], {}
+        for t in sorted(range(1, N), key=lambda t: len(topo.engines(core, peer(t)))):
+            free = [e for e in topo.engines(core, peer(t)) if e not in used][:4]
+            used += free
+            out[t] = sum(1 << e for e in free)
+        return out
+
+    def fused(src_of, dst_of):
+        mk = masks()
+        tr = []
+        for t in range(1, N):
+            rid, pid, _ = topo.addr(peer(t))
+            tr.append(RemoteDMATransfer(dst_ids=[DstId(rid=rid, pnc=pid)], dma_engine_mask=mk[t], remote_sem=T.sem["aq%d" % t],
+                                        src=src_of(t), dst=dst_of(t)))
+        return g.remote_dma_fused(tr, local_sem=T.sem.ls)
+
+    a1 = node("G", lambda: fused(lambda t: T.qT0[:], lambda t: T["qT%d" % t][:]), [A("qT0")], [], 1500, remote=1)
+    a2 = node("G", lambda: fused(lambda t: T.hvu[:, 16 * t:16 * t + 16], lambda t: T["hl%d" % t][:]), [A("hvu")], [], 1500, remote=1)
+    sent[0] += 24
+    for t in range(1, N):
+        node("R", None, [], [A("qT%d" % t), A("hl%d" % t)], 0, sem=T.sem["aq%d" % t], cnt=8, after=[a1, a2], lat=4000)
+
+    nxt = peer(1)
+    rid1, pid1, _ = topo.addr(nxt)
+    mask1 = topo.mask(core, nxt)
+    ne1 = len(topo.engines(core, nxt))
+    ne_in = len(topo.engines(peer(-1), core))
+    rot = {"pe": 0, "rl": 0, "kr": 0, "E": 0, "W": 0}
+
+    def nx(k, m):
+        rot[k] += 1
+        return "%s#%d" % (k, rot[k])
+
+    def step(t, s, z):
+        base = B + 256 * t
+        gs = 3 * t + s
+        wd, wn = "wd%d%d" % (z, gs % 2), "wd%d%d" % (z, (gs + 1) % 2)
+        i0 = H * z
+        h, n0, K = i0 // 128, i0 % 128, H // 16
+        k0 = n0 // 16
+        if s == 0:
+            lst = A("hvu" if t == 0 else "hl%d" % t, i0 // 16, i0 // 16 + K)
+        else:
+            lst = A("vl%d" % h, 8 * (s - 1) + k0, 8 * (s - 1) + k0 + K)
+        kc, Wb = A("kc", i0, i0 + H), nx("W", 2)
+        if s == 0 and t > 0:
+            act(A(wd, Y, 2 * Y, 16), A("pl", L * (t - 1) + i0, L * (t - 1) + i0 + H), FN.Copy)
+        cp(A("ku", i0, i0 + H), IND(A("chf", 0, base), lst))
+        pick = s < 2 or h == 0
+        types = TYPES0 if gs == 0 else TYPES.split()[2 * s + h]
+        keyw = A("key", 0, base)
+        qt = A("qT%d" % t, 128 * h, 128 * h + 128)
+        for c in range(H // 32):
+            ch = n0 // 32 + c
+            f0 = i0 // 16 + 2 * c
+            ty = types[ch]
+            y = A(wd, 512 * c, 512 * c + 512)
+            src = IND(keyw, A("ku", i0 + 32 * c, i0 + 32 * c + 32))
+            terms = [(A("idb"), y)]
+            if ty == "Z":
+                cp(y, src)
+            elif ty == "Y":
+                act(y, src, FN.Copy)
+            elif ty in "ST":
+                kr, D = A(nx("kr", 2)), nx("E", 2)
+                if ty == "S":
+                    act(kr, src, FN.Copy)
+                else:
+                    cp(kr, src)
+                pz = A(wd, Y + 512 * c, Y + 512 * c + 512, 16)
+                mm([(A(D), A("idb"), kr, True, False)] + [(A(D, j, 512, 16), A("nid"), pz, False, j == 15) for j in range(16)])
+                act(y, A(D), FN.Abs)
+            else:
+                pe = A(nx("pe", 3))
+                scan(pe, A("mask"), A(wd, Y + 512 * c, Y + 512 * c + 512), OP.mult, OP.add)
+                tt(y, src, pe, OP.subtract)
+                if ty == "R":
+                    rl = A(nx("rl", 4))
+                    ts(rl, y, 0.0, OP.max)
+                    terms = [(A("two"), rl), (A("nid"), y)]
+                else:
+                    act(y, y, FN.Abs)
+            E = A(nx("E", 2))
+            mm(acc(E, [(qt, A("eq", 512 * ch, 512 * ch + 512))] + terms))
+            act(F4(f0, f0 + 2), E, FN.Abs)
+            if c % 2 == 1:
+                o = A(Wb, 32 * (c - 1), 32 * (c + 1))
+                mm(acc(o, [(A("idh"), A("sth", 32 * (c - 1), 32 * (c + 1)))]
+                       + [(A("bgb", 15 - u, 143 - u), F4(f0 - 2, f0 + 2, u)) for u in range(16)]))
+            if c == 0 and pick:
+                act(kc, IND(A("chf", 0, base), lst), FN.Identity, bias=A("cf", 7, 8))
+                if h == 0 and s > 0:
+                    act(A("rr", 128 * (s - 1) + n0, 128 * (s - 1) + n0 + H), kc, FN.Identity, bias=A("cf", 8, 9))
+        oi, oj, ou = [A(x, i0 // 16, i0 // 16 + K) for x in ("oi", "oj", "ou")]
+        scan(A("sc", i0, i0 + H), A("rst%d" % (t % 2), 0, H), A(Wb, 0, H), OP.max, OP.min)
+        cp(oi, A("sc", i0 + 15, i0 + H, 16))
+        ts(oj, oi, 4095, OP.bitwise_and)
+        cp(ou, oj)
+        if pick:
+            nm, lo = ("sela", 128 * s + n0) if h == 0 else ("selb", n0)
+            tt(A(nm, lo, lo + H), IND(A("tab"), ou), kc, OP.min)
+            if s < 2:
+                Wc = A(nx("W", 2), 0, K)
+                mm(acc(Wc, [(A("bgh", 15 - u, 143 - u), A(nm, lo + u, lo + H, 16)) for u in range(16)]))
+                ts(A("vl%d" % h, 8 * s + k0, 8 * s + k0 + K), Wc, 2.0 ** -12, OP.mult, 32768.0, OP.add)
+        if s < 2:
+            act(A(wn, Y, 2 * Y, 16), IND(A(wd), ou), FN.Abs)
+        else:
+            o = A("ps", L * t + i0, L * t + i0 + H)
+            act(o, IND(A(wd), ou), FN.Abs)
+            dst = A("pl", L * t + i0, L * t + i0 + H)
+            sem = T.sem["ap%d" % (NS * t + z)]
+            a = node("G", lambda: g.remote_dma(dst[0], o[0], sem, T.sem.ls, pid1, rid1, mask1), [o], [], 1200, remote=1)
+            sent[0] += ne1
+            node("R", None, [], [dst], 0, sem=sem, cnt=ne_in, after=[a], lat=3500)
+            if t == NT - 1:
+                dma("Y", T.yp[:, i0:i0 + H], dst[0], [dst], [], 2500)
+
+    def early(t):
+        base = B + 256 * t
+        mm([(A("XB", 0, 256), A("boh"), A("sela", 0, 256), True, True)])
+        ts(A("uh"), A("XB", 0, 256), 30720.0, OP.add)
+        mm(acc(A("FB", 128, 136), [(A("sela", 0, 128), A("bsh", 0, 8)), (A("sela", 128, 256), A("bsh", 8, 16))])
+           + [(A("FB", 136, 144), A("sela", 128, 256), A("bsh", 16, 24), True, True)])
+        ts(A("pre", 8, 16), A("FB", 128, 136), 0.0, OP.not_equal, wcol, OP.mult)
+        ts(A("pre", 16, 24), A("FB", 136, 144), -2048.0, OP.is_equal)
+        tt(A("pre", 0, 8), A("pre", 8, 16), A("pre", 16, 24), OP.mult)
+        cp(A("ab"), A("vl0"))
+        tt(A("da"), A("ab"), A("dum"), OP.subtract)
+        ts(A("ab"), A("da"), 2.0 ** -16, OP.mult)
+        if t < NT - 1:
+            for e in range(2):
+                act(A("key", base + e, base + 256, 2), IND(A("key", 0, base), A("vl0", 8 * e, 8 * e + 8)), FN.Copy)
+        ts(A("oh", 0, 128), A("sela", 128, 256), -2048.0, OP.is_gt)
+        o1 = A("oh", 0, 128)
+        mm([(A("XB", 128 * k, 128 * k + 128), A(nm), o1, True, True) for k, nm in enumerate(("tle", "tgt", "tsh", "idb"))])
+        tt(A("t1", 0, 128), A("XB", 0, 128), A("rr", 0, 128), OP.mult)
+        tt(A("t4", 0, 128), A("XB", 128, 256), A("rr", 0, 128), OP.mult)
+        tt(A("t2"), A("XB", 256, 384), A("mt", 128 * t, 128 * t + 128), OP.mult)
+        tt(A("t3"), A("XB", 384, 512), A("ni", 128 * t, 128 * t + 128), OP.mult)
+        tt(A("t4", 0, 128), A("t4", 0, 128), A("t3"), OP.add)
+
+    def diffs(q):
+        D = nx("E", 2)
+        lst = []
+        for e in range(2):
+            for f in range(2):
+                lst += acc(A(D, 256 * e + 128 * f, 256 * e + 128 * f + 128),
+                           [(A("uh", 128 * e, 128 * e + 128), A("gp", 128 * q, 128 * q + 128)),
+                            (A("gn", 128 * q, 128 * q + 128), A("uh", 128 * f, 128 * f + 128))])
+        mm(lst)
+        if q < DIRECT:
+            nodes[-1]["rd"].append(("wc", 8, 16))
+        return D
+
+    def middle(t):
+        for q in range(DIRECT, 8):
+            act(A("db", 512 * q, 512 * q + 512), A(diffs(q)), FN.Copy)
+
+    def late(t):
+        base = B + 256 * t
+        mm([(A("FB", 144, 152), A("sela", 256, 384), A("bsh", 0, 8), True, True)])
+        ts(A("wc", 8, 16), A("FB", 144, 152), -32767.5, OP.is_gt)
+        tt(A("wc", 0, 8), A("wc", 8, 16), A("pre", 0, 8), OP.mult)
+        order = list(range(DIRECT, 8)) + list(range(DIRECT))
+        for q in order:
+            src = A("db", 512 * q, 512 * q + 512) if q >= DIRECT else A(diffs(q))
+            ts(A("eqw", 512 * q, 512 * q + 512), src, 0.0, OP.is_equal, A("wc", q, q + 1), OP.mult)
+        full = acc(A("FB", 0, 128), [(A("og", 112 - 16 * q, 240 - 16 * q), A("eqw", 512 * q + 128 * e, 512 * q + 128 * e + 128))
+                                     for q in order for e in range(4)])
+        for k in range(0, 32, 8):
+            mm(full[k:k + 8])
+        ts(A("oh", 128, 256), A("sela", 256, 384), -2048.0, OP.is_gt)
+        o2 = A("oh", 128, 256)
+        mm([(A("XB", 128 * k, 128 * k + 128), A(nm), o2, True, True) for k, nm in enumerate(("tle", "tgt"))])
+        tt(A("t1", 128, 256), A("XB", 0, 128), A("rr", 128, 256), OP.mult)
+        tt(A("t4", 128, 256), A("XB", 128, 256), A("rr", 128, 256), OP.mult)
+        tt(A("hi"), A("FB", 0, 128), A("whi"), OP.is_lt)
+        tt(A("lo"), A("FB", 0, 128), A("wlo"), OP.is_gt)
+        tt(A("st"), A("hi"), A("lo"), OP.mult)
+        for e in range(2):
+            tt(A("fl", e, 128, 2), A("st", 0, 128, 2), A("st", 1, 128, 2), OP.mult)
+        mm(acc(A("FB", 160, 168), [(A("bgb", 15 - u, 143 - u), A("fl", u, 128, 16)) for u in range(16)]))
+        for e in range(2):
+            tt(A("of", 8 * e, 8 * e + 8), A("FB", 160, 168), A("ab", 8 * e, 8 * e + 8), OP.mult)
+        tt(A("og2"), A("of"), A("dum"), OP.add)
+        cp(A("so"), A("og2"))
+        tb = "chf" if t < NT - 1 else "cho"
+        tt(IND(A(tb), A("so", 0, 8)), A("t1", 0, 128), A("t2"), OP.add)
+        cp(IND(A(tb), A("so", 8, 16)), A("t1", 128, 256))
+        for e in range(2):
+            tt(A(tb, base + e, base + 256, 2), A("t4", 128 * e, 128 * e + 128), A("fl"), OP.mult)
+        if t < NT - 1:
+            mm([(A("XB", 256, 384), A("six"), A("fl"), True, True)])
+            act(A("zj"), A("XB", 256, 384), FN.Identity, 1.0, A("zc", 0, 1))
+            cp(A("zi", 0, 1), A("zc", 0, 1))
+            ts(A("zk", 0, 1), A("zi", 0, 1), 63, OP.bitwise_and)
+            ts(A("za", 0, 1), A("zk", 0, 1), 4096.0, OP.mult)
+            ts(A("rst%d" % ((t + 1) % 2), 0, 128, 16), A("rb"), A("za", 0, 1), OP.add)
+
+    def store():
+        dma("Y", T.yc[:], T.cho[:, 0:W], [A("cho", 0, W)], [], 9000)
+
+    for t in range(NT):
+        if t == NT - 1:
+            top = B + 256 * t
+            dma("Y", T.cho[:, 0:top], T.chf[:, 0:top], [A("chf", 0, top)], [A("cho", 0, top)], 9000)
+            cp(A("cho", 0, 1), A("ch0", 0, 1))
+        for w in (ORDER if t < NT - 1 else ORDERL).split():
+            if w[0] in "AB":
+                for z in range(NS // 2):
+                    step(t, int(w[1]), "AB".index(w[0]) * NS // 2 + z)
+            else:
+                {"e": early, "m": middle, "l": late}[w](t)
+                if w == "l" and t == NT - 1:
+                    store()
+    return nodes, sent[0]
+
+
+def plan(nodes):
+    n = len(nodes)
+    hist = {}
+    deps = []
+    for i, d in enumerate(nodes):
+        dd = {}
+        for regs, w in ((d["rd"], False), (d["wr"], True)):
+            for nm, lo, hi in regs:
+                ps = isps(nm)
+                for j, lo2, hi2, w2 in hist.get(nm, []):
+                    same = nodes[j]["eng"] == d["eng"] and "sem" not in nodes[j]
+                    if ps and not same:
+                        dd[j] = True
+                    elif ps:
+                        dd[j] = dd.get(j, False) or (d["eng"] != "P" and (w2 or w) and lo < hi2 and lo2 < hi)
+                    elif lo < hi2 and lo2 < hi and (w or w2):
+                        dd[j] = True
+        for j in d.get("after", []):
+            dd[j] = False
+        for regs, w in ((d["rd"], False), (d["wr"], True)):
+            for nm, lo, hi in set(regs):
+                h = hist.setdefault(nm, [])
+                if isps(nm):
+                    h[:] = [e for e in h if nodes[e[0]]["eng"] == d["eng"]]
+                elif w:
+                    h[:] = [e for e in h if not (lo <= e[1] and e[2] <= hi) or e[0] == i]
+                h.append((i, lo, hi, w))
+        dd.pop(i, None)
+        deps.append(dd)
+    LAT = 70
+    succ = [[] for _ in range(n)]
+    for i in range(n):
+        for j in deps[i]:
+            succ[j].append(i)
+    rank = [0.0] * n
+    for i in range(n - 1, -1, -1):
+        rank[i] = nodes[i]["cost"] + nodes[i].get("lat", 0) + max([rank[k] + LAT for k in succ[i]] + [0])
+    x = SEED
+    for i in range(n):
+        x = (x * 1103515245 + 12345) % 2147483648
+        rank[i] += NOISE * (x / 2147483648.0)
+    left = [len(deps[i]) for i in range(n)]
+    ready = {e: [] for e in "VSPGYR"}
+    at = [0.0] * n
+    fin = [0.0] * n
+    free = {e: 0.0 for e in ready}
+    order = {e: [] for e in ready}
+    for i in range(n):
+        if left[i] == 0:
+            ready[nodes[i]["eng"]].append(i)
+    users, first = {}, {}
+    for i, d in enumerate(nodes):
+        for nm in set(r[0] for r in d["rd"] + d["wr"] if "#" in r[0]):
+            if nm not in users:
+                users[nm] = []
+                first[i] = nm
+            users[nm].append(i)
+    open_ = {nm: len(u) for nm, u in users.items()}
+    held = {b: None for p in POOL.values() for b in p}
+    phys = {}
+
+    def slot(k):
+        bs = [(0.0 if held[b] is None else max(fin[j] for j in users[held[b]]) + LAT, b)
+              for b in POOL[first[k].split("#")[0]] if held[b] is None or open_[held[b]] == 0]
+        return min(bs) if bs else (1e18, None)
+
+    done = 0
+    while done < n:
+        best = None
+        eff = {}
+        for e in ready:
+            for k in ready[e]:
+                eff[k] = max(at[k], slot(k)[0]) if k in first else at[k]
+            if ready[e]:
+                t0 = max(free[e], min(eff[i] for i in ready[e]))
+                if best is None or t0 < best[0]:
+                    best = (t0, e)
+        t0, e = best
+        i = max((k for k in ready[e] if eff[k] <= t0 + SLACK), key=lambda k: (rank[k] - BETA * k, -k))
+        ready[e].remove(i)
+        t0 = max(t0, eff[i])
+        if i in first:
+            b = slot(i)[1]
+            if held[b] is not None:
+                for j in users[held[b]]:
+                    deps[i][j] = deps[i].get(j, False) or not (e == "P" and nodes[j]["eng"] == "P")
+            held[b] = first[i]
+            phys[first[i]] = b
+        free[e] = t0 + nodes[i]["cost"]
+        fin[i] = free[e] + nodes[i].get("lat", 0)
+        for nm in set(r[0] for r in nodes[i]["rd"] + nodes[i]["wr"] if "#" in r[0]):
+            open_[nm] -= 1
+        order[e].append(i)
+        done += 1
+        for k in succ[i]:
+            at[k] = max(at[k], fin[i] + (LAT if deps[k][i] else 0))
+            left[k] -= 1
+            if left[k] == 0:
+                ready[nodes[k]["eng"]].append(k)
+    return deps, order, fin, phys
+
+
+def rank_program(g, core, T, topo):
+    rank = T.rank_of(core)
+    if rank is None:
+        return
+    deps, order, fin, phys = plan(build(g, core, T, topo, rank, {})[0])
+    nodes, sent = build(g, core, T, topo, rank, phys)
+    queue = {"V": g.vector, "S": g.scalar, "P": g.tensor, "G": g, "Y": g.sync}
+    esem = {"V": T.sem.sV, "S": T.sem.sS, "P": T.sem.sP, "G": T.sem.sG}
+    need = set(j for i in range(len(nodes)) if nodes[i]["eng"] != "R" for j, w in deps[i].items() if w)
+    mark = {}
+    for e in esem:
+        c = 0
+        for i in order[e]:
+            if "sem" not in nodes[i] and "remote" not in nodes[i] and i in need:
+                c += 1
+                mark[i] = (e, esem[e], c)
+    for i, d in enumerate(nodes):
+        if "sem" in d:
+            mark[i] = ("n%d" % i, d["sem"], d["cnt"])
+    waited = set()
+    for e in queue:
+        seen = {}
+        for i in order[e]:
+            want = {}
+            for j, w in deps[i].items():
+                if w:
+                    k, sem, c = mark[j]
+                    waited.add(j)
+                    if c > seen.get(k, 0) and c > want.get(k, (None, 0))[1]:
+                        want[k] = (sem, c)
+            for k, (sem, c) in want.items():
+                queue[e].wait_ge(sem, c)
+                seen[k] = c
+            r = nodes[i]["emit"]()
+            if i in mark and "sem" not in nodes[i]:
+                r.then_inc(mark[i][1], 1)
+    for i, d in enumerate(nodes):
+        if "sem" in d and i not in waited:
+            g.wait_ge(d["sem"], d["cnt"])
+    g.wait_ge(T.sem.ls, sent)

@@ -7,80 +7,83 @@ W = B + 256 * NT
 WD = W + 256
 KNONE = 640.0
 BASE = 3.5
-TYPES = "SRXX XSRX SXRX SRXX XSRX SXRX"
-ORDER = "A0 B0 A1 B1 e A2 m B2 l"
-ORDERL = "A0 B0 A1 e B1 A2 m l B2"
-TYPES0 = "ZYZY"
-DIRECT = 2
+Y = 2048
 NLOAD = 4
-NS = 2
-H = L // NS
-Y = 16 * H
-GF, PEF = 1.56, 0.5
+STREAM = {"A": (0, 128), "B": (128, 128)}
+CUT = {}
+for _s in ("first", 0, 1, 2):
+    CUT[_s, "A"] = CUT[_s, "B"] = "Z1 Y1 Z1 Y1|1 1 1 1|2 2" if _s == "first" else "S1 X1 X1 X1|1 1 1 1|2 2"
+ORDER = ["A0 c B0 A1 B1 e A2 B2k l B2r"] + ["A0 B0 A1 B1 e A2 B2k l B2r"] * 2 + ["o A0 B0 A1 e B1 A2 l B2"]
+PAR = {"GF": 1.56, "SC": 3.5, "PEF": 0.5, "PMM": 8, "VO": 60, "SO": 75, "LAT": 220, "BETA": 1000, "ROUNDS": 4, "PASSES": 3, "SPLIT": 1}
 
 f32, bf, f16, i32, u16 = "float32", "bfloat16", "float16", "int32", "uint16"
 SCRATCH = {}
 for _n, _c, _d in [
     ("chi", B, i32), ("chf", WD, f32), ("cho", WD, f32), ("key", W, bf), ("ch0", 4, f32), ("qraw", L, bf), ("hvi", 64, i32), ("hvu", 64, u16),
     ("qT0", L, bf), ("qT1", L, bf), ("qT2", L, bf), ("qT3", L, bf), ("hl1", 16, u16), ("hl2", 16, u16), ("hl3", 16, u16),
-    ("tab", Y + 2048, bf), ("eq", 2048, bf), ("mask", 512, bf), ("pe0", 512, bf), ("pe1", 512, bf), ("pe2", 512, bf),
-    ("rl0", 512, bf), ("rl1", 512, bf), ("rl2", 512, bf), ("rl3", 512, bf), ("kr0", 512, bf), ("kr1", 512, bf), ("kr2", 512, bf),
-    ("ku", 256, u16), ("kc", 256, f32), ("vl0", 16, u16), ("vl1", 16, u16),
-    ("sc", 256, f32), ("oi", 16, i32), ("oj", 16, i32), ("ou", 16, u16), ("sela", 384, f16), ("selb", 128, f16), ("rst0", 128, f32), ("rst1", 128, f32),
+    ("tab", 2 * Y, bf), ("eq", Y, bf), ("ramp", Y, bf), ("pe0", Y, bf), ("pe1", Y, bf),
+    ("rl0", Y, bf), ("rl1", Y, bf), ("kr0", Y, bf), ("kr1", Y, bf),
+    ("ku", 256, u16), ("kc", 256, f16), ("vl", 32, u16),
+    ("sc", 256, f32), ("oi", 16, i32), ("oj", 48, i32), ("ou", 16, u16), ("sela", 256, f16), ("selb", 128, f16), ("rst0", 128, f32), ("rst1", 128, f32),
     ("ps", 1024, bf), ("pl", 1024, bf),
-    ("ones", 128, bf), ("idb", 128, bf), ("nid", 128, bf), ("two", 128, bf), ("idh", 128, f16), ("six", 128, bf),
-    ("bgb", 144, bf), ("bgh", 144, f16), ("og", 240, bf), ("gp", 1024, f16), ("gn", 1024, f16), ("bsh", 24, f16), ("boh", 128, f16),
+    ("ones", 128, bf), ("idb", 128, bf), ("nid", 128, bf), ("two", 128, bf), ("idh", 128, f16), ("six", 128, f32),
+    ("bgb", 144, bf), ("bgh", 144, f16), ("bg1", 144, bf), ("boh", 128, f16), ("wk", 1024, bf),
     ("tle", 128, bf), ("tgt", 128, bf), ("tsh", 128, bf), ("sth", 128, f16),
-    ("ci", 8, i32), ("cf", 12, f32), ("w1", 144, f32), ("w2", 144, f32), ("w3", 128, f32), ("wi", 128, i32),
-    ("whi", 128, f32), ("wlo", 128, f32), ("mt", 512, f32), ("ni", 512, f32), ("dum", 16, f32), ("rb", 8, f32),
-    ("uh", 256, f16), ("db", 4096, bf), ("eqw", 4096, bf), ("oh", 256, bf), ("rr", 256, f32), ("t1", 256, f32), ("t4", 256, f32),
-    ("t2", 128, f32), ("t3", 128, f32), ("pre", 24, f32), ("wc", 16, f32), ("hi", 128, bf), ("lo", 128, bf), ("st", 128, bf),
+    ("ci", 8, i32), ("cf", 12, f32), ("w1", 144, f32), ("w2", 144, f32), ("w3", 128, f32), ("w4", 128, f32), ("w5", 128, f32), ("wi", 128, i32),
+    ("whi", 128, f32), ("wlo", 128, f32), ("wl", 16, f32), ("mt", 512, f32), ("ni", 512, f32), ("dum", 16, f32), ("dmc", 16, f32), ("rb", 8, f32),
+    ("uh", 256, f16), ("eqw", 2304, bf), ("oh", 256, bf), ("rr", 256, f32), ("t1", 256, f32), ("t4", 256, f32),
+    ("pre", 32, f32), ("j15", 8, i32), ("hi", 128, bf), ("lo", 128, bf),
     ("fl", 128, bf), ("ab", 16, f32), ("da", 16, f32), ("of", 16, f32), ("og2", 16, f32), ("so", 16, u16),
-    ("zj", 128, f32), ("zc", 4, f32), ("zi", 4, i32), ("zk", 4, i32), ("za", 4, f32),
+    ("zc", 4, f32), ("zi", 4, i32), ("zk", 4, i32), ("za", 4, f32),
 ]:
     SCRATCH[_n] = ("sbuf", [128, _c], _d)
 SCRATCH["fa"] = ("sbuf", [128, 16, 16, 16], bf)
-for _n in range(NS):
-    SCRATCH["wd%d0" % _n] = ("sbuf", [128, 2 * Y], bf)
-    SCRATCH["wd%d1" % _n] = ("sbuf", [128, 2 * Y], bf)
-PSUM = ["E0", "E1", "E2", "E3", "W0", "W1", "XB", "FB"]
-POOL = {"E": ["E0", "E1", "E2", "E3"], "W": ["W0", "W1"], "pe": ["pe0", "pe1", "pe2"], "rl": ["rl0", "rl1", "rl2", "rl3"], "kr": ["kr0", "kr1", "kr2"]}
-SLACK = 40
-BETA = 1000
-SEED, NOISE = 816, 1000
-
-
-def isps(nm):
-    return nm in PSUM or nm[:2] in ("E#", "W#")
-
-
-for _n in PSUM:
-    SCRATCH[_n] = ("psum", [128, 512], f32)
+for _n in "AaBb":
+    SCRATCH["wd%s0" % _n] = ("sbuf", [128, 2 * Y], bf)
+    SCRATCH["wd%s1" % _n] = ("sbuf", [128, 2 * Y], bf)
+for _n in range(4):
+    SCRATCH["pm%d" % _n] = ("psum", [128, 1024], f32)
 SEMAPHORES = (["sV", "sS", "sP", "sG", "ls"] + ["d%d" % k for k in range(24)] + ["aq%d" % t for t in range(1, 4)]
-              + ["ap%d" % k for k in range(4 * NS)])
+              + ["ap%d" % k for k in range(4 * NT)])
 OP = AluOpType
 FN = ActivationFunctionType
 
 
-def build(g, core, T, topo, rank, phys):
+def isps(nm):
+    return "#" in nm
+
+
+def build(g, core, T, topo, rank, phys, par=None):
+    par = par or PAR
     nodes = []
     V, S, P = g.vector, g.scalar, g.tensor
+    VO, SO = par["VO"], par["SO"]
 
     def A(name, lo=0, hi=None, step=1):
-        b = phys.get(name, name.split("#")[0] + "0") if "#" in name else name
+        b, o = name, 0
+        if isps(name):
+            b, o = "pm%d" % (phys.get(name, 0) // 2), 512 * (phys.get(name, 0) % 2)
         if hi is None:
-            hi = SCRATCH[b][1][1]
-        ap = T[b][:, lo:hi] if step == 1 else T[b][:, lo:hi:step]
+            hi = SCRATCH[name][1][1]
+        ap = T[b][:, o + lo:o + hi] if step == 1 else T[b][:, o + lo:o + hi:step]
         n = (hi - lo + step - 1) // step
-        return (ap, [(name, lo, lo + (n - 1) * step + 1)], n, SCRATCH[b][2], 0)
+        end = lo + (n - 1) * step + 1
+        if isps(name):
+            return (ap, [("%s/%d" % (name, k), lo, end) for k in range(lo // 512, (end - 1) // 512 + 1)], n, f32, 0)
+        return (ap, [(name, lo, end)], n, SCRATCH[name][2], 0)
+
+    tiles = [0]
+
+    def tile():
+        tiles[0] += 1
+        return "#%d" % tiles[0]
 
     def IND(win, off):
         return (win[0].indirect(off[0]), win[1] + off[1], 16 * off[2], win[3], 1)
 
     def F4(a, b, ilo=None):
-        name = "fa"
-        ap = T[name][:, a:b, :, :] if ilo is None else T[name][:, a:b, ilo, :]
-        return (ap, [(name, 256 * a, 256 * b)], (b - a) * (256 if ilo is None else 16), bf, 0)
+        ap = T.fa[:, a:b, :, :] if ilo is None else T.fa[:, a:b, ilo, :]
+        return (ap, [("fa", 256 * a, 256 * b)], (b - a) * (256 if ilo is None else 16), bf, 0)
 
     def node(eng, emit, rd, wr, cost, **kw):
         d = {"eng": eng, "emit": emit, "rd": [r for x in rd for r in x[1]], "wr": [r for x in wr for r in x[1]], "cost": cost}
@@ -93,8 +96,8 @@ def build(g, core, T, topo, rank, phys):
 
     def rate(o, i, base):
         if o[4]:
-            return 3.5
-        return GF if i[4] else base
+            return par["SC"]
+        return par["GF"] if i[4] else base
 
     def split_out(o):
         return ((None, o[1][:1]), (None, o[1][1:])) if o[4] else (o, (None, []))
@@ -107,36 +110,34 @@ def build(g, core, T, topo, rank, phys):
 
     def cp(o, i):
         w, r = split_out(o)
-        node("V", lambda: V.tensor_copy(o[0], i[0]), [i, r], [w], 60 + i[2] * rate(o, i, .5 if two_b(o, i) else 1))
+        node("V", lambda: V.tensor_copy(o[0], i[0]), [i, r], [w], VO + i[2] * rate(o, i, .5 if two_b(o, i) else 1))
 
     def ts(o, i, s1, op0, s2=None, op1=None):
         if op1 is None:
             em = lambda: V.tensor_scalar(o[0], i[0], val(s1), None, op0)
         else:
             em = lambda: V.tensor_scalar(o[0], i[0], val(s1), val(s2), op0, op1)
-        node("V", em, [i] + cols(s1, s2), [o], 60 + i[2] * rate(o, i, .5 if two_b(o, i) else 1))
+        node("V", em, [i] + cols(s1, s2), [o], VO + i[2] * rate(o, i, .5 if two_b(o, i) else 1))
 
     def tt(o, a, b, op):
         w, r = split_out(o)
         ps = isps(a[1][0][0]) or isps(b[1][0][0])
-        node("V", lambda: V.tensor_tensor(o[0], a[0], b[0], op), [a, b, r], [w], 60 + a[2] * rate(o, a, 1 if ps else 2))
+        node("V", lambda: V.tensor_tensor(o[0], a[0], b[0], op), [a, b, r], [w], VO + a[2] * rate(o, a, 1 if ps else 2))
 
     def ms(o, c):
-        node("V", lambda: V.memset(o[0], c), [], [o], 60 + o[2] * (.5 if two_b(o) else 1))
+        node("V", lambda: V.memset(o[0], c), [], [o], VO + o[2] * (.5 if two_b(o) else 1))
 
     def scan(o, d0, d1, op0, op1):
         node("V", lambda: V.tensor_tensor_scan(o[0], d0[0], d1[0], 0.0, op0, op1), [d0, d1], [o],
-             60 + o[2] * (.5 if two_b(o, d0, d1) else 1))
+             VO + o[2] * (.5 if two_b(o, d0, d1) else 1))
 
     def act(o, i, fn, scale=1.0, acc=None, bias=None):
+        kw = {"scale": scale}
         if bias is not None:
-            node("S", lambda: S.activation(o[0], i[0], fn, bias=bias[0]), [i, bias], [o], 75 + i[2] * rate(o, i, 1))
-            return
-        if acc is None:
-            em = lambda: S.activation(o[0], i[0], fn, scale=scale)
-        else:
-            em = lambda: S.activation(o[0], i[0], fn, scale=scale, accum_out=acc[0])
-        node("S", em, [i], [o] + cols(acc), 75 + i[2] * rate(o, i, 1))
+            kw["bias"] = val(bias)
+        if acc is not None:
+            kw["accum_out"] = acc[0]
+        node("S", lambda: S.activation(o[0], i[0], fn, **kw), [i] + cols(bias), [o] + cols(acc), SO + i[2] * rate(o, i, 1))
 
     def mm(lst):
         def em():
@@ -144,7 +145,8 @@ def build(g, core, T, topo, rank, phys):
             for o, l, x, a, b in lst:
                 r = P.matmul(o[0], l[0], x[0], a, b)
             return r
-        node("P", em, [e[1] for e in lst] + [e[2] for e in lst], [e[0] for e in lst], 30 + PEF * sum(max(64, e[2][2]) for e in lst))
+        node("P", em, [e[1] for e in lst] + [e[2] for e in lst], [e[0] for e in lst],
+             30 + sum(par["PMM"] + par["PEF"] * max(64, e[2][2]) * (4 if e[2][3] == f32 else 1) for e in lst))
 
     def acc(o, pairs):
         return [(o, l, x, k == 0, k == len(pairs) - 1) for k, (l, x) in enumerate(pairs)]
@@ -172,12 +174,21 @@ def build(g, core, T, topo, rank, phys):
     def peer(k):
         return T.cores[(rank + k) % N]
 
-    dma("Y", T.hvi[:], T.hv[:], [], [A("hvi")], 2500)
+    dma("S", T.hvi[:], T.hv[:], [], [A("hvi")], 2500)
     dma("S", T.qraw[:], T.qs[:], [], [A("qraw")], 2500)
     cw = B // NLOAD
     for k in range(NLOAD):
-        dma("Y", T.chi[:, k * cw:(k + 1) * cw], T.ch[:, k * cw:(k + 1) * cw], [], [A("chi", k * cw, (k + 1) * cw)], 3000 + 1300 * (k + 1))
-    dma("S", T.key[:, 0:B], T.kb[:], [], [A("key", 0, B)], 9500)
+        dma("Y", T.chi[:, k * cw:(k + 1) * cw], T.ch[:, k * cw:(k + 1) * cw], [], [A("chi", k * cw, (k + 1) * cw)], 2500 + 1100 * (k + 1))
+    dma("Y", T.key[:, 0:B], T.kb[:], [], [A("key", 0, B)], 9000)
+    ms(A("ones"), 1.0)
+    ms(A("tab", Y, 2 * Y), -2048.0)
+    iota(A("ci", 0, 1), [[0, 1]], 0, 1)
+    asel(A("idb"), A("ones"), [[-1, 128]], OP.is_equal, 0, 1)
+    iota(A("w1"), [[1, 144]], 0, 0)
+    iota(A("wi"), [[256, 8], [1, 16]], 0, 16)
+    for k in range(2):
+        asel(A("eq", 1024 * k, 1024 * k + 1024), A("tab", Y, Y + 1024), [[1, 64], [0, 16]], OP.is_equal, 64 * k, -1)
+    iota(A("ramp"), [[0, 128], [256, 16]], 0, 0)
     cp(A("hvu"), A("hvi"))
     for k in range(NLOAD):
         cp(A("chf", k * cw, (k + 1) * cw), A("chi", k * cw, (k + 1) * cw))
@@ -186,19 +197,10 @@ def build(g, core, T, topo, rank, phys):
             ms(A("chf", 0, 1), 0.0)
     ms(A("key", 0, 1), KNONE)
 
-    ms(A("ones"), 1.0)
-    iota(A("ci", 0, 1), [[0, 1]], 0, 1)
-    asel(A("idb"), A("ones"), [[-1, 128]], OP.is_equal, 0, 1)
     ts(A("ci", 1, 2), A("ci", 0, 1), 15, OP.bitwise_and)
     ts(A("ci", 2, 3), A("ci", 0, 1), 112, OP.bitwise_and)
     cp(A("cf", 0, 3), A("ci", 0, 3))
     pc, rowc, g16 = A("cf", 0, 1), A("cf", 1, 2), A("cf", 2, 3)
-    ms(A("cf", 7, 8), -2048.0)
-    ms(A("cf", 8, 9), 2048.0)
-    ms(A("tab", Y, Y + 2048), -2048.0)
-    for k in range(2):
-        asel(A("eq", 1024 * k, 1024 * k + 1024), A("tab", Y, Y + 1024), [[1, 64], [0, 16]], OP.is_equal, 64 * k, -1)
-    iota(A("w1"), [[1, 144]], 0, 0)
     ts(A("w2"), A("w1"), g16, OP.subtract)
     ts(A("bgb"), A("w2"), 15.0, OP.is_equal, 4096.0, OP.mult)
     cp(A("bgh"), A("bgb"))
@@ -208,54 +210,47 @@ def build(g, core, T, topo, rank, phys):
     while n < Y:
         cp(A("tab", n, 2 * n), A("tab", 0, n))
         n *= 2
+    cp(A("idh"), A("idb"))
+    X = tile()
+    mm([(A(X, 128 * h, 128 * h + 128), A("qraw", 128 * h, 128 * h + 128), A("idb"), True, True) for h in range(2)])
+    act(A("qT0"), A(X, 0, 256), FN.Copy, 1.0 / 2048)
     act(A("nid"), A("idb"), FN.Copy, -1.0)
     act(A("two"), A("idb"), FN.Copy, 2.0)
-    act(A("six"), A("ones"), FN.Copy, 1.0 / 16)
-    cp(A("idh"), A("idb"))
-    ms(A("mask"), 1.0)
-    ms(A("mask", 0, 512, 16), 0.0)
-    ms(A("wd00", Y, 2 * Y), 0.0)
-    for k in range(1, 2 * NS):
-        act(A("wd%d%d" % (k % NS, k // NS), Y, 2 * Y), A("wd00", Y, 2 * Y), FN.Copy)
-    iota(A("wi"), [[256, 8], [1, 16]], 0, 16)
+    for k in range(2):
+        for z in STREAM:
+            act(A("wd%s%d" % (z, k), Y, Y + 16 * STREAM[z][1]), A("tab", Y, Y + 16 * STREAM[z][1]), FN.Copy, 0.0)
     ts(A("cf", 3, 4), g16, 16.0, OP.mult)
     ts(A("sth"), A("wi"), A("cf", 3, 4), OP.subtract)
     ts(A("rb"), A("sth", 0, 128, 16), float(4096 * TH + Y), OP.add)
     ms(A("rst0"), 0.0)
     ms(A("rst1"), 0.0)
     cp(A("rst0", 0, 128, 16), A("rb"))
-    ts(A("dum", 0, 8), A("sth", 0, 128, 16), 1.0 / 16, OP.mult, float(W), OP.add)
-    ts(A("dum", 8, 16), A("dum", 0, 8), 128.0, OP.add)
-    for h in range(2):
-        mm([(A("XB", 128 * h, 128 * h + 128), A("qraw", 128 * h, 128 * h + 128), A("idb"), True, True)])
-    act(A("qT0"), A("XB", 0, 256), FN.Copy, 1.0 / 2048)
-    ts(A("w3"), A("w2", 0, 128), 0.0, OP.is_ge)
-    ts(A("zj"), A("w2", 0, 128), 16.0, OP.is_lt)
-    tt(A("boh"), A("w3"), A("zj"), OP.mult)
-    ts(A("zj"), A("w1", 0, 128), pc, OP.is_le)
-    tt(A("tle"), A("w3"), A("zj"), OP.mult)
-    tt(A("tgt"), A("boh"), A("tle"), OP.subtract)
-    ts(A("zj"), A("w1", 0, 128), -1.0, OP.add, pc, OP.is_equal)
-    tt(A("tsh"), A("boh"), A("zj"), OP.mult)
-    cp(A("bsh", 0, 8), A("boh", 0, 128, 16))
-    ts(A("bsh", 8, 16), A("boh", 0, 128, 16), -1.0, OP.mult)
-    ts(A("cf", 4, 5), rowc, 15.0, OP.is_equal)
-    ts(A("bsh", 16, 24), A("boh", 0, 128, 16), A("cf", 4, 5), OP.mult)
-    ts(A("pre", 0, 8), A("boh", 0, 128, 16), 1.0 / 16, OP.mult)
-    for q in range(8):
-        ts(A("gp", 128 * q, 128 * q + 128), A("ones"), A("pre", q, q + 1), OP.mult)
-    ts(A("gn"), A("gp"), -1.0, OP.mult)
-    ms(A("og"), 0.0)
-    ms(A("og", 112, 128), 1.0)
-    iota(A("w3"), [[-1, 128]], 64, 0)
-    iota(A("cf", 5, 6), [[0, 1]], 64, -1)
-    act(A("zj"), A("w3"), FN.Exp, math.log(BASE))
-    act(A("cf", 6, 7), A("cf", 5, 6), FN.Exp, math.log(BASE))
-    wcol = A("cf", 6, 7)
-    ts(A("whi"), A("zj"), 3.15, OP.mult)
-    ts(A("wlo"), A("zj"), 1.4, OP.mult)
-    iota(A("mt"), [[256, 4], [4, 64], [-2, 2]], B + 2, 0)
-    iota(A("ni"), [[256, 4], [2, 128]], B + 1, 0)
+
+    def constants(t):
+        ts(A("dum", 0, 8), A("sth", 0, 128, 16), 1.0 / 16, OP.mult, float(W), OP.add)
+        ts(A("dum", 8, 16), A("dum", 0, 8), 128.0, OP.add)
+        ts(A("dmc"), A("dum"), -2048.0, OP.add)
+        ms(A("cf", 7, 8), -3.0)
+        act(A("six"), A("ones"), FN.Copy, 1.0 / 16)
+        act(A("bg1"), A("bgb"), FN.Copy, 2.0 ** -16)
+        ts(A("w3"), A("w2", 0, 128), 0.0, OP.is_ge)
+        ts(A("w4"), A("w2", 0, 128), 16.0, OP.is_lt)
+        tt(A("boh"), A("w3"), A("w4"), OP.mult)
+        ts(A("w4"), A("w1", 0, 128), pc, OP.is_le)
+        tt(A("tle"), A("w3"), A("w4"), OP.mult)
+        tt(A("tgt"), A("boh"), A("tle"), OP.subtract)
+        ts(A("w4"), A("w1", 0, 128), -1.0, OP.add, pc, OP.is_equal)
+        tt(A("tsh"), A("boh"), A("w4"), OP.mult)
+        iota(A("w5"), [[-1, 128]], 64, 0)
+        ts(A("wl", 8, 16), A("sth", 0, 128, 16), -1.0 / 16, OP.mult, 64.0, OP.add)
+        act(A("w5"), A("w5"), FN.Exp, math.log(BASE))
+        act(A("wl", 0, 8), A("wl", 8, 16), FN.Exp, math.log(BASE))
+        act(A("whi"), A("w5"), FN.Copy, 3.15)
+        act(A("wlo"), A("w5"), FN.Copy, 1.4)
+        for k in range(8):
+            ts(A("wk", 128 * k, 128 * k + 128), A("boh"), A("wl", k, k + 1), OP.mult)
+        iota(A("mt"), [[256, 4], [4, 64], [-2, 2]], B + 2, 0)
+        iota(A("ni"), [[256, 4], [2, 128]], B + 1, 0)
 
     def masks():
         used, out = [], {}
@@ -276,100 +271,119 @@ def build(g, core, T, topo, rank, phys):
 
     a1 = node("G", lambda: fused(lambda t: T.qT0[:], lambda t: T["qT%d" % t][:]), [A("qT0")], [], 1500, remote=1)
     a2 = node("G", lambda: fused(lambda t: T.hvu[:, 16 * t:16 * t + 16], lambda t: T["hl%d" % t][:]), [A("hvu")], [], 1500, remote=1)
-    sent[0] += 24
+    per = {t: bin(m).count("1") for t, m in masks().items()}
+    sent[0] += 2 * sum(per.values())
     for t in range(1, N):
-        node("R", None, [], [A("qT%d" % t), A("hl%d" % t)], 0, sem=T.sem["aq%d" % t], cnt=8, after=[a1, a2], lat=4000)
+        node("R", None, [], [A("qT%d" % t), A("hl%d" % t)], 0, sem=T.sem["aq%d" % t], cnt=2 * per[t], after=[a1, a2], lat=4000)
 
     nxt = peer(1)
     rid1, pid1, _ = topo.addr(nxt)
     mask1 = topo.mask(core, nxt)
     ne1 = len(topo.engines(core, nxt))
     ne_in = len(topo.engines(peer(-1), core))
-    rot = {"pe": 0, "rl": 0, "kr": 0, "E": 0, "W": 0}
 
-    def nx(k, m):
-        rot[k] += 1
-        return "%s#%d" % (k, rot[k])
-
-    def step(t, s, z):
+    def step(t, s, z, part):
         base = B + 256 * t
         gs = 3 * t + s
-        wd, wn = "wd%d%d" % (z, gs % 2), "wd%d%d" % (z, (gs + 1) % 2)
-        i0 = H * z
-        h, n0, K = i0 // 128, i0 % 128, H // 16
-        k0 = n0 // 16
+        wd, wn = "wd%s%d" % (z, gs % 2), "wd%s%d" % (z, (gs + 1) % 2)
+        i0, H = STREAM[z]
+        h, n0, k0, K = i0 // 128, i0 % 128, i0 // 16, H // 16
+        top = Y + 16 * H
         if s == 0:
-            lst = A("hvu" if t == 0 else "hl%d" % t, i0 // 16, i0 // 16 + K)
+            lst = A("hvu" if t == 0 else "hl%d" % t, k0, k0 + K)
         else:
-            lst = A("vl%d" % h, 8 * (s - 1) + k0, 8 * (s - 1) + k0 + K)
-        kc, Wb = A("kc", i0, i0 + H), nx("W", 2)
+            lst = A("vl", 16 * (s - 1) + k0, 16 * (s - 1) + k0 + K)
+        if part != "rest":
+            cp(A("ku", i0, i0 + H), IND(A("chf", 0, base), lst))
+        if part == "kids":
+            return
         if s == 0 and t > 0:
-            act(A(wd, Y, 2 * Y, 16), A("pl", L * (t - 1) + i0, L * (t - 1) + i0 + H), FN.Copy)
-        cp(A("ku", i0, i0 + H), IND(A("chf", 0, base), lst))
-        pick = s < 2 or h == 0
-        types = TYPES0 if gs == 0 else TYPES.split()[2 * s + h]
+            act(A(wd, Y, top, 16), A("pl", L * (t - 1) + i0, L * (t - 1) + i0 + H), FN.Copy)
+        gat, eg, sg = [x.split() for x in CUT["first" if gs == 0 else s, z].split("|")]
         keyw = A("key", 0, base)
         qt = A("qT%d" % t, 128 * h, 128 * h + 128)
-        for c in range(H // 32):
-            ch = n0 // 32 + c
-            f0 = i0 // 16 + 2 * c
-            ty = types[ch]
-            y = A(wd, 512 * c, 512 * c + 512)
-            src = IND(keyw, A("ku", i0 + 32 * c, i0 + 32 * c + 32))
-            terms = [(A("idb"), y)]
+        kr, rl, pe = ["%s%d" % (x, h) for x in ("kr", "rl", "pe")]
+        c0 = 16 * n0
+        Wb = tile()
+        terms, got = {}, {}
+        eu, su = [0, 0], [0, 0]
+        u = 0
+        for gi, w in enumerate(gat):
+            ty, nu = w[0], int(w[1])
+            lo, hi = 512 * u, 512 * (u + nu)
+            y = A(wd, lo, hi)
+            src = IND(keyw, A("ku", i0 + 32 * u, i0 + 32 * (u + nu)))
+            for k in range(u, u + nu):
+                terms[k] = [(A("idb"), A(wd, 512 * k, 512 * k + 512))]
             if ty == "Z":
                 cp(y, src)
             elif ty == "Y":
                 act(y, src, FN.Copy)
             elif ty in "ST":
-                kr, D = A(nx("kr", 2)), nx("E", 2)
+                D = tile()
                 if ty == "S":
-                    act(kr, src, FN.Copy)
+                    act(A(kr, c0 + lo, c0 + hi), src, FN.Copy)
                 else:
-                    cp(kr, src)
-                pz = A(wd, Y + 512 * c, Y + 512 * c + 512, 16)
-                mm([(A(D), A("idb"), kr, True, False)] + [(A(D, j, 512, 16), A("nid"), pz, False, j == 15) for j in range(16)])
-                act(y, A(D), FN.Abs)
+                    cp(A(kr, c0 + lo, c0 + hi), src)
+                for k in range(0, hi - lo, 512):
+                    pz = A(wd, Y + lo + k, Y + lo + k + 512, 16)
+                    mm([(A(D, k, k + 512), A("idb"), A(kr, c0 + lo + k, c0 + lo + k + 512), True, False)]
+                       + [(A(D, k + j, k + 512, 16), A("nid"), pz, False, j == 15) for j in range(16)])
+                act(y, A(D, 0, hi - lo), FN.Abs)
             else:
-                pe = A(nx("pe", 3))
-                scan(pe, A("mask"), A(wd, Y + 512 * c, Y + 512 * c + 512), OP.mult, OP.add)
-                tt(y, src, pe, OP.subtract)
+                scan(A(pe, c0 + lo, c0 + hi), A("ramp", 0, hi - lo), A(wd, Y + lo, Y + hi), OP.min, OP.add)
+                tt(y, src, A(pe, c0 + lo, c0 + hi), OP.subtract)
                 if ty == "R":
-                    rl = A(nx("rl", 4))
-                    ts(rl, y, 0.0, OP.max)
-                    terms = [(A("two"), rl), (A("nid"), y)]
+                    ts(A(rl, c0 + lo, c0 + hi), y, 0.0, OP.max)
+                    for k in range(u, u + nu):
+                        terms[k] = [(A("two"), A(rl, c0 + 512 * k, c0 + 512 * k + 512)), (A("nid"), A(wd, 512 * k, 512 * k + 512))]
                 else:
                     act(y, y, FN.Abs)
-            E = A(nx("E", 2))
-            mm(acc(E, [(qt, A("eq", 512 * ch, 512 * ch + 512))] + terms))
-            act(F4(f0, f0 + 2), E, FN.Abs)
-            if c % 2 == 1:
-                o = A(Wb, 32 * (c - 1), 32 * (c + 1))
-                mm(acc(o, [(A("idh"), A("sth", 32 * (c - 1), 32 * (c + 1)))]
-                       + [(A("bgb", 15 - u, 143 - u), F4(f0 - 2, f0 + 2, u)) for u in range(16)]))
-            if c == 0 and pick:
-                act(kc, IND(A("chf", 0, base), lst), FN.Identity, bias=A("cf", 7, 8))
+            for k in range(u, u + nu):
+                got[k] = max(x for x in range(len(nodes)) if nodes[x]["rd"][:1] == keyw[1])
+            u += nu
+            if gi == 0:
+                if s < 2:
+                    ts(A("kc", i0, i0 + H), A("ku", i0, i0 + H), -2048.0, OP.add)
                 if h == 0 and s > 0:
-                    act(A("rr", 128 * (s - 1) + n0, 128 * (s - 1) + n0 + H), kc, FN.Identity, bias=A("cf", 8, 9))
-        oi, oj, ou = [A(x, i0 // 16, i0 // 16 + K) for x in ("oi", "oj", "ou")]
+                    act(A("rr", 128 * (s - 1) + n0, 128 * (s - 1) + n0 + H), IND(A("chf", 0, base), lst), FN.Copy)
+            while eu[0] < len(eg) and eu[1] + int(eg[eu[0]]) <= u:
+                a, ne = eu[1], int(eg[eu[0]])
+                E = tile()
+                for k in range(ne):
+                    full = acc(A(E, 512 * k, 512 * k + 512), [(qt, A("eq", c0 + 512 * (a + k), c0 + 512 * (a + k + 1)))] + terms[a + k])
+                    if par["SPLIT"]:
+                        mm(full[:1])
+                        nodes[-1]["after"] = [got[a + k]]
+                        mm(full[1:])
+                    else:
+                        mm(full)
+                act(F4(k0 + 2 * a, k0 + 2 * (a + ne)), A(E, 0, 512 * ne), FN.Abs)
+                eu = [eu[0] + 1, a + ne]
+                while su[0] < len(sg) and su[1] + int(sg[su[0]]) <= eu[1]:
+                    a, ns = su[1], int(sg[su[0]])
+                    mm(acc(A(Wb, 32 * a, 32 * (a + ns)), [(A("idh"), A("sth", 32 * a, 32 * (a + ns)))]
+                           + [(A("bgb", 15 - x, 143 - x), F4(k0 + 2 * a, k0 + 2 * (a + ns), x)) for x in range(16)]))
+                    su = [su[0] + 1, a + ns]
+        oi, oj, ou = A("oi", k0, k0 + K), A("oj", 16 * s + k0, 16 * s + k0 + K), A("ou", k0, k0 + K)
         scan(A("sc", i0, i0 + H), A("rst%d" % (t % 2), 0, H), A(Wb, 0, H), OP.max, OP.min)
         cp(oi, A("sc", i0 + 15, i0 + H, 16))
         ts(oj, oi, 4095, OP.bitwise_and)
         cp(ou, oj)
-        if pick:
-            nm, lo = ("sela", 128 * s + n0) if h == 0 else ("selb", n0)
-            tt(A(nm, lo, lo + H), IND(A("tab"), ou), kc, OP.min)
-            if s < 2:
-                Wc = A(nx("W", 2), 0, K)
-                mm(acc(Wc, [(A("bgh", 15 - u, 143 - u), A(nm, lo + u, lo + H, 16)) for u in range(16)]))
-                ts(A("vl%d" % h, 8 * s + k0, 8 * s + k0 + K), Wc, 2.0 ** -12, OP.mult, 32768.0, OP.add)
         if s < 2:
-            act(A(wn, Y, 2 * Y, 16), IND(A(wd), ou), FN.Abs)
+            nm, lo = ("sela", 128 * s + n0) if h == 0 else ("selb", n0)
+            tt(A(nm, lo, lo + H), IND(A("tab", 0, top), ou), A("kc", i0, i0 + H), OP.min)
+            Wc = A(tile(), 0, K)
+            mm(acc(Wc, [(A("bgh", 15 - x, 143 - x), A(nm, lo + x, lo + H, 16)) for x in range(16)]))
+            ts(A("vl", 16 * s + k0, 16 * s + k0 + K), Wc, 2.0 ** -12, OP.mult, 32768.0, OP.add)
+            act(A(wn, Y, top, 16), IND(A(wd, 0, top), ou), FN.Abs)
         else:
             o = A("ps", L * t + i0, L * t + i0 + H)
-            act(o, IND(A(wd), ou), FN.Abs)
+            act(o, IND(A(wd, 0, top), ou), FN.Abs)
+            if h == 0:
+                act(A("oh", 128 + n0, 128 + n0 + H), IND(A("tab", 0, top), ou), FN.Relu, 1.0 / 4096)
             dst = A("pl", L * t + i0, L * t + i0 + H)
-            sem = T.sem["ap%d" % (NS * t + z)]
+            sem = T.sem["ap%d" % (4 * t + i0 // 64)]
             a = node("G", lambda: g.remote_dma(dst[0], o[0], sem, T.sem.ls, pid1, rid1, mask1), [o], [], 1200, remote=1)
             sent[0] += ne1
             node("R", None, [], [dst], 0, sem=sem, cnt=ne_in, after=[a], lat=3500)
@@ -378,107 +392,85 @@ def build(g, core, T, topo, rank, phys):
 
     def early(t):
         base = B + 256 * t
-        mm([(A("XB", 0, 256), A("boh"), A("sela", 0, 256), True, True)])
-        ts(A("uh"), A("XB", 0, 256), 30720.0, OP.add)
-        mm(acc(A("FB", 128, 136), [(A("sela", 0, 128), A("bsh", 0, 8)), (A("sela", 128, 256), A("bsh", 8, 16))])
-           + [(A("FB", 136, 144), A("sela", 128, 256), A("bsh", 16, 24), True, True)])
-        ts(A("pre", 8, 16), A("FB", 128, 136), 0.0, OP.not_equal, wcol, OP.mult)
-        ts(A("pre", 16, 24), A("FB", 136, 144), -2048.0, OP.is_equal)
-        tt(A("pre", 0, 8), A("pre", 8, 16), A("pre", 16, 24), OP.mult)
-        cp(A("ab"), A("vl0"))
-        tt(A("da"), A("ab"), A("dum"), OP.subtract)
-        ts(A("ab"), A("da"), 2.0 ** -16, OP.mult)
+        X = tile()
+        mm([(A(X, e, 256, 2), A("boh"), A("sela", 128 * e, 128 * e + 128), True, True) for e in range(2)])
+        ts(A("uh"), A(X, 0, 256), 30720.0, OP.add)
+        for e in range(2):
+            ts(A("ab", 8 * e, 8 * e + 8), A("vl", 16 * e, 16 * e + 8), -2048.0, OP.add)
+        tt(A("da"), A("ab"), A("dmc"), OP.subtract)
+        tt(A("pre", 0, 8), A("ab", 0, 8), A("ab", 8, 16), OP.not_equal)
+        ts(A("j15"), A("oj", 16, 24), 15, OP.bitwise_and)
+        ts(A("pre", 8, 16), A("j15"), 15.0, OP.is_lt, A("rst%d" % (t % 2), 0, 1), OP.mult)
+        tt(A("pre", 16, 24), A("pre", 0, 8), A("pre", 8, 16), OP.mult)
         if t < NT - 1:
             for e in range(2):
-                act(A("key", base + e, base + 256, 2), IND(A("key", 0, base), A("vl0", 8 * e, 8 * e + 8)), FN.Copy)
+                act(A("key", base + e, base + 256, 2), IND(A("key", 0, base), A("vl", 16 * e, 16 * e + 8)), FN.Copy)
         ts(A("oh", 0, 128), A("sela", 128, 256), -2048.0, OP.is_gt)
-        o1 = A("oh", 0, 128)
-        mm([(A("XB", 128 * k, 128 * k + 128), A(nm), o1, True, True) for k, nm in enumerate(("tle", "tgt", "tsh", "idb"))])
-        tt(A("t1", 0, 128), A("XB", 0, 128), A("rr", 0, 128), OP.mult)
-        tt(A("t4", 0, 128), A("XB", 128, 256), A("rr", 0, 128), OP.mult)
-        tt(A("t2"), A("XB", 256, 384), A("mt", 128 * t, 128 * t + 128), OP.mult)
-        tt(A("t3"), A("XB", 384, 512), A("ni", 128 * t, 128 * t + 128), OP.mult)
-        tt(A("t4", 0, 128), A("t4", 0, 128), A("t3"), OP.add)
-
-    def diffs(q):
-        D = nx("E", 2)
-        lst = []
-        for e in range(2):
-            for f in range(2):
-                lst += acc(A(D, 256 * e + 128 * f, 256 * e + 128 * f + 128),
-                           [(A("uh", 128 * e, 128 * e + 128), A("gp", 128 * q, 128 * q + 128)),
-                            (A("gn", 128 * q, 128 * q + 128), A("uh", 128 * f, 128 * f + 128))])
-        mm(lst)
-        if q < DIRECT:
-            nodes[-1]["rd"].append(("wc", 8, 16))
-        return D
-
-    def middle(t):
-        for q in range(DIRECT, 8):
-            act(A("db", 512 * q, 512 * q + 512), A(diffs(q)), FN.Copy)
+        X = tile()
+        mm([(A(X, 128 * k, 128 * k + 128), A(nm), A("oh", 0, 128), True, True) for k, nm in enumerate(("tle", "tgt", "tsh", "idb"))])
+        tt(A("t1", 0, 128), A(X, 0, 128), A("rr", 0, 128), OP.mult)
+        tt(A("t4", 0, 128), A(X, 128, 256), A("rr", 0, 128), OP.mult)
+        tt(A(X, 256, 384), A(X, 256, 384), A("mt", 128 * t, 128 * t + 128), OP.mult)
+        tt(A(X, 384, 512), A(X, 384, 512), A("ni", 128 * t, 128 * t + 128), OP.mult)
+        tt(A("t1", 0, 128), A(X, 256, 384), A("t1", 0, 128), OP.add)
+        tt(A("t4", 0, 128), A(X, 384, 512), A("t4", 0, 128), OP.add)
 
     def late(t):
         base = B + 256 * t
-        mm([(A("FB", 144, 152), A("sela", 256, 384), A("bsh", 0, 8), True, True)])
-        ts(A("wc", 8, 16), A("FB", 144, 152), -32767.5, OP.is_gt)
-        tt(A("wc", 0, 8), A("wc", 8, 16), A("pre", 0, 8), OP.mult)
-        order = list(range(DIRECT, 8)) + list(range(DIRECT))
-        for q in order:
-            src = A("db", 512 * q, 512 * q + 512) if q >= DIRECT else A(diffs(q))
-            ts(A("eqw", 512 * q, 512 * q + 512), src, 0.0, OP.is_equal, A("wc", q, q + 1), OP.mult)
-        full = acc(A("FB", 0, 128), [(A("og", 112 - 16 * q, 240 - 16 * q), A("eqw", 512 * q + 128 * e, 512 * q + 128 * e + 128))
-                                     for q in order for e in range(4)])
-        for k in range(0, 32, 8):
-            mm(full[k:k + 8])
-        ts(A("oh", 128, 256), A("sela", 256, 384), -2048.0, OP.is_gt)
-        o2 = A("oh", 128, 256)
-        mm([(A("XB", 128 * k, 128 * k + 128), A(nm), o2, True, True) for k, nm in enumerate(("tle", "tgt"))])
-        tt(A("t1", 128, 256), A("XB", 0, 128), A("rr", 128, 256), OP.mult)
-        tt(A("t4", 128, 256), A("XB", 128, 256), A("rr", 128, 256), OP.mult)
-        tt(A("hi"), A("FB", 0, 128), A("whi"), OP.is_lt)
-        tt(A("lo"), A("FB", 0, 128), A("wlo"), OP.is_gt)
-        tt(A("st"), A("hi"), A("lo"), OP.mult)
+        tt(A("pre", 24, 32), A("sc", 15, 128, 16), A("pre", 16, 24), OP.is_lt)
+        order = [(0, 0)] + [(k, e) for k in range(1, 8) for e in range(2)] + [(0, 1)]
+        at = 0
+        F = tile()
+        for x, (k, e) in enumerate(order):
+            n = 256 - 32 * k
+            ts(A("eqw", at, at + n), A("uh", 32 * k, 256), A("ab", 8 * e + k, 8 * e + k + 1), OP.is_equal, A("pre", 24 + k, 25 + k), OP.mult)
+            mm([(A(F, 16 * k, 128), A("wk", 128 * k, 128 * k + 128), A("eqw", at + f, at + n, 2), x + f == 0, x + f == 16) for f in range(2)])
+            at += n
+        tt(A("hi"), A(F, 0, 128), A("whi"), OP.is_lt)
+        tt(A("lo"), A(F, 0, 128), A("wlo"), OP.is_gt)
+        X = tile()
+        mm([(A(X, 128 * k, 128 * k + 128), A(nm), A("oh", 128, 256), True, True) for k, nm in enumerate(("tle", "tgt"))])
+        tt(A("t1", 128, 256), A(X, 0, 128), A("rr", 128, 256), OP.mult)
+        tt(A("t4", 128, 256), A(X, 128, 256), A("rr", 128, 256), OP.mult)
+        X = tile()
+        mm([m for e in range(2) for m in acc(A(X, e, 128, 2), [(A("idb"), A(nm, f, 128, 2)) for nm in ("hi", "lo") for f in range(2)])])
+        act(A("fl"), A(X, 0, 128), FN.Relu, acc=A("zc", 0, 1) if t < NT - 1 else None, bias=A("cf", 7, 8))
+        F, X = tile(), tile()
+        mm(acc(A(F, 0, 8), [(A("bg1", 15 - x, 143 - x), A("fl", x, 128, 16)) for x in range(16)]))
+        mm([(A(X, 0, 128), A("idb"), A("fl"), True, True)] + ([(A(X, 128, 129), A("six"), A("zc", 0, 1), True, True)] if t < NT - 1 else []))
         for e in range(2):
-            tt(A("fl", e, 128, 2), A("st", 0, 128, 2), A("st", 1, 128, 2), OP.mult)
-        mm(acc(A("FB", 160, 168), [(A("bgb", 15 - u, 143 - u), A("fl", u, 128, 16)) for u in range(16)]))
-        for e in range(2):
-            tt(A("of", 8 * e, 8 * e + 8), A("FB", 160, 168), A("ab", 8 * e, 8 * e + 8), OP.mult)
+            tt(A("of", 8 * e, 8 * e + 8), A(F, 0, 8), A("da", 8 * e, 8 * e + 8), OP.mult)
         tt(A("og2"), A("of"), A("dum"), OP.add)
         cp(A("so"), A("og2"))
         tb = "chf" if t < NT - 1 else "cho"
-        tt(IND(A(tb), A("so", 0, 8)), A("t1", 0, 128), A("t2"), OP.add)
-        cp(IND(A(tb), A("so", 8, 16)), A("t1", 128, 256))
         for e in range(2):
-            tt(A(tb, base + e, base + 256, 2), A("t4", 128 * e, 128 * e + 128), A("fl"), OP.mult)
+            tt(A(tb, base + e, base + 256, 2), A(X, 0, 128), A("t4", 128 * e, 128 * e + 128), OP.mult)
+        cp(IND(A(tb), A("so")), A("t1"))
         if t < NT - 1:
-            mm([(A("XB", 256, 384), A("six"), A("fl"), True, True)])
-            act(A("zj"), A("XB", 256, 384), FN.Identity, 1.0, A("zc", 0, 1))
-            cp(A("zi", 0, 1), A("zc", 0, 1))
+            cp(A("zi", 0, 1), A(X, 128, 129))
             ts(A("zk", 0, 1), A("zi", 0, 1), 63, OP.bitwise_and)
             ts(A("za", 0, 1), A("zk", 0, 1), 4096.0, OP.mult)
             ts(A("rst%d" % ((t + 1) % 2), 0, 128, 16), A("rb"), A("za", 0, 1), OP.add)
+        else:
+            dma("Y", T.yc[:], T.cho[:, 0:W], [A("cho", 0, W)], [], 9000)
 
-    def store():
-        dma("Y", T.yc[:], T.cho[:, 0:W], [A("cho", 0, W)], [], 9000)
+    def copy_rows(t):
+        top = B + 256 * t
+        dma("Y", T.cho[:, 0:top], T.chf[:, 0:top], [A("chf", 0, top)], [A("cho", 0, top)], 9000)
+        cp(A("cho", 0, 1), A("ch0", 0, 1))
 
     for t in range(NT):
-        if t == NT - 1:
-            top = B + 256 * t
-            dma("Y", T.cho[:, 0:top], T.chf[:, 0:top], [A("chf", 0, top)], [A("cho", 0, top)], 9000)
-            cp(A("cho", 0, 1), A("ch0", 0, 1))
-        for w in (ORDER if t < NT - 1 else ORDERL).split():
-            if w[0] in "AB":
-                for z in range(NS // 2):
-                    step(t, int(w[1]), "AB".index(w[0]) * NS // 2 + z)
+        for w in ORDER[t].split():
+            v = t - w.count("'")
+            w = w.strip("'")
+            if w[0] in STREAM:
+                step(v, int(w[1]), w[0], {"": "all", "k": "kids", "r": "rest"}[w[2:]])
             else:
-                {"e": early, "m": middle, "l": late}[w](t)
-                if w == "l" and t == NT - 1:
-                    store()
+                {"c": constants, "e": early, "l": late, "o": copy_rows}[w](v)
     return nodes, sent[0]
 
 
-def plan(nodes):
-    n = len(nodes)
+def depend(nodes):
     hist = {}
     deps = []
     for i, d in enumerate(nodes):
@@ -497,7 +489,7 @@ def plan(nodes):
         for j in d.get("after", []):
             dd[j] = False
         for regs, w in ((d["rd"], False), (d["wr"], True)):
-            for nm, lo, hi in set(regs):
+            for nm, lo, hi in sorted(set(regs)):
                 h = hist.setdefault(nm, [])
                 if isps(nm):
                     h[:] = [e for e in h if nodes[e[0]]["eng"] == d["eng"]]
@@ -506,77 +498,124 @@ def plan(nodes):
                 h.append((i, lo, hi, w))
         dd.pop(i, None)
         deps.append(dd)
-    LAT = 70
-    succ = [[] for _ in range(n)]
+    return deps
+
+
+def place(nodes, seq, before, lat):
+    busy = {e: [] for e in "VSPGYR"}
+    start = [0.0] * len(nodes)
+    for i in seq:
+        c = nodes[i]["cost"]
+        t0 = max([0.0] + [start[j] + nodes[j]["cost"] + x for j, x in before[i]])
+        iv = busy[nodes[i]["eng"]]
+        k = len(iv)
+        while k > 0 and iv[k - 1][1] > t0:
+            k -= 1
+        while k < len(iv) and iv[k][0] < t0 + c:
+            t0 = max(t0, iv[k][1])
+            k += 1
+        iv.insert(k, (t0, t0 + c))
+        start[i] = t0
+    return start, max(start[i] + nodes[i]["cost"] + lat[i] for i in seq)
+
+
+def ordered(n, deps, key):
+    seq, seen = [], set()
+    for r in sorted(range(n), key=lambda i: (key[i], i)):
+        stack = [r]
+        while stack:
+            i = stack[-1]
+            todo = [j for j in deps[i] if j not in seen]
+            if i in seen:
+                stack.pop()
+            elif todo:
+                stack.append(min(todo, key=lambda j: (key[j], j)))
+            else:
+                seen.add(i)
+                seq.append(i)
+                stack.pop()
+    return seq
+
+
+def pack(nodes, deps, key, par):
+    n = len(nodes)
+    lat = [d.get("lat", 0) for d in nodes]
+    before = [[(j, lat[j] + (par["LAT"] if w else 0)) for j, w in deps[i].items()] for i in range(n)]
+    after = [[] for _ in range(n)]
     for i in range(n):
-        for j in deps[i]:
-            succ[j].append(i)
-    rank = [0.0] * n
-    for i in range(n - 1, -1, -1):
-        rank[i] = nodes[i]["cost"] + nodes[i].get("lat", 0) + max([rank[k] + LAT for k in succ[i]] + [0])
-    x = SEED
+        for j, x in before[i]:
+            after[j].append((i, x))
     for i in range(n):
-        x = (x * 1103515245 + 12345) % 2147483648
-        rank[i] += NOISE * (x / 2147483648.0)
-    left = [len(deps[i]) for i in range(n)]
-    ready = {e: [] for e in "VSPGYR"}
-    at = [0.0] * n
-    fin = [0.0] * n
-    free = {e: 0.0 for e in ready}
-    order = {e: [] for e in ready}
-    for i in range(n):
-        if left[i] == 0:
-            ready[nodes[i]["eng"]].append(i)
-    users, first = {}, {}
+        if not after[i]:
+            after[i].append((n, lat[i]))
+    ext = nodes + [{"eng": "R", "cost": 0}]
+    seq = ordered(n, deps, key)
+    best = None
+    for _ in range(par["ROUNDS"]):
+        start, end = place(nodes, seq, before, lat)
+        if best is None or end < best[1]:
+            best = (start, end)
+        pos = {i: k for k, i in enumerate(seq)}
+        rev = sorted(range(n), key=lambda i: (-start[i] - nodes[i]["cost"], -pos[i]))
+        back, _e = place(ext, [n] + rev, after + [[]], lat + [0])
+        pos = {i: k for k, i in enumerate(rev)}
+        seq = sorted(range(n), key=lambda i: (-back[i] - nodes[i]["cost"], -pos[i]))
+    return best
+
+
+def banks(nodes, base, start):
+    deps = [dict(d) for d in base]
+    users = {}
     for i, d in enumerate(nodes):
-        for nm in set(r[0] for r in d["rd"] + d["wr"] if "#" in r[0]):
-            if nm not in users:
-                users[nm] = []
-                first[i] = nm
-            users[nm].append(i)
-    open_ = {nm: len(u) for nm, u in users.items()}
-    held = {b: None for p in POOL.values() for b in p}
+        for nm in sorted(set(r[0] for r in d["rd"] + d["wr"] if isps(r[0]))):
+            users.setdefault(nm.split("/")[0], {}).setdefault(int(nm.split("/")[1]), []).append(i)
+    held = [[] for _ in range(8)]
     phys = {}
 
-    def slot(k):
-        bs = [(0.0 if held[b] is None else max(fin[j] for j in users[held[b]]) + LAT, b)
-              for b in POOL[first[k].split("#")[0]] if held[b] is None or open_[held[b]] == 0]
-        return min(bs) if bs else (1e18, None)
+    def needs(js, first):
+        seen, stack = set(), list(js)
+        while stack:
+            j = stack.pop()
+            if j in first:
+                return True
+            if j not in seen and start[j] >= min(start[f] for f in first) - 1e-6:
+                seen.add(j)
+                stack.extend(deps[j])
+        return False
 
-    done = 0
-    while done < n:
-        best = None
-        eff = {}
-        for e in ready:
-            for k in ready[e]:
-                eff[k] = max(at[k], slot(k)[0]) if k in first else at[k]
-            if ready[e]:
-                t0 = max(free[e], min(eff[i] for i in ready[e]))
-                if best is None or t0 < best[0]:
-                    best = (t0, e)
-        t0, e = best
-        i = max((k for k in ready[e] if eff[k] <= t0 + SLACK), key=lambda k: (rank[k] - BETA * k, -k))
-        ready[e].remove(i)
-        t0 = max(t0, eff[i])
-        if i in first:
-            b = slot(i)[1]
-            if held[b] is not None:
-                for j in users[held[b]]:
-                    deps[i][j] = deps[i].get(j, False) or not (e == "P" and nodes[j]["eng"] == "P")
-            held[b] = first[i]
-            phys[first[i]] = b
-        free[e] = t0 + nodes[i]["cost"]
-        fin[i] = free[e] + nodes[i].get("lat", 0)
-        for nm in set(r[0] for r in nodes[i]["rd"] + nodes[i]["wr"] if "#" in r[0]):
-            open_[nm] -= 1
-        order[e].append(i)
-        done += 1
-        for k in succ[i]:
-            at[k] = max(at[k], fin[i] + (LAT if deps[k][i] else 0))
-            left[k] -= 1
-            if left[k] == 0:
-                ready[nodes[k]["eng"]].append(k)
-    return deps, order, fin, phys
+    for nm in sorted(users, key=lambda nm: min((start[u[0]], u[0]) for u in users[nm].values())):
+        n = len(users[nm])
+        first = set(u[0] for u in users[nm].values())
+        t0 = min(start[f] for f in first)
+        opts = []
+        for b in range(0, 8, n):
+            old = [j for k in range(n) for j in held[b + k]]
+            end = max([0.0] + [start[j] + nodes[j]["cost"] for j in old])
+            opts.append((max(end, t0 - 3000), b, old))
+        b = [o[1] for o in sorted(opts) if not needs(o[2], first)][0]
+        phys[nm] = b
+        for k in range(n):
+            i = users[nm][k][0]
+            for j in held[b + k]:
+                deps[i][j] = deps[i].get(j, False) or not (nodes[i]["eng"] == "P" and nodes[j]["eng"] == "P")
+            held[b + k] = users[nm][k]
+    return deps, phys
+
+
+def plan(nodes, par=None):
+    par = par or PAR
+    n = len(nodes)
+    base = depend(nodes)
+    start, _e = pack(nodes, base, list(range(n)), par)
+    best = None
+    for _ in range(par["PASSES"]):
+        deps, phys = banks(nodes, base, start)
+        start, end = pack(nodes, deps, start, par)
+        if best is None or end < best[0]:
+            best = (end, start, deps, phys)
+    end, start, deps, phys = best
+    order = {e: sorted((i for i in range(n) if nodes[i]["eng"] == e), key=lambda i: (start[i], i)) for e in "VSPGYR"}
+    return deps, order, [start[i] + nodes[i]["cost"] + nodes[i].get("lat", 0) for i in range(n)], phys
 
 
 def rank_program(g, core, T, topo):
@@ -585,37 +624,45 @@ def rank_program(g, core, T, topo):
         return
     deps, order, fin, phys = plan(build(g, core, T, topo, rank, {})[0])
     nodes, sent = build(g, core, T, topo, rank, phys)
+    n = len(nodes)
     queue = {"V": g.vector, "S": g.scalar, "P": g.tensor, "G": g, "Y": g.sync}
     esem = {"V": T.sem.sV, "S": T.sem.sS, "P": T.sem.sP, "G": T.sem.sG}
-    need = set(j for i in range(len(nodes)) if nodes[i]["eng"] != "R" for j, w in deps[i].items() if w)
+    pos = {i: k for e in order for k, i in enumerate(order[e])}
+    lane = [("n%d" % i if "sem" in d else d["eng"]) for i, d in enumerate(nodes)]
+    known = {e: {} for e in order}
+    behind, waits = {}, {}
+    for i in sorted(range(n), key=lambda i: (fin[i] - nodes[i].get("lat", 0) - nodes[i]["cost"], i)):
+        kn = known[nodes[i]["eng"]]
+        waits[i] = []
+        if nodes[i]["eng"] != "R":
+            for j in sorted((j for j, w in deps[i].items() if w), key=lambda j: -fin[j]):
+                if kn.get(lane[j], -1) < pos[j]:
+                    waits[i].append(j)
+                    kn[lane[j]] = pos[j]
+                    for k, p in behind[j].items():
+                        kn[k] = max(kn.get(k, -1), p)
+            behind[i] = dict(kn)
+        else:
+            behind[i] = {}
+    need = set(j for i in waits for j in waits[i])
     mark = {}
     for e in esem:
         c = 0
         for i in order[e]:
-            if "sem" not in nodes[i] and "remote" not in nodes[i] and i in need:
+            if "sem" not in nodes[i] and i in need:
                 c += 1
-                mark[i] = (e, esem[e], c)
+                mark[i] = (esem[e], c)
     for i, d in enumerate(nodes):
         if "sem" in d:
-            mark[i] = ("n%d" % i, d["sem"], d["cnt"])
-    waited = set()
+            mark[i] = (d["sem"], d["cnt"])
     for e in queue:
-        seen = {}
         for i in order[e]:
-            want = {}
-            for j, w in deps[i].items():
-                if w:
-                    k, sem, c = mark[j]
-                    waited.add(j)
-                    if c > seen.get(k, 0) and c > want.get(k, (None, 0))[1]:
-                        want[k] = (sem, c)
-            for k, (sem, c) in want.items():
-                queue[e].wait_ge(sem, c)
-                seen[k] = c
+            for j in waits[i]:
+                queue[e].wait_ge(*mark[j])
             r = nodes[i]["emit"]()
             if i in mark and "sem" not in nodes[i]:
-                r.then_inc(mark[i][1], 1)
+                r.then_inc(mark[i][0], 1)
     for i, d in enumerate(nodes):
-        if "sem" in d and i not in waited:
+        if "sem" in d and i not in need:
             g.wait_ge(d["sem"], d["cnt"])
     g.wait_ge(T.sem.ls, sent)

@@ -1,4 +1,5 @@
 import math
+import numpy
 from concourse.bass import DstId, RemoteDMATransfer
 from concourse.mybir import AluOpType, ActivationFunctionType
 
@@ -12,9 +13,11 @@ NLOAD = 4
 STREAM = {"A": (0, 128), "B": (128, 128)}
 CUT = {}
 for _s in ("first", 0, 1, 2):
-    CUT[_s, "A"] = CUT[_s, "B"] = "Z1 Y1 Z1 Y1|1 1 1 1|2 2" if _s == "first" else "S1 X1 X1 X1|1 1 1 1|2 2"
+    CUT[_s, "A"] = "Z1 Y1 Z1 Y1|1 1 1 1|2 2" if _s == "first" else "S1 X1 X1 R1|1 1 1 1|2 2"
+    CUT[_s, "B"] = "Z1 Y1 Z1 Y1|1 1 1 1|2 2" if _s == "first" else "S1 X1 X1 X1|1 1 1 1|2 2"
 ORDER = ["A0 c B0 A1 B1 e A2 B2k l B2r"] + ["A0 B0 A1 B1 e A2 B2k l B2r"] * 2 + ["o A0 B0 A1 e B1 A2 l B2"]
-PAR = {"GF": 1.56, "SC": 3.5, "PEF": 0.5, "PMM": 8, "VO": 60, "SO": 75, "LAT": 220, "BETA": 1000, "ROUNDS": 4, "PASSES": 3, "SPLIT": 1}
+PAR = {"GF": 1.56, "SC": 3.5, "PEF": 0.5, "PMM": 8, "VO": 60, "SO": 75, "LAT": 220, "BETA": 1000, "ROUNDS": 4, "PASSES": 3, "SPLIT": 1, "SPR": 2, "PFIRST": 0, "TURN": "S", "SHAKES": 3000, "SHAKE": 300.0}
+PLAN = []
 
 f32, bf, f16, i32, u16 = "float32", "bfloat16", "float16", "int32", "uint16"
 SCRATCH = {}
@@ -24,8 +27,8 @@ for _n, _c, _d in [
     ("tab", 2 * Y, bf), ("eq", Y, bf), ("ramp", Y, bf), ("pe0", Y, bf), ("pe1", Y, bf),
     ("rl0", Y, bf), ("rl1", Y, bf), ("kr0", Y, bf), ("kr1", Y, bf),
     ("ku", 256, u16), ("kc", 256, f16), ("vl", 32, u16),
-    ("sc", 256, f32), ("oi", 16, i32), ("oj", 48, i32), ("ou", 16, u16), ("sela", 256, f16), ("selb", 128, f16), ("rst0", 128, f32), ("rst1", 128, f32),
-    ("ps", 1024, bf), ("pl", 1024, bf),
+    ("sc", 256, i32), ("oj", 16, i32), ("ou", 16, u16), ("sela", 256, f16), ("selb", 128, f16), ("rst0", 128, f32), ("rst1", 128, f32),
+    ("ps", 1024, bf), ("pl", 1024, bf), ("pT0", 128, bf), ("pT1", 128, bf),
     ("ones", 128, bf), ("idb", 128, bf), ("nid", 128, bf), ("two", 128, bf), ("idh", 128, f16), ("six", 128, f32),
     ("bgb", 144, bf), ("bgh", 144, f16), ("bg1", 144, bf), ("boh", 128, f16), ("wk", 1024, bf),
     ("tle", 128, bf), ("tgt", 128, bf), ("tsh", 128, bf), ("sth", 128, f16),
@@ -307,7 +310,8 @@ def build(g, core, T, topo, rank, phys, par=None):
         Wb = tile()
         terms, got = {}, {}
         eu, su = [0, 0], [0, 0]
-        u = 0
+        u = spread = 0
+        turned = False
         for gi, w in enumerate(gat):
             ty, nu = w[0], int(w[1])
             lo, hi = 512 * u, 512 * (u + nu)
@@ -327,11 +331,30 @@ def build(g, core, T, topo, rank, phys, par=None):
                     cp(A(kr, c0 + lo, c0 + hi), src)
                 for k in range(0, hi - lo, 512):
                     pz = A(wd, Y + lo + k, Y + lo + k + 512, 16)
-                    mm([(A(D, k, k + 512), A("idb"), A(kr, c0 + lo + k, c0 + lo + k + 512), True, False)]
-                       + [(A(D, k + j, k + 512, 16), A("nid"), pz, False, j == 15) for j in range(16)])
+                    if par["TURN"]:
+                        if not turned:
+                            X = tile()
+                            mm([(A(X, 0, 128), A(wd, Y, top, 16), A("idb"), True, True)])
+                            if par["TURN"] == "S":
+                                act(A("pT%d" % h), A(X, 0, 128), FN.Copy, 1.0 / 2048)
+                            else:
+                                ts(A("pT%d" % h), A(X, 0, 128), 1.0 / 2048, OP.mult)
+                            turned = True
+                        mm([(A(D, k, k + 512), A("pT%d" % h), A("eq", lo + k, lo + k + 512), True, False)])
+                        mm([(A(D, k, k + 512), A("idb"), A(kr, c0 + lo + k, c0 + lo + k + 512), False, True)])
+                    elif par["PFIRST"]:
+                        mm([(A(D, k + j, k + 512, 16), A("nid"), pz, j == 0, False) for j in range(16)])
+                        mm([(A(D, k, k + 512), A("idb"), A(kr, c0 + lo + k, c0 + lo + k + 512), False, True)])
+                    else:
+                        mm([(A(D, k, k + 512), A("idb"), A(kr, c0 + lo + k, c0 + lo + k + 512), True, False)]
+                           + [(A(D, k + j, k + 512, 16), A("nid"), pz, False, j == 15) for j in range(16)])
                 act(y, A(D, 0, hi - lo), FN.Abs)
             else:
-                scan(A(pe, c0 + lo, c0 + hi), A("ramp", 0, hi - lo), A(wd, Y + lo, Y + hi), OP.min, OP.add)
+                if lo >= spread:
+                    kinds = "".join(x[0] * int(x[1]) for x in gat) + "."
+                    run = min(k for k in range(u, len(kinds)) if kinds[k] not in "XR") - u
+                    spread = lo + 512 * max(nu, min(run, par["SPR"]))
+                    scan(A(pe, c0 + lo, c0 + spread), A("ramp", 0, spread - lo), A(wd, Y + lo, Y + spread), OP.min, OP.add)
                 tt(y, src, A(pe, c0 + lo, c0 + hi), OP.subtract)
                 if ty == "R":
                     ts(A(rl, c0 + lo, c0 + hi), y, 0.0, OP.max)
@@ -365,11 +388,12 @@ def build(g, core, T, topo, rank, phys, par=None):
                     mm(acc(A(Wb, 32 * a, 32 * (a + ns)), [(A("idh"), A("sth", 32 * a, 32 * (a + ns)))]
                            + [(A("bgb", 15 - x, 143 - x), F4(k0 + 2 * a, k0 + 2 * (a + ns), x)) for x in range(16)]))
                     su = [su[0] + 1, a + ns]
-        oi, oj, ou = A("oi", k0, k0 + K), A("oj", 16 * s + k0, 16 * s + k0 + K), A("ou", k0, k0 + K)
+        ou = A("ou", k0, k0 + K)
         scan(A("sc", i0, i0 + H), A("rst%d" % (t % 2), 0, H), A(Wb, 0, H), OP.max, OP.min)
-        cp(oi, A("sc", i0 + 15, i0 + H, 16))
-        ts(oj, oi, 4095, OP.bitwise_and)
-        cp(ou, oj)
+        ts(A("oj", k0, k0 + K), A("sc", i0 + 15, i0 + H, 16), 4095, OP.bitwise_and)
+        cp(ou, A("oj", k0, k0 + K))
+        if h == 0 and s == 1:
+            ts(A("j15", k0, k0 + K), A("sc", i0 + 15, i0 + H, 16), 15, OP.bitwise_and)
         if s < 2:
             nm, lo = ("sela", 128 * s + n0) if h == 0 else ("selb", n0)
             tt(A(nm, lo, lo + H), IND(A("tab", 0, top), ou), A("kc", i0, i0 + H), OP.min)
@@ -399,7 +423,6 @@ def build(g, core, T, topo, rank, phys, par=None):
             ts(A("ab", 8 * e, 8 * e + 8), A("vl", 16 * e, 16 * e + 8), -2048.0, OP.add)
         tt(A("da"), A("ab"), A("dmc"), OP.subtract)
         tt(A("pre", 0, 8), A("ab", 0, 8), A("ab", 8, 16), OP.not_equal)
-        ts(A("j15"), A("oj", 16, 24), 15, OP.bitwise_and)
         ts(A("pre", 8, 16), A("j15"), 15.0, OP.is_lt, A("rst%d" % (t % 2), 0, 1), OP.mult)
         tt(A("pre", 16, 24), A("pre", 0, 8), A("pre", 8, 16), OP.mult)
         if t < NT - 1:
@@ -602,6 +625,26 @@ def banks(nodes, base, start):
     return deps, phys
 
 
+def polish(nodes, deps, start, end, par):
+    n = len(nodes)
+    lat = [d.get("lat", 0) for d in nodes]
+    before = [[(j, lat[j] + (par["LAT"] if w else 0)) for j, w in deps[i].items()] for i in range(n)]
+    seq = sorted(range(n), key=lambda i: (start[i], i))
+    rng = numpy.random.default_rng(1)
+    for _ in range(par["SHAKES"]):
+        a = rng.random() * end
+        noise = rng.normal(0.0, par["SHAKE"], n)
+        key = [start[i] + (float(noise[i]) if a < start[i] < a + 8000 else 0.0) for i in range(n)]
+        for i in seq:
+            for j in deps[i]:
+                if key[j] >= key[i]:
+                    key[i] = key[j] + 0.01
+        s1, e1 = place(nodes, sorted(range(n), key=lambda i: (key[i], i)), before, lat)
+        if e1 <= end:
+            start, end = s1, e1
+    return start
+
+
 def plan(nodes, par=None):
     par = par or PAR
     n = len(nodes)
@@ -614,6 +657,7 @@ def plan(nodes, par=None):
         if best is None or end < best[0]:
             best = (end, start, deps, phys)
     end, start, deps, phys = best
+    start = polish(nodes, deps, start, end, par)
     order = {e: sorted((i for i in range(n) if nodes[i]["eng"] == e), key=lambda i: (start[i], i)) for e in "VSPGYR"}
     return deps, order, [start[i] + nodes[i]["cost"] + nodes[i].get("lat", 0) for i in range(n)], phys
 
@@ -622,7 +666,9 @@ def rank_program(g, core, T, topo):
     rank = T.rank_of(core)
     if rank is None:
         return
-    deps, order, fin, phys = plan(build(g, core, T, topo, rank, {})[0])
+    if not PLAN:
+        PLAN.append(plan(build(g, core, T, topo, rank, {})[0]))
+    deps, order, fin, phys = PLAN[0]
     nodes, sent = build(g, core, T, topo, rank, phys)
     n = len(nodes)
     queue = {"V": g.vector, "S": g.scalar, "P": g.tensor, "G": g, "Y": g.sync}

@@ -16,32 +16,32 @@ for _s in ("first", 0, 1, 2):
     CUT[_s, "A"] = "Z1 Y1 Z1 Y1|1 1 1 1|2 2" if _s == "first" else "S1 X1 X1 R1|1 1 1 1|2 2"
     CUT[_s, "B"] = "Z1 Y1 Z1 Y1|1 1 1 1|2 2" if _s == "first" else "S1 X1 X1 X1|1 1 1 1|2 2"
 ORDER = ["A0 c B0 A1 B1 e A2 B2k l B2r"] + ["A0 B0 A1 B1 e A2 B2k l B2r"] * 2 + ["o A0 B0 A1 e B1 A2 l B2"]
-PAR = {"GF": 1.56, "SC": 3.5, "PEF": 0.5, "PMM": 8, "VO": 60, "SO": 75, "LAT": 220, "BETA": 1000, "ROUNDS": 4, "PASSES": 3, "SPLIT": 1, "SPR": 2, "PFIRST": 0, "TURN": "S", "SHAKES": 3000, "SHAKE": 300.0}
+PAR = {"GF": 1.56, "SC": 3.5, "PEF": 0.5, "PMM": 8, "VO": 60, "SO": 75, "LAT": 220, "BETA": 1000, "ROUNDS": 4, "PASSES": 3, "SPLIT": 1, "SPR": 1, "PFIRST": 0, "TURN": "V", "COPY": 0, "LIST": "AB", "SHAKES": 5000, "SHAKE": 500.0, "STRETCH": 3000, "SEED": 2}
 PLAN = []
 
 f32, bf, f16, i32, u16 = "float32", "bfloat16", "float16", "int32", "uint16"
 SCRATCH = {}
 for _n, _c, _d in [
-    ("chi", B, i32), ("chf", WD, f32), ("cho", WD, f32), ("key", W, bf), ("ch0", 4, f32), ("qraw", L, bf), ("hvi", 64, i32), ("hvu", 64, u16),
+    ("chi", B, i32), ("chf", WD, f32), ("cho", WD, f32), ("chp", WD, f32), ("key", W, bf), ("ch0", 4, f32), ("qraw", L, bf), ("hvi", 64, i32), ("hvu", 64, u16),
     ("qT0", L, bf), ("qT1", L, bf), ("qT2", L, bf), ("qT3", L, bf), ("hl1", 16, u16), ("hl2", 16, u16), ("hl3", 16, u16),
     ("tab", 2 * Y, bf), ("eq", Y, bf), ("ramp", Y, bf), ("pe0", Y, bf), ("pe1", Y, bf),
     ("rl0", Y, bf), ("rl1", Y, bf), ("kr0", Y, bf), ("kr1", Y, bf),
     ("ku", 256, u16), ("kc", 256, f16), ("vl", 32, u16),
-    ("sc", 256, i32), ("oj", 16, i32), ("ou", 16, u16), ("sela", 256, f16), ("selb", 128, f16), ("rst0", 128, f32), ("rst1", 128, f32),
+    ("sc", 256, i32), ("oj", 16, i32), ("ou", 16, u16), ("vs", 256, f32), ("cut", 128, f32), ("sela", 256, f16), ("selb", 128, f16), ("rst0", 128, f32), ("rst1", 128, f32),
     ("ps", 1024, bf), ("pl", 1024, bf), ("pT0", 128, bf), ("pT1", 128, bf),
     ("ones", 128, bf), ("idb", 128, bf), ("nid", 128, bf), ("two", 128, bf), ("idh", 128, f16), ("six", 128, f32),
-    ("bgb", 144, bf), ("bgh", 144, f16), ("bg1", 144, bf), ("boh", 128, f16), ("wk", 1024, bf),
+    ("bgb", 144, bf), ("bgh", 144, f16), ("bg2", 144, bf), ("boh", 128, f16), ("wk", 1024, bf),
     ("tle", 128, bf), ("tgt", 128, bf), ("tsh", 128, bf), ("sth", 128, f16),
-    ("ci", 8, i32), ("cf", 12, f32), ("w1", 144, f32), ("w2", 144, f32), ("w3", 128, f32), ("w4", 128, f32), ("w5", 128, f32), ("wi", 128, i32),
-    ("whi", 128, f32), ("wlo", 128, f32), ("wl", 16, f32), ("mt", 512, f32), ("ni", 512, f32), ("dum", 16, f32), ("dmc", 16, f32), ("rb", 8, f32),
+    ("ci", 8, i32), ("cf", 12, f32), ("w1", 144, f32), ("w2", 144, f32), ("w3", 128, f32), ("w4", 128, f32), ("w5", 128, f32), ("w6", 144, bf), ("wi", 128, i32),
+    ("whi", 128, f32), ("wl", 16, f32), ("mt", 512, f32), ("ni", 512, f32), ("dum", 16, f32), ("dmc", 16, f32), ("rb", 8, f32),
     ("uh", 256, f16), ("eqw", 2304, bf), ("oh", 256, bf), ("rr", 256, f32), ("t1", 256, f32), ("t4", 256, f32),
-    ("pre", 32, f32), ("j15", 8, i32), ("hi", 128, bf), ("lo", 128, bf),
-    ("fl", 128, bf), ("ab", 16, f32), ("da", 16, f32), ("of", 16, f32), ("og2", 16, f32), ("so", 16, u16),
+    ("pre", 24, f32), ("cand", 8, f32), ("cw", 8, bf), ("j15", 8, i32), ("hi", 128, bf), ("st", 128, bf), ("alt", 128, bf), ("nil", 128, bf),
+    ("own", Y, bf), ("fl", 64, bf), ("ab", 16, f32), ("da", 32, f32), ("og2", 32, f32), ("so", 16, u16),
     ("zc", 4, f32), ("zi", 4, i32), ("zk", 4, i32), ("za", 4, f32),
 ]:
     SCRATCH[_n] = ("sbuf", [128, _c], _d)
 SCRATCH["fa"] = ("sbuf", [128, 16, 16, 16], bf)
-for _n in "AaBb":
+for _n in "AaB":
     SCRATCH["wd%s0" % _n] = ("sbuf", [128, 2 * Y], bf)
     SCRATCH["wd%s1" % _n] = ("sbuf", [128, 2 * Y], bf)
 for _n in range(4):
@@ -183,6 +183,7 @@ def build(g, core, T, topo, rank, phys, par=None):
     for k in range(NLOAD):
         dma("Y", T.chi[:, k * cw:(k + 1) * cw], T.ch[:, k * cw:(k + 1) * cw], [], [A("chi", k * cw, (k + 1) * cw)], 2500 + 1100 * (k + 1))
     dma("Y", T.key[:, 0:B], T.kb[:], [], [A("key", 0, B)], 9000)
+    keys = len(nodes) - 1
     ms(A("ones"), 1.0)
     ms(A("tab", Y, 2 * Y), -2048.0)
     iota(A("ci", 0, 1), [[0, 1]], 0, 1)
@@ -219,9 +220,11 @@ def build(g, core, T, topo, rank, phys, par=None):
     act(A("qT0"), A(X, 0, 256), FN.Copy, 1.0 / 2048)
     act(A("nid"), A("idb"), FN.Copy, -1.0)
     act(A("two"), A("idb"), FN.Copy, 2.0)
-    for k in range(2):
-        for z in STREAM:
-            act(A("wd%s%d" % (z, k), Y, Y + 16 * STREAM[z][1]), A("tab", Y, Y + 16 * STREAM[z][1]), FN.Copy, 0.0)
+    wds = ["wd%s%d" % (z, k) for z in STREAM for k in range(2)]
+    act(A(wds[0], Y, 2 * Y), A("tab", Y, 2 * Y), FN.Copy, 0.0)
+    for k, w in enumerate(wds[1:]):
+        dma("Y", T[w][:, Y:2 * Y], T[wds[0]][:, Y:2 * Y], [A(wds[0], Y, 2 * Y)], [A(w, Y, 2 * Y)], 2500 + 2000 * (k + 1))
+        nodes[-1]["behind"] = [keys]
     ts(A("cf", 3, 4), g16, 16.0, OP.mult)
     ts(A("sth"), A("wi"), A("cf", 3, 4), OP.subtract)
     ts(A("rb"), A("sth", 0, 128, 16), float(4096 * TH + Y), OP.add)
@@ -229,16 +232,26 @@ def build(g, core, T, topo, rank, phys, par=None):
     ms(A("rst1"), 0.0)
     cp(A("rst0", 0, 128, 16), A("rb"))
 
+    ts(A("w3"), A("w2", 0, 128), 0.0, OP.is_ge)
+    ts(A("w4"), A("w2", 0, 128), 16.0, OP.is_lt)
+    tt(A("boh"), A("w3"), A("w4"), OP.mult)
+    if par["LIST"]:
+        ms(A("cut"), 0.0)
+        ms(A("cut", 0, 128, 16), -65536.0)
+
     def constants(t):
         ts(A("dum", 0, 8), A("sth", 0, 128, 16), 1.0 / 16, OP.mult, float(W), OP.add)
         ts(A("dum", 8, 16), A("dum", 0, 8), 128.0, OP.add)
         ts(A("dmc"), A("dum"), -2048.0, OP.add)
-        ms(A("cf", 7, 8), -3.0)
+        cp(A("da", 1, 32, 2), A("dum"))
         act(A("six"), A("ones"), FN.Copy, 1.0 / 16)
-        act(A("bg1"), A("bgb"), FN.Copy, 2.0 ** -16)
-        ts(A("w3"), A("w2", 0, 128), 0.0, OP.is_ge)
-        ts(A("w4"), A("w2", 0, 128), 16.0, OP.is_lt)
-        tt(A("boh"), A("w3"), A("w4"), OP.mult)
+        act(A("nil"), A("ones"), FN.Copy, 0.0)
+        ts(A("w6"), A("w2"), 14.0, OP.is_equal, 1.0 / 16, OP.mult)
+        act(A("bg2"), A("bgb"), FN.Copy, 2.0 ** -16)
+        tt(A("bg2"), A("bg2"), A("w6"), OP.add)
+        iota(A("alt"), [[0, 64], [-1, 2]], 1, 0)
+        for k in range(2):
+            asel(A("own", 1024 * k, 1024 * k + 1024), A("tab", Y, Y + 1024), [[-1, 8], [-16, 8], [0, 16]], OP.is_equal, -8 * k, 1)
         ts(A("w4"), A("w1", 0, 128), pc, OP.is_le)
         tt(A("tle"), A("w3"), A("w4"), OP.mult)
         tt(A("tgt"), A("boh"), A("tle"), OP.subtract)
@@ -248,8 +261,8 @@ def build(g, core, T, topo, rank, phys, par=None):
         ts(A("wl", 8, 16), A("sth", 0, 128, 16), -1.0 / 16, OP.mult, 64.0, OP.add)
         act(A("w5"), A("w5"), FN.Exp, math.log(BASE))
         act(A("wl", 0, 8), A("wl", 8, 16), FN.Exp, math.log(BASE))
-        act(A("whi"), A("w5"), FN.Copy, 3.15)
-        act(A("wlo"), A("w5"), FN.Copy, 1.4)
+        act(A("whi"), A("w5"), FN.Copy, -0.85)
+        act(A("wl", 8, 16), A("wl", 0, 8), FN.Copy, 4.0 / 2048)
         for k in range(8):
             ts(A("wk", 128 * k, 128 * k + 128), A("boh"), A("wl", k, k + 1), OP.mult)
         iota(A("mt"), [[256, 4], [4, 64], [-2, 2]], B + 2, 0)
@@ -285,6 +298,8 @@ def build(g, core, T, topo, rank, phys, par=None):
     ne1 = len(topo.engines(core, nxt))
     ne_in = len(topo.engines(peer(-1), core))
 
+    rows = ["chf", "cho", "chp", "chf", "cho"] if par["COPY"] else ["chf"] * NT + ["cho"]
+
     def step(t, s, z, part):
         base = B + 256 * t
         gs = 3 * t + s
@@ -297,7 +312,7 @@ def build(g, core, T, topo, rank, phys, par=None):
         else:
             lst = A("vl", 16 * (s - 1) + k0, 16 * (s - 1) + k0 + K)
         if part != "rest":
-            cp(A("ku", i0, i0 + H), IND(A("chf", 0, base), lst))
+            cp(A("ku", i0, i0 + H), IND(A(rows[t], 0, base), lst))
         if part == "kids":
             return
         if s == 0 and t > 0:
@@ -369,7 +384,7 @@ def build(g, core, T, topo, rank, phys, par=None):
                 if s < 2:
                     ts(A("kc", i0, i0 + H), A("ku", i0, i0 + H), -2048.0, OP.add)
                 if h == 0 and s > 0:
-                    act(A("rr", 128 * (s - 1) + n0, 128 * (s - 1) + n0 + H), IND(A("chf", 0, base), lst), FN.Copy)
+                    act(A("rr", 128 * (s - 1) + n0, 128 * (s - 1) + n0 + H), IND(A(rows[t], 0, base), lst), FN.Copy)
             while eu[0] < len(eg) and eu[1] + int(eg[eu[0]]) <= u:
                 a, ne = eu[1], int(eg[eu[0]])
                 E = tile()
@@ -397,9 +412,15 @@ def build(g, core, T, topo, rank, phys, par=None):
         if s < 2:
             nm, lo = ("sela", 128 * s + n0) if h == 0 else ("selb", n0)
             tt(A(nm, lo, lo + H), IND(A("tab", 0, top), ou), A("kc", i0, i0 + H), OP.min)
-            Wc = A(tile(), 0, K)
-            mm(acc(Wc, [(A("bgh", 15 - x, 143 - x), A(nm, lo + x, lo + H, 16)) for x in range(16)]))
-            ts(A("vl", 16 * s + k0, 16 * s + k0 + K), Wc, 2.0 ** -12, OP.mult, 32768.0, OP.add)
+            if z in par["LIST"]:
+                Wc = A(tile(), 0, H)
+                mm(acc(Wc, [(A("idb"), A("tab", 0, H)), (A("boh"), A(nm, lo, lo + H))]))
+                scan(A("vs", i0, i0 + H), A("cut", 0, H), Wc, OP.min, OP.max)
+                ts(A("vl", 16 * s + k0, 16 * s + k0 + K), A("vs", i0 + 15, i0 + H, 16), 32768.0 - 4096.0, OP.add)
+            else:
+                Wc = A(tile(), 0, K)
+                mm(acc(Wc, [(A("bgh", 15 - x, 143 - x), A(nm, lo + x, lo + H, 16)) for x in range(16)]))
+                ts(A("vl", 16 * s + k0, 16 * s + k0 + K), Wc, 2.0 ** -12, OP.mult, 32768.0, OP.add)
             act(A(wn, Y, top, 16), IND(A(wd, 0, top), ou), FN.Abs)
         else:
             o = A("ps", L * t + i0, L * t + i0 + H)
@@ -421,7 +442,7 @@ def build(g, core, T, topo, rank, phys, par=None):
         ts(A("uh"), A(X, 0, 256), 30720.0, OP.add)
         for e in range(2):
             ts(A("ab", 8 * e, 8 * e + 8), A("vl", 16 * e, 16 * e + 8), -2048.0, OP.add)
-        tt(A("da"), A("ab"), A("dmc"), OP.subtract)
+        tt(A("da", 0, 32, 2), A("ab"), A("dmc"), OP.subtract)
         tt(A("pre", 0, 8), A("ab", 0, 8), A("ab", 8, 16), OP.not_equal)
         ts(A("pre", 8, 16), A("j15"), 15.0, OP.is_lt, A("rst%d" % (t % 2), 0, 1), OP.mult)
         tt(A("pre", 16, 24), A("pre", 0, 8), A("pre", 8, 16), OP.mult)
@@ -440,47 +461,54 @@ def build(g, core, T, topo, rank, phys, par=None):
 
     def late(t):
         base = B + 256 * t
-        tt(A("pre", 24, 32), A("sc", 15, 128, 16), A("pre", 16, 24), OP.is_lt)
+        tt(A("cand"), A("sc", 15, 128, 16), A("pre", 16, 24), OP.is_lt)
         order = [(0, 0)] + [(k, e) for k in range(1, 8) for e in range(2)] + [(0, 1)]
         at = 0
         F = tile()
         for x, (k, e) in enumerate(order):
             n = 256 - 32 * k
-            ts(A("eqw", at, at + n), A("uh", 32 * k, 256), A("ab", 8 * e + k, 8 * e + k + 1), OP.is_equal, A("pre", 24 + k, 25 + k), OP.mult)
+            ts(A("eqw", at, at + n), A("uh", 32 * k, 256), A("ab", 8 * e + k, 8 * e + k + 1), OP.is_equal, A("cand", k, k + 1), OP.mult)
             mm([(A(F, 16 * k, 128), A("wk", 128 * k, 128 * k + 128), A("eqw", at + f, at + n, 2), x + f == 0, x + f == 16) for f in range(2)])
             at += n
+            if x == 0:
+                tt(A("cw"), A("cand"), A("wl", 8, 16), OP.mult)
+                for u in range(0, 16, 4):
+                    mm([(A(F, m, 128, 16), A("own", 128 * m, 128 * m + 128), A("cw"), False, False) for m in range(u, u + 4)])
         tt(A("hi"), A(F, 0, 128), A("whi"), OP.is_lt)
-        tt(A("lo"), A(F, 0, 128), A("wlo"), OP.is_gt)
+        scan(A("st"), A("alt"), A("hi"), OP.max, OP.min)
         X = tile()
         mm([(A(X, 128 * k, 128 * k + 128), A(nm), A("oh", 128, 256), True, True) for k, nm in enumerate(("tle", "tgt"))])
         tt(A("t1", 128, 256), A(X, 0, 128), A("rr", 128, 256), OP.mult)
         tt(A("t4", 128, 256), A(X, 128, 256), A("rr", 128, 256), OP.mult)
-        X = tile()
-        mm([m for e in range(2) for m in acc(A(X, e, 128, 2), [(A("idb"), A(nm, f, 128, 2)) for nm in ("hi", "lo") for f in range(2)])])
-        act(A("fl"), A(X, 0, 128), FN.Relu, acc=A("zc", 0, 1) if t < NT - 1 else None, bias=A("cf", 7, 8))
         F, X = tile(), tile()
-        mm(acc(A(F, 0, 8), [(A("bg1", 15 - x, 143 - x), A("fl", x, 128, 16)) for x in range(16)]))
-        mm([(A(X, 0, 128), A("idb"), A("fl"), True, True)] + ([(A(X, 128, 129), A("six"), A("zc", 0, 1), True, True)] if t < NT - 1 else []))
+        mm([(A(F, 0, 16), A("nil"), A("ones", 0, 16), True, False)]
+           + [(A(F, 1, 16, 2), A("bg2", 14 - x, 142 - x), A("st", x + 1, 128, 16), False, x == 14) for x in range(0, 16, 2)])
+        mm([(A(X, e, 128, 2), A("idb"), A("st", 1, 128, 2), True, True) for e in range(2)])
         for e in range(2):
-            tt(A("of", 8 * e, 8 * e + 8), A(F, 0, 8), A("da", 8 * e, 8 * e + 8), OP.mult)
-        tt(A("og2"), A("of"), A("dum"), OP.add)
-        cp(A("so"), A("og2"))
-        tb = "chf" if t < NT - 1 else "cho"
+            scan(A("og2", 16 * e, 16 * e + 16), A(F, 0, 16), A("da", 16 * e, 16 * e + 16), OP.mult, OP.add)
+        cp(A("so"), A("og2", 1, 32, 2))
+        tb = rows[t + 1]
         for e in range(2):
             tt(A(tb, base + e, base + 256, 2), A(X, 0, 128), A("t4", 128 * e, 128 * e + 128), OP.mult)
         cp(IND(A(tb), A("so")), A("t1"))
         if t < NT - 1:
-            cp(A("zi", 0, 1), A(X, 128, 129))
+            act(A("fl", 0, 64), A("st", 1, 128, 2), FN.Copy, 2.0, acc=A("zc", 0, 1))
+            X = tile()
+            mm([(A(X, 0, 1), A("six"), A("zc", 0, 1), True, True)])
+            cp(A("zi", 0, 1), A(X, 0, 1))
             ts(A("zk", 0, 1), A("zi", 0, 1), 63, OP.bitwise_and)
             ts(A("za", 0, 1), A("zk", 0, 1), 4096.0, OP.mult)
             ts(A("rst%d" % ((t + 1) % 2), 0, 128, 16), A("rb"), A("za", 0, 1), OP.add)
         else:
-            dma("Y", T.yc[:], T.cho[:, 0:W], [A("cho", 0, W)], [], 9000)
+            dma("Y", T.yc[:], T[tb][:, 0:W], [A(tb, 0, W)], [], 9000)
 
     def copy_rows(t):
         top = B + 256 * t
-        dma("Y", T.cho[:, 0:top], T.chf[:, 0:top], [A("chf", 0, top)], [A("cho", 0, top)], 9000)
-        cp(A("cho", 0, 1), A("ch0", 0, 1))
+        a, b = rows[t], rows[t + 1]
+        landed = [A("pl", L * (t - 1), L * t)] if t > 0 and par["COPY"] else []
+        dma("Y", T[b][:, 0:top], T[a][:, 0:top], [A(a, 0, top)] + landed, [A(b, 0, top)], 9000)
+        if t == NT - 1:
+            cp(A(b, 0, 1), A("ch0", 0, 1))
 
     for t in range(NT):
         for w in ORDER[t].split():
@@ -511,6 +539,8 @@ def depend(nodes):
                         dd[j] = True
         for j in d.get("after", []):
             dd[j] = False
+        for j in d.get("behind", []):
+            dd[j] = True
         for regs, w in ((d["rd"], False), (d["wr"], True)):
             for nm, lo, hi in sorted(set(regs)):
                 h = hist.setdefault(nm, [])
@@ -628,21 +658,45 @@ def banks(nodes, base, start):
 def polish(nodes, deps, start, end, par):
     n = len(nodes)
     lat = [d.get("lat", 0) for d in nodes]
-    before = [[(j, lat[j] + (par["LAT"] if w else 0)) for j, w in deps[i].items()] for i in range(n)]
+    cost = [d["cost"] for d in nodes]
+    eng = [d["eng"] for d in nodes]
+    before = [[(j, cost[j] + lat[j] + (par["LAT"] if w else 0)) for j, w in deps[i].items()] for i in range(n)]
     seq = sorted(range(n), key=lambda i: (start[i], i))
-    rng = numpy.random.default_rng(1)
+    rng = numpy.random.default_rng(par["SEED"])
     for _ in range(par["SHAKES"]):
         a = rng.random() * end
-        noise = rng.normal(0.0, par["SHAKE"], n)
-        key = [start[i] + (float(noise[i]) if a < start[i] < a + 8000 else 0.0) for i in range(n)]
-        for i in seq:
-            for j in deps[i]:
-                if key[j] >= key[i]:
-                    key[i] = key[j] + 0.01
-        s1, e1 = place(nodes, sorted(range(n), key=lambda i: (key[i], i)), before, lat)
+        p0, p1 = [int(x) for x in numpy.searchsorted([start[i] for i in seq], [a, a + par["STRETCH"]])]
+        key = dict(zip(seq[p0:p1], [float(x) for x in rng.normal(0.0, par["SHAKE"], p1 - p0)]))
+        for i in seq[p0:p1]:
+            key[i] = max([key[i] + start[i]] + [key[j] + 0.01 for j, _x in before[i] if j in key])
+        s1, e1 = start[:], 0.0
+        on, off = {e: [] for e in "VSPGYR"}, {e: [] for e in "VSPGYR"}
+        for i in seq[:p0]:
+            on[eng[i]].append(start[i])
+            off[eng[i]].append(start[i] + cost[i])
+            e1 = max(e1, start[i] + cost[i] + lat[i])
+        for i in sorted(seq[p0:p1], key=key.get) + seq[p1:]:
+            c, t0 = cost[i], 0.0
+            for j, x in before[i]:
+                if s1[j] + x > t0:
+                    t0 = s1[j] + x
+            b, e = on[eng[i]], off[eng[i]]
+            k = len(b)
+            while k > 0 and e[k - 1] > t0:
+                k -= 1
+            while k < len(b) and b[k] < t0 + c:
+                if e[k] > t0:
+                    t0 = e[k]
+                k += 1
+            b.insert(k, t0)
+            e.insert(k, t0 + c)
+            s1[i] = t0
+            if t0 + c + lat[i] > e1:
+                e1 = t0 + c + lat[i]
         if e1 <= end:
             start, end = s1, e1
-    return start
+            seq = sorted(range(n), key=lambda i: (start[i], i))
+    return start, end
 
 
 def plan(nodes, par=None):
@@ -654,10 +708,10 @@ def plan(nodes, par=None):
     for _ in range(par["PASSES"]):
         deps, phys = banks(nodes, base, start)
         start, end = pack(nodes, deps, start, par)
+        start, end = polish(nodes, deps, start, end, par)
         if best is None or end < best[0]:
             best = (end, start, deps, phys)
     end, start, deps, phys = best
-    start = polish(nodes, deps, start, end, par)
     order = {e: sorted((i for i in range(n) if nodes[i]["eng"] == e), key=lambda i: (start[i], i)) for e in "VSPGYR"}
     return deps, order, [start[i] + nodes[i]["cost"] + nodes[i].get("lat", 0) for i in range(n)], phys
 

@@ -1,4 +1,3 @@
-import math
 import numpy
 from concourse.bass import DstId, RemoteDMATransfer
 from concourse.mybir import AluOpType, ActivationFunctionType
@@ -7,47 +6,57 @@ N, B, L, NT, TH = 4, 2560, 256, 4, 1240
 W = B + 256 * NT
 WD = W + 256
 KNONE = 640.0
-BASE = 3.5
 Y = 2048
 NLOAD = 4
+MEET, BIG = 16384.0, 262144.0
+BLK = [8 * m * (m + 1) + 3 * m for m in range(9)]
 STREAM = {"A": (0, 128), "B": (128, 128)}
 CUT = {}
-for _s in ("first", 0, 1, 2):
-    CUT[_s, "A"] = "Z1 Y1 Z1 Y1|1 1 1 1|2 2" if _s == "first" else "S1 X1 X1 R1|1 1 1 1|2 2"
-    CUT[_s, "B"] = "Z1 Y1 Z1 Y1|1 1 1 1|2 2" if _s == "first" else "S1 X1 X1 X1|1 1 1 1|2 2"
+for _z in STREAM:
+    CUT["first", _z] = "Z1 Y1 Z1 Y1|1 1 1 1|2 2"
+    CUT[0, _z] = "T1 S1 R1 X1|2 1 1|2 2" if _z == "A" else "N1 S1 R1 N1|2 1 1|2 2"
+    CUT[1, _z] = "X1 X1 R1 M1g|2 1 1|2 2"
+    CUT[2, _z] = "X1 X1 X1 M1g|2 1 1|2 2"
 ORDER = ["A0 c B0 A1 B1 e A2 B2k l B2r"] + ["A0 B0 A1 B1 e A2 B2k l B2r"] * 2 + ["o A0 B0 A1 e B1 A2 l B2"]
-PAR = {"GF": 1.56, "SC": 3.5, "PEF": 0.5, "PMM": 8, "VO": 60, "SO": 75, "LAT": 220, "BETA": 1000, "ROUNDS": 4, "PASSES": 3, "SPLIT": 1, "SPR": 1, "PFIRST": 0, "TURN": "V", "COPY": 0, "LIST": "AB", "SHAKES": 5000, "SHAKE": 500.0, "STRETCH": 3000, "SEED": 2}
+PAR = {"GF": 1.56, "SC": 3.5, "PEF": 0.57, "PMM": 8, "VO": 60, "SO": 75, "GO": 205, "LAT": 220, "CUT": CUT, "ORDER": ORDER,
+       "TURN": "S", "LIST": "AB", "OH": "V", "UH": "S", "KC": "B0", "FAT": 1, "KEPT": 0, "SPR": 1, "TABS": 256, "QFROM": 1, "OJ": 1, "CONV": "GGGG", "Q0": "", "RL": 1.0, "DL": 0.65,
+       "ROUNDS": 4, "PASSES": 7, "SEED": 2, "WINDOW": 70, "SWEEPS": 3, "MOVES": 1000, "STALE": 300, "NOISE": 400}
 PLAN = []
 
 f32, bf, f16, i32, u16 = "float32", "bfloat16", "float16", "int32", "uint16"
 SCRATCH = {}
 for _n, _c, _d in [
-    ("chi", B, i32), ("chf", WD, f32), ("cho", WD, f32), ("chp", WD, f32), ("key", W, bf), ("ch0", 4, f32), ("qraw", L, bf), ("hvi", 64, i32), ("hvu", 64, u16),
+    ("chi", B, i32), ("chf", WD, f32), ("cho", WD, f32), ("key", W, bf), ("ch0", 4, f32), ("qraw", L, bf), ("hvi", 64, i32), ("hvu", 64, u16),
     ("qT0", L, bf), ("qT1", L, bf), ("qT2", L, bf), ("qT3", L, bf), ("hl1", 16, u16), ("hl2", 16, u16), ("hl3", 16, u16),
-    ("tab", 2 * Y, bf), ("eq", Y, bf), ("ramp", Y, bf), ("pe0", Y, bf), ("pe1", Y, bf),
+    ("tab", 2 * Y, bf), ("ramp", 1536, bf), ("pe0", Y, bf), ("pe1", Y, bf), ("kf0", Y, f16), ("kf1", Y, f16), ("df0", Y, f16), ("df1", Y, f16),
     ("rl0", Y, bf), ("rl1", Y, bf), ("kr0", Y, bf), ("kr1", Y, bf),
     ("ku", 256, u16), ("kc", 256, f16), ("vl", 32, u16),
     ("sc", 256, i32), ("oj", 16, i32), ("ou", 16, u16), ("vs", 256, f32), ("cut", 128, f32), ("sela", 256, f16), ("selb", 128, f16), ("rst0", 128, f32), ("rst1", 128, f32),
     ("ps", 1024, bf), ("pl", 1024, bf), ("pT0", 128, bf), ("pT1", 128, bf),
-    ("ones", 128, bf), ("idb", 128, bf), ("nid", 128, bf), ("two", 128, bf), ("idh", 128, f16), ("six", 128, f32),
-    ("bgb", 144, bf), ("bgh", 144, f16), ("bg2", 144, bf), ("boh", 128, f16), ("wk", 1024, bf),
-    ("tle", 128, bf), ("tgt", 128, bf), ("tsh", 128, bf), ("sth", 128, f16),
-    ("ci", 8, i32), ("cf", 12, f32), ("w1", 144, f32), ("w2", 144, f32), ("w3", 128, f32), ("w4", 128, f32), ("w5", 128, f32), ("w6", 144, bf), ("wi", 128, i32),
-    ("whi", 128, f32), ("wl", 16, f32), ("mt", 512, f32), ("ni", 512, f32), ("dum", 16, f32), ("dmc", 16, f32), ("rb", 8, f32),
-    ("uh", 256, f16), ("eqw", 2304, bf), ("oh", 256, bf), ("rr", 256, f32), ("t1", 256, f32), ("t4", 256, f32),
-    ("pre", 24, f32), ("cand", 8, f32), ("cw", 8, bf), ("j15", 8, i32), ("hi", 128, bf), ("st", 128, bf), ("alt", 128, bf), ("nil", 128, bf),
-    ("own", Y, bf), ("fl", 64, bf), ("ab", 16, f32), ("da", 32, f32), ("og2", 32, f32), ("so", 16, u16),
+    ("ones", 128, bf), ("idb", 128, bf), ("nid", 128, bf), ("two", 128, bf), ("idh", 128, f16),
+    ("bgb", 144, bf), ("bgh", 144, f16), ("boh", 128, f16),
+    ("nle", 128, bf), ("ngt", 128, bf), ("nlt", 128, bf), ("shh", 128, f16), ("nsh", 128, bf), ("ns4", 128, bf), ("nih", 128, f16), ("sth", 128, f16),
+    ("ci", 8, i32), ("cf", 12, f32), ("w1", 144, f32), ("w2", 144, f32), ("w3", 128, f32), ("w4", 128, f32), ("w5", 128, f32), ("wi", 128, i32),
+    ("nh", 512, f16), ("ni", 512, f32), ("dum", 16, f32), ("rb", 8, f32),
+    ("uh", 256, f16), ("eqw", 4 * BLK[8], bf), ("oh", 256, bf), ("ka", 256, f16), ("ohn", 128, f16), ("t1", 256, f32),
+    ("pre", 24, f32), ("cand", 8, bf), ("cw", 16, bf), ("j15", 8, i32),
+    ("prs", 128, bf), ("prn", 128, bf), ("bup", 128, bf), ("la", 128, f16), ("lb", 128, f16), ("npre", 128, f16),
+    ("mas", 132, bf), ("lid", BLK[8] + 1, f32), ("fix", BLK[8], bf), ("bs", BLK[8], f32), ("end", 2, u16),
+    ("eq", Y, bf), ("nbo", 128, f16), ("cwx", 128, f16), ("rep", 8, u16), ("fl", 8, f32), ("ab", 16, f32), ("og2", 16, f32), ("so", 16, u16),
     ("zc", 4, f32), ("zi", 4, i32), ("zk", 4, i32), ("za", 4, f32),
 ]:
     SCRATCH[_n] = ("sbuf", [128, _c], _d)
 SCRATCH["fa"] = ("sbuf", [128, 16, 16, 16], bf)
-for _n in "AaB":
-    SCRATCH["wd%s0" % _n] = ("sbuf", [128, 2 * Y], bf)
-    SCRATCH["wd%s1" % _n] = ("sbuf", [128, 2 * Y], bf)
+for _n in range(2):
+    SCRATCH["p4%d" % _n] = ("sbuf", [128, 512], bf)
+    for _k, _c in (("q1", 128), ("q4", 512), ("qe", Y), ("ef", Y)):
+        SCRATCH["%s%d" % (_k, _n)] = ("sbuf", [128, _c], f16)
+    SCRATCH["wdA%d" % _n] = ("sbuf", [128, 2 * Y], bf)
+    SCRATCH["wdB%d" % _n] = ("sbuf", [128, 2 * Y], bf)
 for _n in range(4):
     SCRATCH["pm%d" % _n] = ("psum", [128, 1024], f32)
 SEMAPHORES = (["sV", "sS", "sP", "sG", "ls"] + ["d%d" % k for k in range(24)] + ["aq%d" % t for t in range(1, 4)]
-              + ["ap%d" % k for k in range(4 * NT)])
+              + ["ap%d" % k for k in range(2 * NT)])
 OP = AluOpType
 FN = ActivationFunctionType
 
@@ -77,9 +86,9 @@ def build(g, core, T, topo, rank, phys, par=None):
 
     tiles = [0]
 
-    def tile():
+    def tile(kind=""):
         tiles[0] += 1
-        return "#%d" % tiles[0]
+        return "#%s%d" % (kind, tiles[0])
 
     def IND(win, off):
         return (win[0].indirect(off[0]), win[1] + off[1], 16 * off[2], win[3], 1)
@@ -88,9 +97,15 @@ def build(g, core, T, topo, rank, phys, par=None):
         ap = T.fa[:, a:b, :, :] if ilo is None else T.fa[:, a:b, ilo, :]
         return (ap, [("fa", 256 * a, 256 * b)], (b - a) * (256 if ilo is None else 16), bf, 0)
 
+    def LANE(name, lo, hi, c=None):
+        x = A(name, lo, hi) if c is None else A(name, lo + c, hi, 4)
+        return (x[0], [("%s~%d" % (name, k), lo, hi) for k in (range(4) if c is None else [c])]) + x[2:]
+
     def node(eng, emit, rd, wr, cost, **kw):
         d = {"eng": eng, "emit": emit, "rd": [r for x in rd for r in x[1]], "wr": [r for x in wr for r in x[1]], "cost": cost}
         d.update(kw)
+        if eng == "R" or "remote" in d:
+            d["cost"], d["lat"] = cost * par["RL"], d.get("lat", 0) * par["RL"]
         nodes.append(d)
         return len(nodes) - 1
 
@@ -130,8 +145,8 @@ def build(g, core, T, topo, rank, phys, par=None):
     def ms(o, c):
         node("V", lambda: V.memset(o[0], c), [], [o], VO + o[2] * (.5 if two_b(o) else 1))
 
-    def scan(o, d0, d1, op0, op1):
-        node("V", lambda: V.tensor_tensor_scan(o[0], d0[0], d1[0], 0.0, op0, op1), [d0, d1], [o],
+    def scan(o, d0, d1, op0, op1, first=0.0):
+        node("V", lambda: V.tensor_tensor_scan(o[0], d0[0], d1[0], first, op0, op1), [d0, d1], [o],
              VO + o[2] * (.5 if two_b(o, d0, d1) else 1))
 
     def act(o, i, fn, scale=1.0, acc=None, bias=None):
@@ -161,8 +176,11 @@ def build(g, core, T, topo, rank, phys, par=None):
             em = lambda: g.iota(o[0], pat, base, cm, allow_small_or_imprecise_dtypes=True)
         node("G", em, [], [o], 160 + 2 * o[2])
 
-    def asel(o, i, pat, op, base, cm):
-        node("G", lambda: g.affine_select(o[0], i[0], pat, op, 0.0, base, cm), [i], [o], 200 + 2 * o[2])
+    def asel(o, i, pat, op, base, cm, fill=0.0):
+        node("G", lambda: g.affine_select(o[0], i[0], pat, op, fill, base, cm), [i], [o], par["GO"] + 2 * o[2])
+
+    def gcopy(o, i):
+        asel(o, i, [[0, o[2]]], OP.is_ge, 0, 0)
 
     ndma = [0]
 
@@ -170,7 +188,7 @@ def build(g, core, T, topo, rank, phys, par=None):
         sem = T.sem["d%d" % ndma[0]]
         ndma[0] += 1
         e = g.sync if q == "Y" else g.scalar
-        node(q, lambda: e.dma_start(o, i).then_inc(sem, 16), rd, wr, 60, sem=sem, cnt=16, lat=lat)
+        node(q, lambda: e.dma_start(o, i).then_inc(sem, 16), rd, wr, 60, sem=sem, cnt=16, lat=lat * par["DL"])
 
     sent = [0]
 
@@ -184,6 +202,8 @@ def build(g, core, T, topo, rank, phys, par=None):
         dma("Y", T.chi[:, k * cw:(k + 1) * cw], T.ch[:, k * cw:(k + 1) * cw], [], [A("chi", k * cw, (k + 1) * cw)], 2500 + 1100 * (k + 1))
     dma("Y", T.key[:, 0:B], T.kb[:], [], [A("key", 0, B)], 9000)
     keys = len(nodes) - 1
+    for d in nodes:
+        d["load"] = True
     ms(A("ones"), 1.0)
     ms(A("tab", Y, 2 * Y), -2048.0)
     iota(A("ci", 0, 1), [[0, 1]], 0, 1)
@@ -192,13 +212,18 @@ def build(g, core, T, topo, rank, phys, par=None):
     iota(A("wi"), [[256, 8], [1, 16]], 0, 16)
     for k in range(2):
         asel(A("eq", 1024 * k, 1024 * k + 1024), A("tab", Y, Y + 1024), [[1, 64], [0, 16]], OP.is_equal, 64 * k, -1)
-    iota(A("ramp"), [[0, 128], [256, 16]], 0, 0)
+    iota(A("ramp", 0, 512 * par["SPR"]), [[0, 32 * par["SPR"]], [256, 16]], 0, 0)
     cp(A("hvu"), A("hvi"))
+    cp(A("ch0", 0, 1), A("chi", 0, 1))
+    ms(A("chi", 0, 1), 0)
     for k in range(NLOAD):
-        cp(A("chf", k * cw, (k + 1) * cw), A("chi", k * cw, (k + 1) * cw))
-        if k == 0:
-            cp(A("ch0", 0, 1), A("chi", 0, 1))
-            ms(A("chf", 0, 1), 0.0)
+        o, i = A("chf", k * cw, (k + 1) * cw), A("chi", k * cw, (k + 1) * cw)
+        if par["CONV"][k] == "S":
+            act(o, i, FN.Copy)
+        else:
+            {"V": cp, "G": gcopy}[par["CONV"][k]](o, i)
+        if par["CONV"][k] != "V":
+            nodes[-1]["behind"] = [keys]
     ms(A("key", 0, 1), KNONE)
 
     ts(A("ci", 1, 2), A("ci", 0, 1), 15, OP.bitwise_and)
@@ -207,17 +232,23 @@ def build(g, core, T, topo, rank, phys, par=None):
     pc, rowc, g16 = A("cf", 0, 1), A("cf", 1, 2), A("cf", 2, 3)
     ts(A("w2"), A("w1"), g16, OP.subtract)
     ts(A("bgb"), A("w2"), 15.0, OP.is_equal, 4096.0, OP.mult)
-    cp(A("bgh"), A("bgb"))
+    if par["LIST"] != "AB":
+        cp(A("bgh"), A("bgb"))
     ts(A("w3", 0, 16), A("w1", 0, 16), rowc, OP.is_equal, 6144.0, OP.mult)
     ts(A("tab", 0, 16), A("w3", 0, 16), -2048.0, OP.add)
     n = 16
     while n < Y:
-        cp(A("tab", n, 2 * n), A("tab", 0, n))
+        if n < par["TABS"]:
+            cp(A("tab", n, 2 * n), A("tab", 0, n))
+        else:
+            act(A("tab", n, 2 * n), A("tab", 0, n), FN.Copy)
         n *= 2
     cp(A("idh"), A("idb"))
     X = tile()
     mm([(A(X, 128 * h, 128 * h + 128), A("qraw", 128 * h, 128 * h + 128), A("idb"), True, True) for h in range(2)])
     act(A("qT0"), A(X, 0, 256), FN.Copy, 1.0 / 2048)
+    for k in range(par["KEPT"]):
+        mm([(A("#f%d" % k, 0, 512), A("idb"), A("tab", Y, Y + 512), True, False)])
     act(A("nid"), A("idb"), FN.Copy, -1.0)
     act(A("two"), A("idb"), FN.Copy, 2.0)
     wds = ["wd%s%d" % (z, k) for z in STREAM for k in range(2)]
@@ -235,38 +266,58 @@ def build(g, core, T, topo, rank, phys, par=None):
     ts(A("w3"), A("w2", 0, 128), 0.0, OP.is_ge)
     ts(A("w4"), A("w2", 0, 128), 16.0, OP.is_lt)
     tt(A("boh"), A("w3"), A("w4"), OP.mult)
-    if par["LIST"]:
-        ms(A("cut"), 0.0)
-        ms(A("cut", 0, 128, 16), -65536.0)
+    ms(A("cf", 8, 9), 256.0)
+    ms(A("cf", 9, 10), -2048.0)
+    ms(A("cf", 10, 11), 768.0)
+    ms(A("cut"), 0.0)
+    ms(A("cut", 0, 128, 16), -65536.0)
 
     def constants(t):
-        ts(A("dum", 0, 8), A("sth", 0, 128, 16), 1.0 / 16, OP.mult, float(W), OP.add)
-        ts(A("dum", 8, 16), A("dum", 0, 8), 128.0, OP.add)
-        ts(A("dmc"), A("dum"), -2048.0, OP.add)
-        cp(A("da", 1, 32, 2), A("dum"))
-        act(A("six"), A("ones"), FN.Copy, 1.0 / 16)
-        act(A("nil"), A("ones"), FN.Copy, 0.0)
-        ts(A("w6"), A("w2"), 14.0, OP.is_equal, 1.0 / 16, OP.mult)
-        act(A("bg2"), A("bgb"), FN.Copy, 2.0 ** -16)
-        tt(A("bg2"), A("bg2"), A("w6"), OP.add)
-        iota(A("alt"), [[0, 64], [-1, 2]], 1, 0)
-        for k in range(2):
-            asel(A("own", 1024 * k, 1024 * k + 1024), A("tab", Y, Y + 1024), [[-1, 8], [-16, 8], [0, 16]], OP.is_equal, -8 * k, 1)
-        ts(A("w4"), A("w1", 0, 128), pc, OP.is_le)
-        tt(A("tle"), A("w3"), A("w4"), OP.mult)
-        tt(A("tgt"), A("boh"), A("tle"), OP.subtract)
-        ts(A("w4"), A("w1", 0, 128), -1.0, OP.add, pc, OP.is_equal)
-        tt(A("tsh"), A("boh"), A("w4"), OP.mult)
-        iota(A("w5"), [[-1, 128]], 64, 0)
-        ts(A("wl", 8, 16), A("sth", 0, 128, 16), -1.0 / 16, OP.mult, 64.0, OP.add)
-        act(A("w5"), A("w5"), FN.Exp, math.log(BASE))
-        act(A("wl", 0, 8), A("wl", 8, 16), FN.Exp, math.log(BASE))
-        act(A("whi"), A("w5"), FN.Copy, -0.85)
-        act(A("wl", 8, 16), A("wl", 0, 8), FN.Copy, 4.0 / 2048)
-        for k in range(8):
-            ts(A("wk", 128 * k, 128 * k + 128), A("boh"), A("wl", k, k + 1), OP.mult)
-        iota(A("mt"), [[256, 4], [4, 64], [-2, 2]], B + 2, 0)
-        iota(A("ni"), [[256, 4], [2, 128]], B + 1, 0)
+        act(A("nbo"), A("boh"), FN.Copy, -1.0)
+        cp(A("rep"), A("w1", 0, 8))
+        ms(A("dum", 11, 12), 2048.0 - 15 * 2048)
+        ms(A("dum", 12, 13), 128.0)
+        act(A("ngt"), A("boh"), FN.Copy, -8192.0)
+        asel(A("nle"), A("ngt"), [[-1, 128]], OP.is_ge, 0, 1)
+        asel(A("ngt"), A("ngt"), [[1, 128]], OP.is_gt, 0, -1)
+        asel(A("nlt"), A("nle"), [[-1, 128]], OP.not_equal, 0, 1, -1.0)
+        asel(A("shh"), A("boh"), [[1, 128]], OP.is_equal, -1, -1)
+        act(A("nsh"), A("shh"), FN.Copy, -1.0)
+        act(A("ns4"), A("shh"), FN.Copy, -4.0)
+        act(A("nih"), A("idb"), FN.Copy, -1.0)
+        iota(A("ni"), [[256, 4], [2, 128]], B + 1 - 2047, 0)
+        act(A("nh"), A("ni"), FN.Copy)
+        ts(A("ci", 4, 5), A("ci", 0, 1), 14, OP.bitwise_and)
+        ts(A("ci", 5, 6), A("ci", 0, 1), 7, OP.bitwise_and)
+        cp(A("cf", 5, 7), A("ci", 4, 6))
+        act(A("bup"), A("boh"), FN.Copy, BIG)
+        asel(A("prn"), A("bup"), [[-2, 64], [0, 2]], OP.is_ge, 0, 1)
+        asel(A("prn"), A("prn"), [[2, 64], [0, 2]], OP.is_ge, 1, -1)
+        act(A("prs"), A("prn"), FN.Copy, MEET / BIG)
+        for a in (0, 2 * BLK[8]):
+            dma("Y", T.eqw[:, a:a + 2 * BLK[8]], T[wds[0]][:, Y:Y + 2 * BLK[8]], [A(wds[0], Y, 2 * Y)], [A("eqw", a, a + 2 * BLK[8])], 9000)
+            nodes[-1]["behind"] = [keys]
+        ts(A("cf", 7, 8), A("cf", 5, 6), 111.0, OP.add)
+        ts(A("w5"), A("w1", 0, 128), A("cf", 7, 8), OP.subtract, 0.0, OP.max)
+        ts(A("mas", 0, 128), A("w5"), -2 * MEET, OP.mult, -BIG - MEET / 2, OP.add)
+        ms(A("mas", 128, 129), -0.5 * BIG)
+        ms(A("mas", 129, 131), -4 * BIG)
+        iota(A("lid"), [[0, BLK[8] + 1]], int(16 * BIG), 0)
+        ts(A("dum", 0, 1), rowc, float(W + 128 - 2048), OP.add)
+        ts(A("dum", 1, 2), rowc, float(W - 2048), OP.add)
+        ms(A("dum", 2, 3), -16 * BIG)
+        for m in range(8):
+            gcopy(A("fix", BLK[m], BLK[m + 1]), A("mas", 112 - 16 * m, 131))
+            ts(A("lid", BLK[m + 1] - 2, BLK[m + 1] + 1), A("dum", 0, 3), 16.0 * m, OP.add)
+        ts(A("dum", 4, 5), A("cf", 6, 7), 8.0, OP.mult, 27.0, OP.add)
+        ts(A("dum", 5, 6), rowc, 8.0, OP.is_ge, 17.0, OP.add)
+        ts(A("end", 0, 1), A("dum", 4, 5), A("cf", 6, 7), OP.mult, A("dum", 5, 6), OP.add)
+        asel(A("la"), A("boh"), [[0, 8], [-1, 16]], OP.not_equal, 15, 0)
+        act(A("lb"), A("boh"), FN.Copy, -1.0)
+        act(A("lb", 15, 128, 16), A("ngt", 15, 128, 16), FN.Copy, -1.0 / 8192)
+        ts(A("dum", 7, 8), rowc, 15.0, OP.is_equal, -15.0 * 2048, OP.mult)
+        ms(A("dum", 8, 9), 30720.0)
+        ms(A("dum", 10, 11), 2048.0)
 
     def masks():
         used, out = [], {}
@@ -298,30 +349,62 @@ def build(g, core, T, topo, rank, phys, par=None):
     ne1 = len(topo.engines(core, nxt))
     ne_in = len(topo.engines(peer(-1), core))
 
-    rows = ["chf", "cho", "chp", "chf", "cho"] if par["COPY"] else ["chf"] * NT + ["cho"]
+    rows = ["chf"] * NT + ["cho"]
+    seen = {}
+    up = A("dum", 10, 11)
 
     def step(t, s, z, part):
         base = B + 256 * t
         gs = 3 * t + s
         wd, wn = "wd%s%d" % (z, gs % 2), "wd%s%d" % (z, (gs + 1) % 2)
         i0, H = STREAM[z]
-        h, n0, k0, K = i0 // 128, i0 % 128, i0 // 16, H // 16
+        h, k0, K = i0 // 128, i0 // 16, H // 16
         top = Y + 16 * H
         if s == 0:
             lst = A("hvu" if t == 0 else "hl%d" % t, k0, k0 + K)
         else:
-            lst = A("vl", 16 * (s - 1) + k0, 16 * (s - 1) + k0 + K)
+            lst = A("vl", 8 * (s - 1) + 2 * k0, 8 * (s - 1) + 2 * k0 + K)
+        kids = IND(A(rows[t] if t else "chi", 0, base if s else B), lst)
         if part != "rest":
-            cp(A("ku", i0, i0 + H), IND(A(rows[t], 0, base), lst))
+            cp(A("ku", i0, i0 + H), kids)
         if part == "kids":
             return
+        gat, eg, sg = [x.split() for x in par["CUT"]["first" if gs == 0 else s, z].split("|")]
+
+        def pnow(a, b):
+            if s == 0:
+                return A("pl", L * (t - 1) + i0 + a, L * (t - 1) + i0 + b)
+            return A(wd, Y + 16 * a, Y + 16 * b, 16)
         if s == 0 and t > 0:
-            act(A(wd, Y, top, 16), A("pl", L * (t - 1) + i0, L * (t - 1) + i0 + H), FN.Copy)
-        gat, eg, sg = [x.split() for x in CUT["first" if gs == 0 else s, z].split("|")]
+            act(A(wd, Y, top, 16), pnow(0, H), FN.Copy)
+        us = [k for x in ((0, 1, 2) if t else ("first",)) for k, c in enumerate(
+            c for y in par["CUT"][x, z].split("|")[0].split() for c in ("q" if "q" in y else ".") * int(y[1])) if c == "q"]
+        if s == 0 and us:
+            a, b = 32 * min(us), 32 * max(us) + 32
+            if t:
+                X = tile()
+                mm([(A(X, 0, b - a), A("qT%d" % t, 128 * h, 128 * h + 128), A("idb", a, b), True, True)])
+                act(A("q1%d" % h, a, b), A(X, 0, b - a), FN.Identity, 2048.0, bias=A("cf", 10, 11))
+            for c in range(4):
+                if t:
+                    gcopy(LANE("q4%d" % h, 4 * a, 4 * b, c), A("q1%d" % h, a, b))
+                else:
+                    act(LANE("q4%d" % h, 4 * a, 4 * b, c), A("qraw", i0 + a, i0 + b), FN.Identity, bias=A("cf", 10, 11))
+            for c in range(4):
+                (gcopy if t or par["Q0"] == "G" else cp)(LANE("qe%d" % h, 16 * a, 16 * b, c), LANE("q4%d" % h, 4 * a, 4 * b))
+        kinds = "".join((x[2:].replace("q", "") or ".") * int(x[1]) for x in gat)
+        for ch in sorted(set(kinds) - set(".")):
+            a, b = 32 * kinds.index(ch), 32 * (kinds.rindex(ch) + 1)
+            if ch in "hi":
+                scan(LANE("p4%d" % h, 4 * a, 4 * b), A("ramp", 0, 16 * (b - a), 4), A(wd, Y + 16 * a, Y + 16 * b, 4), OP.min, OP.add)
+            for c in range(0 if ch in "hi" else 4):
+                gcopy(LANE("p4%d" % h, 4 * a, 4 * b, c), pnow(a, b))
+            for c in range(4):
+                gcopy(LANE("pe%d" % h, 16 * a, 16 * b, c), LANE("p4%d" % h, 4 * a, 4 * b))
         keyw = A("key", 0, base)
+        kc = A("ka", 128 * s - 128, 128 * s) if h == 0 and s else A("kc", i0, i0 + H)
         qt = A("qT%d" % t, 128 * h, 128 * h + 128)
-        kr, rl, pe = ["%s%d" % (x, h) for x in ("kr", "rl", "pe")]
-        c0 = 16 * n0
+        kr, rl = ["%s%d" % (x, h) for x in ("kr", "rl")]
         Wb = tile()
         terms, got = {}, {}
         eu, su = [0, 0], [0, 0]
@@ -341,63 +424,76 @@ def build(g, core, T, topo, rank, phys, par=None):
             elif ty in "ST":
                 D = tile()
                 if ty == "S":
-                    act(A(kr, c0 + lo, c0 + hi), src, FN.Copy)
+                    act(A(kr, lo, hi), src, FN.Copy)
                 else:
-                    cp(A(kr, c0 + lo, c0 + hi), src)
-                for k in range(0, hi - lo, 512):
-                    pz = A(wd, Y + lo + k, Y + lo + k + 512, 16)
-                    if par["TURN"]:
-                        if not turned:
-                            X = tile()
-                            mm([(A(X, 0, 128), A(wd, Y, top, 16), A("idb"), True, True)])
-                            if par["TURN"] == "S":
-                                act(A("pT%d" % h), A(X, 0, 128), FN.Copy, 1.0 / 2048)
-                            else:
-                                ts(A("pT%d" % h), A(X, 0, 128), 1.0 / 2048, OP.mult)
-                            turned = True
-                        mm([(A(D, k, k + 512), A("pT%d" % h), A("eq", lo + k, lo + k + 512), True, False)])
-                        mm([(A(D, k, k + 512), A("idb"), A(kr, c0 + lo + k, c0 + lo + k + 512), False, True)])
-                    elif par["PFIRST"]:
-                        mm([(A(D, k + j, k + 512, 16), A("nid"), pz, j == 0, False) for j in range(16)])
-                        mm([(A(D, k, k + 512), A("idb"), A(kr, c0 + lo + k, c0 + lo + k + 512), False, True)])
+                    cp(A(kr, lo, hi), src)
+                if not turned:
+                    X = tile()
+                    mm([(A(X, 0, 128), pnow(0, H), A("idb"), True, True)])
+                    if par["TURN"] == "S":
+                        act(A("pT%d" % h), A(X, 0, 128), FN.Copy, 1.0 / 2048)
                     else:
-                        mm([(A(D, k, k + 512), A("idb"), A(kr, c0 + lo + k, c0 + lo + k + 512), True, False)]
-                           + [(A(D, k + j, k + 512, 16), A("nid"), pz, False, j == 15) for j in range(16)])
+                        ts(A("pT%d" % h), A(X, 0, 128), 1.0 / 2048, OP.mult)
+                    turned = True
+                for k in range(0, hi - lo, 512):
+                    mm([(A(D, k, k + 512), A("pT%d" % h), A("eq", lo + k, lo + k + 512), True, False)])
+                    mm([(A(D, k, k + 512), A("idb"), A(kr, lo + k, lo + k + 512), False, True)])
                 act(y, A(D, 0, hi - lo), FN.Abs)
             else:
-                if lo >= spread:
-                    kinds = "".join(x[0] * int(x[1]) for x in gat) + "."
-                    run = min(k for k in range(u, len(kinds)) if kinds[k] not in "XR") - u
-                    spread = lo + 512 * max(nu, min(run, par["SPR"]))
-                    scan(A(pe, c0 + lo, c0 + spread), A("ramp", 0, spread - lo), A(wd, Y + lo, Y + spread), OP.min, OP.add)
-                tt(y, src, A(pe, c0 + lo, c0 + hi), OP.subtract)
-                if ty == "R":
-                    ts(A(rl, c0 + lo, c0 + hi), y, 0.0, OP.max)
+                wide = LANE("pe%d" % h, lo, hi)
+                if ty in "MN":
+                    if kinds[u] == ".":
+                        scan(wide, A("ramp", 0, hi - lo), A(wd, Y + lo, Y + hi), OP.min, OP.add)
+                    kf = A("kf%d" % h, lo, hi)
+                    if ty == "M":
+                        act(kf, src, FN.Identity, bias=A("cf", 8, 9))
+                    else:
+                        ts(kf, src, 256.0, OP.add)
+                    scan(A("df%d" % h, lo, hi), wide, kf, OP.max, OP.subtract)
+                else:
                     for k in range(u, u + nu):
-                        terms[k] = [(A("two"), A(rl, c0 + 512 * k, c0 + 512 * k + 512)), (A("nid"), A(wd, 512 * k, 512 * k + 512))]
+                        if kinds[k] == "." and 512 * k >= spread:
+                            spread = 512 * k + 512
+                            scan(LANE("pe%d" % h, 512 * k, spread), A("ramp", 0, 512), A(wd, Y + 512 * k, Y + spread), OP.min, OP.add)
+                        tt(A(wd, 512 * k, 512 * k + 512), IND(keyw, A("ku", i0 + 32 * k, i0 + 32 * k + 32)),
+                           LANE("pe%d" % h, 512 * k, 512 * k + 512), OP.subtract)
+                if ty in "MN":
+                    act(y, A("df%d" % h, lo, hi), FN.Abs, bias=A("cf", 8, 9))
+                elif ty == "R":
+                    ts(A(rl, lo, hi), y, 0.0, OP.max)
+                    for k in range(u, u + nu):
+                        terms[k] = [(A("two"), A(rl, 512 * k, 512 * k + 512)), (A("nid"), A(wd, 512 * k, 512 * k + 512))]
                 else:
                     act(y, y, FN.Abs)
             for k in range(u, u + nu):
+                if "q" in w and k in range(min(us + [9]), max(us + [-1]) + 1):
+                    terms[k] = None
                 got[k] = max(x for x in range(len(nodes)) if nodes[x]["rd"][:1] == keyw[1])
             u += nu
             if gi == 0:
-                if s < 2:
-                    ts(A("kc", i0, i0 + H), A("ku", i0, i0 + H), -2048.0, OP.add)
-                if h == 0 and s > 0:
-                    act(A("rr", 128 * (s - 1) + n0, 128 * (s - 1) + n0 + H), IND(A(rows[t], 0, base), lst), FN.Copy)
+                if s == 2 and h:
+                    pass
+                elif z + str(s) in par["KC"]:
+                    act(kc, A("ku", i0, i0 + H), FN.Identity, bias=A("cf", 9, 10))
+                else:
+                    ts(kc, A("ku", i0, i0 + H), -2048.0, OP.add)
             while eu[0] < len(eg) and eu[1] + int(eg[eu[0]]) <= u:
                 a, ne = eu[1], int(eg[eu[0]])
-                E = tile()
-                for k in range(ne):
-                    full = acc(A(E, 512 * k, 512 * k + 512), [(qt, A("eq", c0 + 512 * (a + k), c0 + 512 * (a + k + 1)))] + terms[a + k])
-                    if par["SPLIT"]:
+                if terms[a] is None:
+                    ef = A("ef%d" % h, 512 * a, 512 * (a + ne))
+                    scan(ef, A(wd, 512 * a, 512 * (a + ne)), LANE("qe%d" % h, 512 * a, 512 * (a + ne)), OP.max, OP.subtract)
+                    act(F4(k0 + 2 * a, k0 + 2 * (a + ne)), ef, FN.Abs, bias=A("cf", 10, 11))
+                else:
+                    E = tile()
+                    for k in range(ne):
+                        full = acc(A(E, 512 * k, 512 * k + 512), [(qt, A("eq", 512 * (a + k), 512 * (a + k + 1)))] + terms[a + k])
                         mm(full[:1])
                         nodes[-1]["after"] = [got[a + k]]
                         mm(full[1:])
-                    else:
-                        mm(full)
-                act(F4(k0 + 2 * a, k0 + 2 * (a + ne)), A(E, 0, 512 * ne), FN.Abs)
+                    act(F4(k0 + 2 * a, k0 + 2 * (a + ne)), A(E, 0, 512 * ne), FN.Abs)
                 eu = [eu[0] + 1, a + ne]
+                if z == "A":
+                    seen[eu[0]] = len(nodes) - 1
                 while su[0] < len(sg) and su[1] + int(sg[su[0]]) <= eu[1]:
                     a, ns = su[1], int(sg[su[0]])
                     mm(acc(A(Wb, 32 * a, 32 * (a + ns)), [(A("idh"), A("sth", 32 * a, 32 * (a + ns)))]
@@ -405,30 +501,37 @@ def build(g, core, T, topo, rank, phys, par=None):
                     su = [su[0] + 1, a + ns]
         ou = A("ou", k0, k0 + K)
         scan(A("sc", i0, i0 + H), A("rst%d" % (t % 2), 0, H), A(Wb, 0, H), OP.max, OP.min)
-        ts(A("oj", k0, k0 + K), A("sc", i0 + 15, i0 + H, 16), 4095, OP.bitwise_and)
-        cp(ou, A("oj", k0, k0 + K))
+        if par["OJ"]:
+            ts(A("oj", k0, k0 + K), A("sc", i0 + 15, i0 + H, 16), 4095, OP.bitwise_and)
+            cp(ou, A("oj", k0, k0 + K))
+        else:
+            ts(ou, A("sc", i0 + 15, i0 + H, 16), 4095, OP.bitwise_and)
         if h == 0 and s == 1:
             ts(A("j15", k0, k0 + K), A("sc", i0 + 15, i0 + H, 16), 15, OP.bitwise_and)
         if s < 2:
-            nm, lo = ("sela", 128 * s + n0) if h == 0 else ("selb", n0)
-            tt(A(nm, lo, lo + H), IND(A("tab", 0, top), ou), A("kc", i0, i0 + H), OP.min)
+            nm, lo = ("sela", 128 * s) if h == 0 else ("selb", 0)
+            tt(A(nm, lo, lo + H), IND(A("tab", 0, top), ou), kc, OP.min)
+            if h == 0 and s == 1:
+                tt(A("ohn"), IND(A("tab", 0, top), ou), A("nh", 128 * t, 128 * t + 128), OP.min)
             if z in par["LIST"]:
                 Wc = A(tile(), 0, H)
                 mm(acc(Wc, [(A("idb"), A("tab", 0, H)), (A("boh"), A(nm, lo, lo + H))]))
                 scan(A("vs", i0, i0 + H), A("cut", 0, H), Wc, OP.min, OP.max)
-                ts(A("vl", 16 * s + k0, 16 * s + k0 + K), A("vs", i0 + 15, i0 + H, 16), 32768.0 - 4096.0, OP.add)
+                ts(A("vl", 8 * s + 2 * k0, 8 * s + 2 * k0 + K), A("vs", i0 + 15, i0 + H, 16), 32768.0 - 4096.0, OP.add)
             else:
                 Wc = A(tile(), 0, K)
                 mm(acc(Wc, [(A("bgh", 15 - x, 143 - x), A(nm, lo + x, lo + H, 16)) for x in range(16)]))
-                ts(A("vl", 16 * s + k0, 16 * s + k0 + K), Wc, 2.0 ** -12, OP.mult, 32768.0, OP.add)
+                ts(A("vl", 8 * s + 2 * k0, 8 * s + 2 * k0 + K), Wc, 2.0 ** -12, OP.mult, 32768.0, OP.add)
             act(A(wn, Y, top, 16), IND(A(wd, 0, top), ou), FN.Abs)
         else:
             o = A("ps", L * t + i0, L * t + i0 + H)
             act(o, IND(A(wd, 0, top), ou), FN.Abs)
-            if h == 0:
-                act(A("oh", 128 + n0, 128 + n0 + H), IND(A("tab", 0, top), ou), FN.Relu, 1.0 / 4096)
+            if h == 0 and par["OH"] == "S":
+                act(A("oh", 128, 128 + H), IND(A("tab", 0, top), ou), FN.Relu, 1.0 / 4096)
+            elif h == 0:
+                ts(A("oh", 128, 128 + H), IND(A("tab", 0, top), ou), 0.0, OP.is_gt)
             dst = A("pl", L * t + i0, L * t + i0 + H)
-            sem = T.sem["ap%d" % (4 * t + i0 // 64)]
+            sem = T.sem["ap%d" % (2 * t + h)]
             a = node("G", lambda: g.remote_dma(dst[0], o[0], sem, T.sem.ls, pid1, rid1, mask1), [o], [], 1200, remote=1)
             sent[0] += ne1
             node("R", None, [], [dst], 0, sem=sem, cnt=ne_in, after=[a], lat=3500)
@@ -438,86 +541,92 @@ def build(g, core, T, topo, rank, phys, par=None):
     def early(t):
         base = B + 256 * t
         X = tile()
-        mm([(A(X, e, 256, 2), A("boh"), A("sela", 128 * e, 128 * e + 128), True, True) for e in range(2)])
-        ts(A("uh"), A(X, 0, 256), 30720.0, OP.add)
+        mm(acc(A(X, 0, 128), [(A("la"), A("sela", 0, 128)), (A("lb"), A("sela", 128, 256))]))
+        ts(A("npre"), A(X, 0, 128), A("dum", 7, 8), OP.is_equal, 3600.0, OP.mult)
+        X = tile()
         for e in range(2):
-            ts(A("ab", 8 * e, 8 * e + 8), A("vl", 16 * e, 16 * e + 8), -2048.0, OP.add)
-        tt(A("da", 0, 32, 2), A("ab"), A("dmc"), OP.subtract)
+            mm(acc(A(X, e, 256, 2), [(A("boh"), A("sela", 128 * e, 128 * e + 128)), (A("boh"), A("npre"))]))
+        if par["UH"] == "S":
+            act(A("uh"), A(X, 0, 256), FN.Identity, bias=A("dum", 8, 9))
+        else:
+            ts(A("uh"), A(X, 0, 256), 30720.0, OP.add)
+        ts(A("ab"), A("vl", 0, 16), -2048.0, OP.add)
+        for m in range(8):
+            for e in range(2):
+                at = 2 * (BLK[8] * e + BLK[m])
+                ts(A("eqw", at, at + 32 * m + 32), A("uh", 0, 32 * m + 32), A("ab", 8 * e + m, 8 * e + m + 1), OP.is_equal)
         tt(A("pre", 0, 8), A("ab", 0, 8), A("ab", 8, 16), OP.not_equal)
         ts(A("pre", 8, 16), A("j15"), 15.0, OP.is_lt, A("rst%d" % (t % 2), 0, 1), OP.mult)
         tt(A("pre", 16, 24), A("pre", 0, 8), A("pre", 8, 16), OP.mult)
         if t < NT - 1:
             for e in range(2):
-                act(A("key", base + e, base + 256, 2), IND(A("key", 0, base), A("vl", 16 * e, 16 * e + 8)), FN.Copy)
-        ts(A("oh", 0, 128), A("sela", 128, 256), -2048.0, OP.is_gt)
+                act(A("key", base + e, base + 256, 2), IND(A("key", 0, base), A("vl", 8 * e, 8 * e + 8)), FN.Copy)
+        act(A("oh", 0, 128), A("sela", 128, 256), FN.Sign, bias=up)
         X = tile()
-        mm([(A(X, 128 * k, 128 * k + 128), A(nm), A("oh", 0, 128), True, True) for k, nm in enumerate(("tle", "tgt", "tsh", "idb"))])
-        tt(A("t1", 0, 128), A(X, 0, 128), A("rr", 0, 128), OP.mult)
-        tt(A("t4", 0, 128), A(X, 128, 256), A("rr", 0, 128), OP.mult)
-        tt(A(X, 256, 384), A(X, 256, 384), A("mt", 128 * t, 128 * t + 128), OP.mult)
-        tt(A(X, 384, 512), A(X, 384, 512), A("ni", 128 * t, 128 * t + 128), OP.mult)
-        tt(A("t1", 0, 128), A(X, 256, 384), A("t1", 0, 128), OP.add)
-        tt(A("t4", 0, 128), A(X, 384, 512), A("t4", 0, 128), OP.add)
+        mm(acc(A(X, 0, 128), [(A("idh"), A("ka", 0, 128)), (A("ngt"), A("oh", 0, 128))]))
+        mm([(A(X, 128, 256), A("shh"), A("ohn"), True, False), (A(X, 128, 256), A("nsh"), A("tab", Y, Y + 128), False, False),
+            (A(X, 129, 256, 2), A("ns4"), A("oh", 1, 128, 2), False, True)])
+        act(A("t1", 0, 128), A(X, 0, 128), FN.Relu, bias=up)
+        tt(A("t1", 0, 128), A(X, 128, 256), A("t1", 0, 128), OP.add)
 
     def late(t):
         base = B + 256 * t
-        tt(A("cand"), A("sc", 15, 128, 16), A("pre", 16, 24), OP.is_lt)
-        order = [(0, 0)] + [(k, e) for k in range(1, 8) for e in range(2)] + [(0, 1)]
-        at = 0
         F = tile()
-        for x, (k, e) in enumerate(order):
-            n = 256 - 32 * k
-            ts(A("eqw", at, at + n), A("uh", 32 * k, 256), A("ab", 8 * e + k, 8 * e + k + 1), OP.is_equal, A("cand", k, k + 1), OP.mult)
-            mm([(A(F, 16 * k, 128), A("wk", 128 * k, 128 * k + 128), A("eqw", at + f, at + n, 2), x + f == 0, x + f == 16) for f in range(2)])
-            at += n
-            if x == 0:
-                tt(A("cw"), A("cand"), A("wl", 8, 16), OP.mult)
-                for u in range(0, 16, 4):
-                    mm([(A(F, m, 128, 16), A("own", 128 * m, 128 * m + 128), A("cw"), False, False) for m in range(u, u + 4)])
-        tt(A("hi"), A(F, 0, 128), A("whi"), OP.is_lt)
-        scan(A("st"), A("alt"), A("hi"), OP.max, OP.min)
+        o = 512 - BLK[7]
+
+        def blk(m, a=0, b=None):
+            return A(F, o + BLK[m] + a, o + BLK[m] + (16 * m + 16 if b is None else b))
+        parts = ((0, BLK[7]), (BLK[7], BLK[8]))
+        mm([(A(F, o + a, o + b), A("idb"), A("fix", a, b), True, False) for a, b in parts])
+        nodes[-1]["after"] = [seen[par["FAT"]]]
+        for e in range(2):
+            for f in range(2):
+                mm([(A(F, o + a, o + b), A("prs"), A("eqw", 2 * (BLK[8] * e + a) + f, 2 * (BLK[8] * e + b), 2), False, False) for a, b in parts])
+        tt(A("cand"), A("sc", 15, 128, 16), A("pre", 16, 24), OP.is_ge)
+        mm([(blk(m, 16 * m + 16, 16 * m + 17), A("prn"), A("cand", m, m + 1), False, False) for m in range(8)])
+        mm([(blk(m), A("bup"), A("oh", 128, 144 + 16 * m), False, m >= 6) for m in range(8)])
+        scan(A("bs"), A("lid", 0, BLK[8]), A(F, o, o + BLK[8]), OP.min, OP.max, -BIG)
+        tt(A("og2"), IND(A("bs"), A("end", 0, 1)), A("ab"), OP.max)
+        ts(A("so"), A("og2"), 2048.0, OP.add)
         X = tile()
-        mm([(A(X, 128 * k, 128 * k + 128), A(nm), A("oh", 128, 256), True, True) for k, nm in enumerate(("tle", "tgt"))])
-        tt(A("t1", 128, 256), A(X, 0, 128), A("rr", 128, 256), OP.mult)
-        tt(A("t4", 128, 256), A(X, 128, 256), A("rr", 128, 256), OP.mult)
-        F, X = tile(), tile()
-        mm([(A(F, 0, 16), A("nil"), A("ones", 0, 16), True, False)]
-           + [(A(F, 1, 16, 2), A("bg2", 14 - x, 142 - x), A("st", x + 1, 128, 16), False, x == 14) for x in range(0, 16, 2)])
-        mm([(A(X, e, 128, 2), A("idb"), A("st", 1, 128, 2), True, True) for e in range(2)])
-        for e in range(2):
-            scan(A("og2", 16 * e, 16 * e + 16), A(F, 0, 16), A("da", 16 * e, 16 * e + 16), OP.mult, OP.add)
-        cp(A("so"), A("og2", 1, 32, 2))
+        mm(acc(A(X, 0, 128), [(A("idh"), A("ka", 128, 256)), (A("ngt"), A("oh", 128, 256))]))
+        act(A("t1", 128, 256), A(X, 0, 128), FN.Relu, bias=up)
         tb = rows[t + 1]
-        for e in range(2):
-            tt(A(tb, base + e, base + 256, 2), A(X, 0, 128), A("t4", 128 * e, 128 * e + 128), OP.mult)
         cp(IND(A(tb), A("so")), A("t1"))
+        ts(A("cw", 0, 8), A("og2", 0, 8), float(W - 2048), OP.is_ge, 4096.0, OP.mult)
+        tt(A("cwx"), IND(A("cw", 0, 8), A("rep")), A("tab", 0, 128), OP.min)
+        X = tile()
+        mm([(A(X, 0, 256), A("idh"), A("ka"), True, False), (A(X, 0, 128), A("nih"), A("sela", 128, 256), False, False),
+            (A(X, 0, 128), A("idh"), A("ohn"), False, False), (A(X, 0, 128), A("nlt"), A("oh", 0, 128), False, False),
+            (A(X, 128, 256), A("nle"), A("oh", 128, 256), False, False)])
+        nodes[-1]["after"] = [len(nodes) - 2]
+        mm([(A(X, 128 * e, 128 * e + 128), A("nbo"), A("cwx"), False, e == 1) for e in range(2)])
+        for e in range(2):
+            act(A(tb, base + e, base + 256, 2), A(X, 128 * e, 128 * e + 128), FN.Relu, bias=A("dum", 11, 12))
         if t < NT - 1:
-            act(A("fl", 0, 64), A("st", 1, 128, 2), FN.Copy, 2.0, acc=A("zc", 0, 1))
             X = tile()
-            mm([(A(X, 0, 1), A("six"), A("zc", 0, 1), True, True)])
-            cp(A("zi", 0, 1), A(X, 0, 1))
+            mm([(A(X, 0, 8), A("ones"), A("cw", 0, 8), True, True)])
+            act(A("fl", 0, 8), A(X, 0, 8), FN.Identity, -1.0 / 4096, acc=A("zc", 0, 1), bias=A("dum", 12, 13))
+            cp(A("zi", 0, 1), A("zc", 0, 1))
             ts(A("zk", 0, 1), A("zi", 0, 1), 63, OP.bitwise_and)
             ts(A("za", 0, 1), A("zk", 0, 1), 4096.0, OP.mult)
             ts(A("rst%d" % ((t + 1) % 2), 0, 128, 16), A("rb"), A("za", 0, 1), OP.add)
         else:
-            dma("Y", T.yc[:], T[tb][:, 0:W], [A(tb, 0, W)], [], 9000)
+            dma("Y", T.yc[:, 0:base], T[tb][:, 0:base], [A(tb, 0, base)], [], 9000)
+            dma("S", T.yc[:, base:W], T[tb][:, base:W], [A(tb, base, W)], [], 3000)
 
     def copy_rows(t):
         top = B + 256 * t
         a, b = rows[t], rows[t + 1]
-        landed = [A("pl", L * (t - 1), L * t)] if t > 0 and par["COPY"] else []
-        dma("Y", T[b][:, 0:top], T[a][:, 0:top], [A(a, 0, top)] + landed, [A(b, 0, top)], 9000)
-        if t == NT - 1:
-            cp(A(b, 0, 1), A("ch0", 0, 1))
+        dma("Y", T[b][:, 0:top], T[a][:, 0:top], [A(a, 0, top)], [A(b, 0, top)], 9000)
+        cp(A(b, 0, 1), A("ch0", 0, 1))
 
     for t in range(NT):
-        for w in ORDER[t].split():
-            v = t - w.count("'")
-            w = w.strip("'")
+        for w in par["ORDER"][t].split():
             if w[0] in STREAM:
-                step(v, int(w[1]), w[0], {"": "all", "k": "kids", "r": "rest"}[w[2:]])
+                step(t, int(w[1]), w[0], {"": "all", "k": "kids", "r": "rest"}[w[2:]])
             else:
-                {"c": constants, "e": early, "l": late, "o": copy_rows}[w](v)
+                {"c": constants, "e": early, "l": late, "o": copy_rows}[w](t)
     return nodes, sent[0]
 
 
@@ -552,6 +661,10 @@ def depend(nodes):
         dd.pop(i, None)
         deps.append(dd)
     return deps
+
+
+def gaps(nodes, deps, par):
+    return [[(j, nodes[j].get("lat", 0) + (par["LAT"] if w else 0)) for j, w in dd.items()] for dd in deps]
 
 
 def place(nodes, seq, before, lat):
@@ -593,7 +706,7 @@ def ordered(n, deps, key):
 def pack(nodes, deps, key, par):
     n = len(nodes)
     lat = [d.get("lat", 0) for d in nodes]
-    before = [[(j, lat[j] + (par["LAT"] if w else 0)) for j, w in deps[i].items()] for i in range(n)]
+    before = gaps(nodes, deps, par)
     after = [[] for _ in range(n)]
     for i in range(n):
         for j, x in before[i]:
@@ -616,7 +729,7 @@ def pack(nodes, deps, key, par):
     return best
 
 
-def banks(nodes, base, start):
+def banks(nodes, base, start, par):
     deps = [dict(d) for d in base]
     users = {}
     for i, d in enumerate(nodes):
@@ -624,14 +737,16 @@ def banks(nodes, base, start):
             users.setdefault(nm.split("/")[0], {}).setdefault(int(nm.split("/")[1]), []).append(i)
     held = [[] for _ in range(8)]
     phys = {}
+    kept = par["KEPT"]
 
     def needs(js, first):
         seen, stack = set(), list(js)
+        since = min(start[f] for f in first) - 20000
         while stack:
             j = stack.pop()
             if j in first:
                 return True
-            if j not in seen and start[j] >= min(start[f] for f in first) - 1e-6:
+            if j not in seen and start[j] >= since:
                 seen.add(j)
                 stack.extend(deps[j])
         return False
@@ -641,11 +756,11 @@ def banks(nodes, base, start):
         first = set(u[0] for u in users[nm].values())
         t0 = min(start[f] for f in first)
         opts = []
-        for b in range(0, 8, n):
+        for b in ([7 - int(nm[2:])] if nm[1] == "f" else range(8 - kept, 8, n) if nm[1] == "k" else range(0, 9 - kept - n, n)):
             old = [j for k in range(n) for j in held[b + k]]
             end = max([0.0] + [start[j] + nodes[j]["cost"] for j in old])
             opts.append((max(end, t0 - 3000), b, old))
-        b = [o[1] for o in sorted(opts) if not needs(o[2], first)][0]
+        b = next(o[1] for o in sorted(opts) if not needs(o[2], first))
         phys[nm] = b
         for k in range(n):
             i = users[nm][k][0]
@@ -655,63 +770,134 @@ def banks(nodes, base, start):
     return deps, phys
 
 
-def polish(nodes, deps, start, end, par):
+def improve(nodes, deps, start, par, rng):
     n = len(nodes)
-    lat = [d.get("lat", 0) for d in nodes]
     cost = [d["cost"] for d in nodes]
+    lat = [d.get("lat", 0) for d in nodes]
     eng = [d["eng"] for d in nodes]
-    before = [[(j, cost[j] + lat[j] + (par["LAT"] if w else 0)) for j, w in deps[i].items()] for i in range(n)]
+    pre = [[(j, cost[j] + x) for j, x in b] for b in gaps(nodes, deps, par)]
+    suc = [[] for _ in range(n)]
+    for i in range(n):
+        for j, x in pre[i]:
+            suc[j].append((i, x))
     seq = sorted(range(n), key=lambda i: (start[i], i))
-    rng = numpy.random.default_rng(par["SEED"])
-    for _ in range(par["SHAKES"]):
-        a = rng.random() * end
-        p0, p1 = [int(x) for x in numpy.searchsorted([start[i] for i in seq], [a, a + par["STRETCH"]])]
-        key = dict(zip(seq[p0:p1], [float(x) for x in rng.normal(0.0, par["SHAKE"], p1 - p0)]))
-        for i in seq[p0:p1]:
-            key[i] = max([key[i] + start[i]] + [key[j] + 0.01 for j, _x in before[i] if j in key])
-        s1, e1 = start[:], 0.0
-        on, off = {e: [] for e in "VSPGYR"}, {e: [] for e in "VSPGYR"}
-        for i in seq[:p0]:
-            on[eng[i]].append(start[i])
-            off[eng[i]].append(start[i] + cost[i])
-            e1 = max(e1, start[i] + cost[i] + lat[i])
-        for i in sorted(seq[p0:p1], key=key.get) + seq[p1:]:
-            c, t0 = cost[i], 0.0
-            for j, x in before[i]:
-                if s1[j] + x > t0:
-                    t0 = s1[j] + x
-            b, e = on[eng[i]], off[eng[i]]
-            k = len(b)
-            while k > 0 and e[k - 1] > t0:
-                k -= 1
-            while k < len(b) and b[k] < t0 + c:
-                if e[k] > t0:
-                    t0 = e[k]
-                k += 1
-            b.insert(k, t0)
-            e.insert(k, t0 + c)
-            s1[i] = t0
-            if t0 + c + lat[i] > e1:
-                e1 = t0 + c + lat[i]
-        if e1 <= end:
-            start, end = s1, e1
-            seq = sorted(range(n), key=lambda i: (start[i], i))
-    return start, end
+    up, dn = [-1] * n, [-1] * n
+    last = {}
+    for i in seq:
+        if eng[i] != "R":
+            j = last.get(eng[i], -1)
+            up[i] = j
+            if j >= 0:
+                dn[j] = i
+            last[eng[i]] = i
+    r, q = [0.0] * n, [0.0] * n
+
+    def head(i, t):
+        for j, x in pre[i]:
+            if r[j] + x > t:
+                t = r[j] + x
+        return t
+
+    def tail(i, t):
+        for j, x in suc[i]:
+            if q[j] + x > t:
+                t = q[j] + x
+        return t
+
+    def heads(part):
+        for i in part:
+            j = up[i]
+            r[i] = head(i, r[j] + cost[j] if j >= 0 else 0.0)
+
+    def tails(part):
+        for i in reversed(part):
+            j = dn[i]
+            q[i] = tail(i, cost[i] + (max(q[j], lat[i]) if j >= 0 else lat[i]))
+
+    heads(seq)
+    tails(seq)
+    size = par["WINDOW"]
+    for _ in range(par["SWEEPS"]):
+        p0 = -int(rng.integers(size // 2))
+        while p0 < n:
+            lo, hi = max(p0, 0), min(p0 + size, n)
+            part = seq[lo:hi]
+            inside = set(part)
+            now = best = max(r[i] + q[i] for i in part)
+            keep = (part[:], [(i, up[i], dn[i]) for i in part])
+            tabu = {}
+            stale = 0
+            for it in range(par["MOVES"]):
+                cand = []
+                for v in part:
+                    u = up[v]
+                    if r[v] + q[v] > now - 1e-6 and u in inside and r[u] + cost[u] > r[v] - 1e-6 and u not in deps[v]:
+                        a, b = up[u], dn[v]
+                        rv = head(v, r[a] + cost[a] if a >= 0 else 0.0)
+                        ru = head(u, rv + cost[v])
+                        qu = tail(u, cost[u] + (q[b] if b >= 0 else lat[u]))
+                        qv = tail(v, cost[v] + qu)
+                        est = max(rv + qv, ru + qu)
+                        if tabu.get((v, u), -1) < it or est < best - 1e-6:
+                            cand.append((est + par["NOISE"] * rng.random(), u, v))
+                if not cand or stale > par["STALE"]:
+                    break
+                _e, u, v = min(cand)
+                a, b = up[u], dn[v]
+                up[v], dn[v], up[u], dn[u] = a, u, v, b
+                if a >= 0:
+                    dn[a] = v
+                if b >= 0:
+                    up[b] = u
+                tabu[u, v] = it + 6 + int(rng.integers(8))
+                a, b = part.index(u), part.index(v)
+                mid = part[a + 1:b]
+                dep = {u}
+                for i in mid:
+                    if up[i] in dep or any(j in dep for j in deps[i]):
+                        dep.add(i)
+                part[a:b + 1] = [i for i in mid if i not in dep] + [v, u] + [i for i in mid if i in dep]
+                heads(part[a:])
+                tails(part[:b + 1])
+                now = max(r[i] + q[i] for i in part)
+                stale += 1
+                if now < best - 1e-6:
+                    best, stale = now, 0
+                    keep = (part[:], [(i, up[i], dn[i]) for i in part])
+            for i, a, b in keep[1]:
+                up[i], dn[i] = a, b
+                if a >= 0:
+                    dn[a] = i
+                if b >= 0:
+                    up[b] = i
+            seq[lo:hi] = keep[0]
+            p0 += size // 2
+            heads(seq[lo:min(p0 + size, n)])
+            tails(seq[lo:hi])
+        heads(seq)
+        seq.sort(key=lambda i: r[i])
+        tails(seq)
+    return r[:], max(r[i] + q[i] for i in seq)
 
 
 def plan(nodes, par=None):
     par = par or PAR
     n = len(nodes)
     base = depend(nodes)
+    rng = numpy.random.default_rng(par["SEED"])
     start, _e = pack(nodes, base, list(range(n)), par)
+    start, _e = improve(nodes, base, start, par, rng)
     best = None
     for _ in range(par["PASSES"]):
-        deps, phys = banks(nodes, base, start)
-        start, end = pack(nodes, deps, start, par)
-        start, end = polish(nodes, deps, start, end, par)
+        deps, phys = banks(nodes, base, start, par)
+        start, end = place(nodes, ordered(n, deps, start), gaps(nodes, deps, par), [d.get("lat", 0) for d in nodes])
+        start, end = improve(nodes, deps, start, par, rng)
         if best is None or end < best[0]:
             best = (end, start, deps, phys)
     end, start, deps, phys = best
+    for i in range(n):
+        if "load" in nodes[i]:
+            start[i] = i - n
     order = {e: sorted((i for i in range(n) if nodes[i]["eng"] == e), key=lambda i: (start[i], i)) for e in "VSPGYR"}
     return deps, order, [start[i] + nodes[i]["cost"] + nodes[i].get("lat", 0) for i in range(n)], phys
 

import numpy
from concourse.bass import DstId, RemoteDMATransfer
from concourse.mybir import AluOpType, ActivationFunctionType

N, B, L, NT, TH = 4, 2560, 256, 4, 1240
W = B + 256 * NT
WD = W + 256
KNONE = 640.0
Y = 2048
NLOAD = 4
MEET, BIG = 16384.0, 262144.0
BLK = [8 * m * (m + 1) + 3 * m for m in range(9)]
STREAM = {"A": (0, 128), "B": (128, 128)}
CUT = {}
for _z in STREAM:
    CUT["first", _z] = "Z1 Y1 Z1 Y1|1 1 1 1|2 2"
    CUT[0, _z] = "T1 S1 R1 X1|2 1 1|2 2" if _z == "A" else "N1 S1 R1 N1|2 1 1|2 2"
    CUT[1, _z] = "X1 X1 R1 M1g|2 1 1|2 2"
    CUT[2, _z] = "X1 X1 X1 M1g|2 1 1|2 2"
ORDER = ["A0 c B0 A1 B1 e A2 B2k l B2r"] + ["A0 B0 A1 B1 e A2 B2k l B2r"] * 2 + ["o A0 B0 A1 e B1 A2 l B2"]
PAR = {"GF": 1.56, "SC": 3.5, "PEF": 0.57, "PMM": 8, "VO": 60, "SO": 75, "GO": 205, "LAT": 220, "CUT": CUT, "ORDER": ORDER,
       "TURN": "S", "LIST": "AB", "OH": "V", "UH": "S", "KC": "B0", "FAT": 1, "KEPT": 0, "SPR": 1, "TABS": 256, "QFROM": 1, "OJ": 1, "CONV": "GGGG", "Q0": "", "RL": 1.0, "DL": 0.65,
       "ROUNDS": 4, "PASSES": 7, "SEED": 2, "WINDOW": 70, "SWEEPS": 3, "MOVES": 1000, "STALE": 300, "NOISE": 400}
PLAN = []

f32, bf, f16, i32, u16 = "float32", "bfloat16", "float16", "int32", "uint16"
SCRATCH = {}
for _n, _c, _d in [
    ("chi", B, i32), ("chf", WD, f32), ("cho", WD, f32), ("key", W, bf), ("ch0", 4, f32), ("qraw", L, bf), ("hvi", 64, i32), ("hvu", 64, u16),
    ("qT0", L, bf), ("qT1", L, bf), ("qT2", L, bf), ("qT3", L, bf), ("hl1", 16, u16), ("hl2", 16, u16), ("hl3", 16, u16),
    ("tab", 2 * Y, bf), ("ramp", 1536, bf), ("pe0", Y, bf), ("pe1", Y, bf), ("kf0", Y, f16), ("kf1", Y, f16), ("df0", Y, f16), ("df1", Y, f16),
    ("rl0", Y, bf), ("rl1", Y, bf), ("kr0", Y, bf), ("kr1", Y, bf),
    ("ku", 256, u16), ("kc", 256, f16), ("vl", 32, u16),
    ("sc", 256, i32), ("oj", 16, i32), ("ou", 16, u16), ("vs", 256, f32), ("cut", 128, f32), ("sela", 256, f16), ("selb", 128, f16), ("rst0", 128, f32), ("rst1", 128, f32),
    ("ps", 1024, bf), ("pl", 1024, bf), ("pT0", 128, bf), ("pT1", 128, bf),
    ("ones", 128, bf), ("idb", 128, bf), ("nid", 128, bf), ("two", 128, bf), ("idh", 128, f16),
    ("bgb", 144, bf), ("bgh", 144, f16), ("boh", 128, f16),
    ("nle", 128, bf), ("ngt", 128, bf), ("nlt", 128, bf), ("shh", 128, f16), ("nsh", 128, bf), ("ns4", 128, bf), ("nih", 128, f16), ("sth", 128, f16),
    ("ci", 8, i32), ("cf", 12, f32), ("w1", 144, f32), ("w2", 144, f32), ("w3", 128, f32), ("w4", 128, f32), ("w5", 128, f32), ("wi", 128, i32),
    ("nh", 512, f16), ("ni", 512, f32), ("dum", 16, f32), ("rb", 8, f32),
    ("uh", 256, f16), ("eqw", 4 * BLK[8], bf), ("oh", 256, bf), ("ka", 256, f16), ("ohn", 128, f16), ("t1", 256, f32),
    ("pre", 24, f32), ("cand", 8, bf), ("cw", 16, bf), ("j15", 8, i32),
    ("prs", 128, bf), ("prn", 128, bf), ("bup", 128, bf), ("la", 128, f16), ("lb", 128, f16), ("npre", 128, f16),
    ("mas", 132, bf), ("lid", BLK[8] + 1, f32), ("fix", BLK[8], bf), ("bs", BLK[8], f32), ("end", 2, u16),
    ("eq", Y, bf), ("nbo", 128, f16), ("cwx", 128, f16), ("rep", 8, u16), ("fl", 8, f32), ("ab", 16, f32), ("og2", 16, f32), ("so", 16, u16),
    ("zc", 4, f32), ("zi", 4, i32), ("zk", 4, i32), ("za", 4, f32),
]:
    SCRATCH[_n] = ("sbuf", [128, _c], _d)
SCRATCH["fa"] = ("sbuf", [128, 16, 16, 16], bf)
for _n in range(2):
    SCRATCH["p4%d" % _n] = ("sbuf", [128, 512], bf)
    for _k, _c in (("q1", 128), ("q4", 512), ("qe", Y), ("ef", Y)):
        SCRATCH["%s%d" % (_k, _n)] = ("sbuf", [128, _c], f16)
    SCRATCH["wdA%d" % _n] = ("sbuf", [128, 2 * Y], bf)
    SCRATCH["wdB%d" % _n] = ("sbuf", [128, 2 * Y], bf)
for _n in range(4):
    SCRATCH["pm%d" % _n] = ("psum", [128, 1024], f32)
SEMAPHORES = (["sV", "sS", "sP", "sG", "ls"] + ["d%d" % k for k in range(24)] + ["aq%d" % t for t in range(1, 4)]
              + ["ap%d" % k for k in range(2 * NT)])
OP = AluOpType
FN = ActivationFunctionType


def isps(nm):
    return "#" in nm


def build(g, core, T, topo, rank, phys, par=None):
    par = par or PAR
    nodes = []
    V, S, P = g.vector, g.scalar, g.tensor
    VO, SO = par["VO"], par["SO"]

    def A(name, lo=0, hi=None, step=1):
        b, o = name, 0
        if isps(name):
            b, o = "pm%d" % (phys.get(name, 0) // 2), 512 * (phys.get(name, 0) % 2)
        if hi is None:
            hi = SCRATCH[name][1][1]
        ap = T[b][:, o + lo:o + hi] if step == 1 else T[b][:, o + lo:o + hi:step]
        n = (hi - lo + step - 1) // step
        end = lo + (n - 1) * step + 1
        if isps(name):
            return (ap, [("%s/%d" % (name, k), lo, end) for k in range(lo // 512, (end - 1) // 512 + 1)], n, f32, 0)
        return (ap, [(name, lo, end)], n, SCRATCH[name][2], 0)

    tiles = [0]

    def tile(kind=""):
        tiles[0] += 1
        return "#%s%d" % (kind, tiles[0])

    def IND(win, off):
        return (win[0].indirect(off[0]), win[1] + off[1], 16 * off[2], win[3], 1)

    def F4(a, b, ilo=None):
        ap = T.fa[:, a:b, :, :] if ilo is None else T.fa[:, a:b, ilo, :]
        return (ap, [("fa", 256 * a, 256 * b)], (b - a) * (256 if ilo is None else 16), bf, 0)

    def LANE(name, lo, hi, c=None):
        x = A(name, lo, hi) if c is None else A(name, lo + c, hi, 4)
        return (x[0], [("%s~%d" % (name, k), lo, hi) for k in (range(4) if c is None else [c])]) + x[2:]

    def node(eng, emit, rd, wr, cost, **kw):
        d = {"eng": eng, "emit": emit, "rd": [r for x in rd for r in x[1]], "wr": [r for x in wr for r in x[1]], "cost": cost}
        d.update(kw)
        if eng == "R" or "remote" in d:
            d["cost"], d["lat"] = cost * par["RL"], d.get("lat", 0) * par["RL"]
        nodes.append(d)
        return len(nodes) - 1

    def two_b(*xs):
        return all(x[3] in (bf, f16, u16) for x in xs)

    def rate(o, i, base):
        if o[4]:
            return par["SC"]
        return par["GF"] if i[4] else base

    def split_out(o):
        return ((None, o[1][:1]), (None, o[1][1:])) if o[4] else (o, (None, []))

    def val(x):
        return x[0] if isinstance(x, tuple) else x

    def cols(*xs):
        return [x for x in xs if isinstance(x, tuple)]

    def cp(o, i):
        w, r = split_out(o)
        node("V", lambda: V.tensor_copy(o[0], i[0]), [i, r], [w], VO + i[2] * rate(o, i, .5 if two_b(o, i) else 1))

    def ts(o, i, s1, op0, s2=None, op1=None):
        if op1 is None:
            em = lambda: V.tensor_scalar(o[0], i[0], val(s1), None, op0)
        else:
            em = lambda: V.tensor_scalar(o[0], i[0], val(s1), val(s2), op0, op1)
        node("V", em, [i] + cols(s1, s2), [o], VO + i[2] * rate(o, i, .5 if two_b(o, i) else 1))

    def tt(o, a, b, op):
        w, r = split_out(o)
        ps = isps(a[1][0][0]) or isps(b[1][0][0])
        node("V", lambda: V.tensor_tensor(o[0], a[0], b[0], op), [a, b, r], [w], VO + a[2] * rate(o, a, 1 if ps else 2))

    def ms(o, c):
        node("V", lambda: V.memset(o[0], c), [], [o], VO + o[2] * (.5 if two_b(o) else 1))

    def scan(o, d0, d1, op0, op1, first=0.0):
        node("V", lambda: V.tensor_tensor_scan(o[0], d0[0], d1[0], first, op0, op1), [d0, d1], [o],
             VO + o[2] * (.5 if two_b(o, d0, d1) else 1))

    def act(o, i, fn, scale=1.0, acc=None, bias=None):
        kw = {"scale": scale}
        if bias is not None:
            kw["bias"] = val(bias)
        if acc is not None:
            kw["accum_out"] = acc[0]
        node("S", lambda: S.activation(o[0], i[0], fn, **kw), [i] + cols(bias), [o] + cols(acc), SO + i[2] * rate(o, i, 1))

    def mm(lst):
        def em():
            r = None
            for o, l, x, a, b in lst:
                r = P.matmul(o[0], l[0], x[0], a, b)
            return r
        node("P", em, [e[1] for e in lst] + [e[2] for e in lst], [e[0] for e in lst],
             30 + sum(par["PMM"] + par["PEF"] * max(64, e[2][2]) * (4 if e[2][3] == f32 else 1) for e in lst))

    def acc(o, pairs):
        return [(o, l, x, k == 0, k == len(pairs) - 1) for k, (l, x) in enumerate(pairs)]

    def iota(o, pat, base, cm):
        if o[3] == i32:
            em = lambda: g.iota(o[0], pat, base, cm)
        else:
            em = lambda: g.iota(o[0], pat, base, cm, allow_small_or_imprecise_dtypes=True)
        node("G", em, [], [o], 160 + 2 * o[2])

    def asel(o, i, pat, op, base, cm, fill=0.0):
        node("G", lambda: g.affine_select(o[0], i[0], pat, op, fill, base, cm), [i], [o], par["GO"] + 2 * o[2])

    def gcopy(o, i):
        asel(o, i, [[0, o[2]]], OP.is_ge, 0, 0)

    ndma = [0]

    def dma(q, o, i, rd, wr, lat):
        sem = T.sem["d%d" % ndma[0]]
        ndma[0] += 1
        e = g.sync if q == "Y" else g.scalar
        node(q, lambda: e.dma_start(o, i).then_inc(sem, 16), rd, wr, 60, sem=sem, cnt=16, lat=lat * par["DL"])

    sent = [0]

    def peer(k):
        return T.cores[(rank + k) % N]

    dma("S", T.hvi[:], T.hv[:], [], [A("hvi")], 2500)
    dma("S", T.qraw[:], T.qs[:], [], [A("qraw")], 2500)
    cw = B // NLOAD
    for k in range(NLOAD):
        dma("Y", T.chi[:, k * cw:(k + 1) * cw], T.ch[:, k * cw:(k + 1) * cw], [], [A("chi", k * cw, (k + 1) * cw)], 2500 + 1100 * (k + 1))
    dma("Y", T.key[:, 0:B], T.kb[:], [], [A("key", 0, B)], 9000)
    keys = len(nodes) - 1
    for d in nodes:
        d["load"] = True
    ms(A("ones"), 1.0)
    ms(A("tab", Y, 2 * Y), -2048.0)
    iota(A("ci", 0, 1), [[0, 1]], 0, 1)
    asel(A("idb"), A("ones"), [[-1, 128]], OP.is_equal, 0, 1)
    iota(A("w1"), [[1, 144]], 0, 0)
    iota(A("wi"), [[256, 8], [1, 16]], 0, 16)
    for k in range(2):
        asel(A("eq", 1024 * k, 1024 * k + 1024), A("tab", Y, Y + 1024), [[1, 64], [0, 16]], OP.is_equal, 64 * k, -1)
    iota(A("ramp", 0, 512 * par["SPR"]), [[0, 32 * par["SPR"]], [256, 16]], 0, 0)
    cp(A("hvu"), A("hvi"))
    cp(A("ch0", 0, 1), A("chi", 0, 1))
    ms(A("chi", 0, 1), 0)
    for k in range(NLOAD):
        o, i = A("chf", k * cw, (k + 1) * cw), A("chi", k * cw, (k + 1) * cw)
        if par["CONV"][k] == "S":
            act(o, i, FN.Copy)
        else:
            {"V": cp, "G": gcopy}[par["CONV"][k]](o, i)
        if par["CONV"][k] != "V":
            nodes[-1]["behind"] = [keys]
    ms(A("key", 0, 1), KNONE)

    ts(A("ci", 1, 2), A("ci", 0, 1), 15, OP.bitwise_and)
    ts(A("ci", 2, 3), A("ci", 0, 1), 112, OP.bitwise_and)
    cp(A("cf", 0, 3), A("ci", 0, 3))
    pc, rowc, g16 = A("cf", 0, 1), A("cf", 1, 2), A("cf", 2, 3)
    ts(A("w2"), A("w1"), g16, OP.subtract)
    ts(A("bgb"), A("w2"), 15.0, OP.is_equal, 4096.0, OP.mult)
    if par["LIST"] != "AB":
        cp(A("bgh"), A("bgb"))
    ts(A("w3", 0, 16), A("w1", 0, 16), rowc, OP.is_equal, 6144.0, OP.mult)
    ts(A("tab", 0, 16), A("w3", 0, 16), -2048.0, OP.add)
    n = 16
    while n < Y:
        if n < par["TABS"]:
            cp(A("tab", n, 2 * n), A("tab", 0, n))
        else:
            act(A("tab", n, 2 * n), A("tab", 0, n), FN.Copy)
        n *= 2
    cp(A("idh"), A("idb"))
    X = tile()
    mm([(A(X, 128 * h, 128 * h + 128), A("qraw", 128 * h, 128 * h + 128), A("idb"), True, True) for h in range(2)])
    act(A("qT0"), A(X, 0, 256), FN.Copy, 1.0 / 2048)
    for k in range(par["KEPT"]):
        mm([(A("#f%d" % k, 0, 512), A("idb"), A("tab", Y, Y + 512), True, False)])
    act(A("nid"), A("idb"), FN.Copy, -1.0)
    act(A("two"), A("idb"), FN.Copy, 2.0)
    wds = ["wd%s%d" % (z, k) for z in STREAM for k in range(2)]
    act(A(wds[0], Y, 2 * Y), A("tab", Y, 2 * Y), FN.Copy, 0.0)
    for k, w in enumerate(wds[1:]):
        dma("Y", T[w][:, Y:2 * Y], T[wds[0]][:, Y:2 * Y], [A(wds[0], Y, 2 * Y)], [A(w, Y, 2 * Y)], 2500 + 2000 * (k + 1))
        nodes[-1]["behind"] = [keys]
    ts(A("cf", 3, 4), g16, 16.0, OP.mult)
    ts(A("sth"), A("wi"), A("cf", 3, 4), OP.subtract)
    ts(A("rb"), A("sth", 0, 128, 16), float(4096 * TH + Y), OP.add)
    ms(A("rst0"), 0.0)
    ms(A("rst1"), 0.0)
    cp(A("rst0", 0, 128, 16), A("rb"))

    ts(A("w3"), A("w2", 0, 128), 0.0, OP.is_ge)
    ts(A("w4"), A("w2", 0, 128), 16.0, OP.is_lt)
    tt(A("boh"), A("w3"), A("w4"), OP.mult)
    ms(A("cf", 8, 9), 256.0)
    ms(A("cf", 9, 10), -2048.0)
    ms(A("cf", 10, 11), 768.0)
    ms(A("cut"), 0.0)
    ms(A("cut", 0, 128, 16), -65536.0)

    def constants(t):
        act(A("nbo"), A("boh"), FN.Copy, -1.0)
        cp(A("rep"), A("w1", 0, 8))
        ms(A("dum", 11, 12), 2048.0 - 15 * 2048)
        ms(A("dum", 12, 13), 128.0)
        act(A("ngt"), A("boh"), FN.Copy, -8192.0)
        asel(A("nle"), A("ngt"), [[-1, 128]], OP.is_ge, 0, 1)
        asel(A("ngt"), A("ngt"), [[1, 128]], OP.is_gt, 0, -1)
        asel(A("nlt"), A("nle"), [[-1, 128]], OP.not_equal, 0, 1, -1.0)
        asel(A("shh"), A("boh"), [[1, 128]], OP.is_equal, -1, -1)
        act(A("nsh"), A("shh"), FN.Copy, -1.0)
        act(A("ns4"), A("shh"), FN.Copy, -4.0)
        act(A("nih"), A("idb"), FN.Copy, -1.0)
        iota(A("ni"), [[256, 4], [2, 128]], B + 1 - 2047, 0)
        act(A("nh"), A("ni"), FN.Copy)
        ts(A("ci", 4, 5), A("ci", 0, 1), 14, OP.bitwise_and)
        ts(A("ci", 5, 6), A("ci", 0, 1), 7, OP.bitwise_and)
        cp(A("cf", 5, 7), A("ci", 4, 6))
        act(A("bup"), A("boh"), FN.Copy, BIG)
        asel(A("prn"), A("bup"), [[-2, 64], [0, 2]], OP.is_ge, 0, 1)
        asel(A("prn"), A("prn"), [[2, 64], [0, 2]], OP.is_ge, 1, -1)
        act(A("prs"), A("prn"), FN.Copy, MEET / BIG)
        for a in (0, 2 * BLK[8]):
            dma("Y", T.eqw[:, a:a + 2 * BLK[8]], T[wds[0]][:, Y:Y + 2 * BLK[8]], [A(wds[0], Y, 2 * Y)], [A("eqw", a, a + 2 * BLK[8])], 9000)
            nodes[-1]["behind"] = [keys]
        ts(A("cf", 7, 8), A("cf", 5, 6), 111.0, OP.add)
        ts(A("w5"), A("w1", 0, 128), A("cf", 7, 8), OP.subtract, 0.0, OP.max)
        ts(A("mas", 0, 128), A("w5"), -2 * MEET, OP.mult, -BIG - MEET / 2, OP.add)
        ms(A("mas", 128, 129), -0.5 * BIG)
        ms(A("mas", 129, 131), -4 * BIG)
        iota(A("lid"), [[0, BLK[8] + 1]], int(16 * BIG), 0)
        ts(A("dum", 0, 1), rowc, float(W + 128 - 2048), OP.add)
        ts(A("dum", 1, 2), rowc, float(W - 2048), OP.add)
        ms(A("dum", 2, 3), -16 * BIG)
        for m in range(8):
            gcopy(A("fix", BLK[m], BLK[m + 1]), A("mas", 112 - 16 * m, 131))
            ts(A("lid", BLK[m + 1] - 2, BLK[m + 1] + 1), A("dum", 0, 3), 16.0 * m, OP.add)
        ts(A("dum", 4, 5), A("cf", 6, 7), 8.0, OP.mult, 27.0, OP.add)
        ts(A("dum", 5, 6), rowc, 8.0, OP.is_ge, 17.0, OP.add)
        ts(A("end", 0, 1), A("dum", 4, 5), A("cf", 6, 7), OP.mult, A("dum", 5, 6), OP.add)
        asel(A("la"), A("boh"), [[0, 8], [-1, 16]], OP.not_equal, 15, 0)
        act(A("lb"), A("boh"), FN.Copy, -1.0)
        act(A("lb", 15, 128, 16), A("ngt", 15, 128, 16), FN.Copy, -1.0 / 8192)
        ts(A("dum", 7, 8), rowc, 15.0, OP.is_equal, -15.0 * 2048, OP.mult)
        ms(A("dum", 8, 9), 30720.0)
        ms(A("dum", 10, 11), 2048.0)

    def masks():
        used, out = [], {}
        for t in sorted(range(1, N), key=lambda t: len(topo.engines(core, peer(t)))):
            free = [e for e in topo.engines(core, peer(t)) if e not in used][:4]
            used += free
            out[t] = sum(1 << e for e in free)
        return out

    def fused(src_of, dst_of):
        mk = masks()
        tr = []
        for t in range(1, N):
            rid, pid, _ = topo.addr(peer(t))
            tr.append(RemoteDMATransfer(dst_ids=[DstId(rid=rid, pnc=pid)], dma_engine_mask=mk[t], remote_sem=T.sem["aq%d" % t],
                                        src=src_of(t), dst=dst_of(t)))
        return g.remote_dma_fused(tr, local_sem=T.sem.ls)

    a1 = node("G", lambda: fused(lambda t: T.qT0[:], lambda t: T["qT%d" % t][:]), [A("qT0")], [], 1500, remote=1)
    a2 = node("G", lambda: fused(lambda t: T.hvu[:, 16 * t:16 * t + 16], lambda t: T["hl%d" % t][:]), [A("hvu")], [], 1500, remote=1)
    per = {t: bin(m).count("1") for t, m in masks().items()}
    sent[0] += 2 * sum(per.values())
    for t in range(1, N):
        node("R", None, [], [A("qT%d" % t), A("hl%d" % t)], 0, sem=T.sem["aq%d" % t], cnt=2 * per[t], after=[a1, a2], lat=4000)

    nxt = peer(1)
    rid1, pid1, _ = topo.addr(nxt)
    mask1 = topo.mask(core, nxt)
    ne1 = len(topo.engines(core, nxt))
    ne_in = len(topo.engines(peer(-1), core))

    rows = ["chf"] * NT + ["cho"]
    seen = {}
    up = A("dum", 10, 11)

    def step(t, s, z, part):
        base = B + 256 * t
        gs = 3 * t + s
        wd, wn = "wd%s%d" % (z, gs % 2), "wd%s%d" % (z, (gs + 1) % 2)
        i0, H = STREAM[z]
        h, k0, K = i0 // 128, i0 // 16, H // 16
        top = Y + 16 * H
        if s == 0:
            lst = A("hvu" if t == 0 else "hl%d" % t, k0, k0 + K)
        else:
            lst = A("vl", 8 * (s - 1) + 2 * k0, 8 * (s - 1) + 2 * k0 + K)
        kids = IND(A(rows[t] if t else "chi", 0, base if s else B), lst)
        if part != "rest":
            cp(A("ku", i0, i0 + H), kids)
        if part == "kids":
            return
        gat, eg, sg = [x.split() for x in par["CUT"]["first" if gs == 0 else s, z].split("|")]

        def pnow(a, b):
            if s == 0:
                return A("pl", L * (t - 1) + i0 + a, L * (t - 1) + i0 + b)
            return A(wd, Y + 16 * a, Y + 16 * b, 16)
        if s == 0 and t > 0:
            act(A(wd, Y, top, 16), pnow(0, H), FN.Copy)
        us = [k for x in ((0, 1, 2) if t else ("first",)) for k, c in enumerate(
            c for y in par["CUT"][x, z].split("|")[0].split() for c in ("q" if "q" in y else ".") * int(y[1])) if c == "q"]
        if s == 0 and us:
            a, b = 32 * min(us), 32 * max(us) + 32
            if t:
                X = tile()
                mm([(A(X, 0, b - a), A("qT%d" % t, 128 * h, 128 * h + 128), A("idb", a, b), True, True)])
                act(A("q1%d" % h, a, b), A(X, 0, b - a), FN.Identity, 2048.0, bias=A("cf", 10, 11))
            for c in range(4):
                if t:
                    gcopy(LANE("q4%d" % h, 4 * a, 4 * b, c), A("q1%d" % h, a, b))
                else:
                    act(LANE("q4%d" % h, 4 * a, 4 * b, c), A("qraw", i0 + a, i0 + b), FN.Identity, bias=A("cf", 10, 11))
            for c in range(4):
                (gcopy if t or par["Q0"] == "G" else cp)(LANE("qe%d" % h, 16 * a, 16 * b, c), LANE("q4%d" % h, 4 * a, 4 * b))
        kinds = "".join((x[2:].replace("q", "") or ".") * int(x[1]) for x in gat)
        for ch in sorted(set(kinds) - set(".")):
            a, b = 32 * kinds.index(ch), 32 * (kinds.rindex(ch) + 1)
            if ch in "hi":
                scan(LANE("p4%d" % h, 4 * a, 4 * b), A("ramp", 0, 16 * (b - a), 4), A(wd, Y + 16 * a, Y + 16 * b, 4), OP.min, OP.add)
            for c in range(0 if ch in "hi" else 4):
                gcopy(LANE("p4%d" % h, 4 * a, 4 * b, c), pnow(a, b))
            for c in range(4):
                gcopy(LANE("pe%d" % h, 16 * a, 16 * b, c), LANE("p4%d" % h, 4 * a, 4 * b))
        keyw = A("key", 0, base)
        kc = A("ka", 128 * s - 128, 128 * s) if h == 0 and s else A("kc", i0, i0 + H)
        qt = A("qT%d" % t, 128 * h, 128 * h + 128)
        kr, rl = ["%s%d" % (x, h) for x in ("kr", "rl")]
        Wb = tile()
        terms, got = {}, {}
        eu, su = [0, 0], [0, 0]
        u = spread = 0
        turned = False
        for gi, w in enumerate(gat):
            ty, nu = w[0], int(w[1])
            lo, hi = 512 * u, 512 * (u + nu)
            y = A(wd, lo, hi)
            src = IND(keyw, A("ku", i0 + 32 * u, i0 + 32 * (u + nu)))
            for k in range(u, u + nu):
                terms[k] = [(A("idb"), A(wd, 512 * k, 512 * k + 512))]
            if ty == "Z":
                cp(y, src)
            elif ty == "Y":
                act(y, src, FN.Copy)
            elif ty in "ST":
                D = tile()
                if ty == "S":
                    act(A(kr, lo, hi), src, FN.Copy)
                else:
                    cp(A(kr, lo, hi), src)
                if not turned:
                    X = tile()
                    mm([(A(X, 0, 128), pnow(0, H), A("idb"), True, True)])
                    if par["TURN"] == "S":
                        act(A("pT%d" % h), A(X, 0, 128), FN.Copy, 1.0 / 2048)
                    else:
                        ts(A("pT%d" % h), A(X, 0, 128), 1.0 / 2048, OP.mult)
                    turned = True
                for k in range(0, hi - lo, 512):
                    mm([(A(D, k, k + 512), A("pT%d" % h), A("eq", lo + k, lo + k + 512), True, False)])
                    mm([(A(D, k, k + 512), A("idb"), A(kr, lo + k, lo + k + 512), False, True)])
                act(y, A(D, 0, hi - lo), FN.Abs)
            else:
                wide = LANE("pe%d" % h, lo, hi)
                if ty in "MN":
                    if kinds[u] == ".":
                        scan(wide, A("ramp", 0, hi - lo), A(wd, Y + lo, Y + hi), OP.min, OP.add)
                    kf = A("kf%d" % h, lo, hi)
                    if ty == "M":
                        act(kf, src, FN.Identity, bias=A("cf", 8, 9))
                    else:
                        ts(kf, src, 256.0, OP.add)
                    scan(A("df%d" % h, lo, hi), wide, kf, OP.max, OP.subtract)
                else:
                    for k in range(u, u + nu):
                        if kinds[k] == "." and 512 * k >= spread:
                            spread = 512 * k + 512
                            scan(LANE("pe%d" % h, 512 * k, spread), A("ramp", 0, 512), A(wd, Y + 512 * k, Y + spread), OP.min, OP.add)
                        tt(A(wd, 512 * k, 512 * k + 512), IND(keyw, A("ku", i0 + 32 * k, i0 + 32 * k + 32)),
                           LANE("pe%d" % h, 512 * k, 512 * k + 512), OP.subtract)
                if ty in "MN":
                    act(y, A("df%d" % h, lo, hi), FN.Abs, bias=A("cf", 8, 9))
                elif ty == "R":
                    ts(A(rl, lo, hi), y, 0.0, OP.max)
                    for k in range(u, u + nu):
                        terms[k] = [(A("two"), A(rl, 512 * k, 512 * k + 512)), (A("nid"), A(wd, 512 * k, 512 * k + 512))]
                else:
                    act(y, y, FN.Abs)
            for k in range(u, u + nu):
                if "q" in w and k in range(min(us + [9]), max(us + [-1]) + 1):
                    terms[k] = None
                got[k] = max(x for x in range(len(nodes)) if nodes[x]["rd"][:1] == keyw[1])
            u += nu
            if gi == 0:
                if s == 2 and h:
                    pass
                elif z + str(s) in par["KC"]:
                    act(kc, A("ku", i0, i0 + H), FN.Identity, bias=A("cf", 9, 10))
                else:
                    ts(kc, A("ku", i0, i0 + H), -2048.0, OP.add)
            while eu[0] < len(eg) and eu[1] + int(eg[eu[0]]) <= u:
                a, ne = eu[1], int(eg[eu[0]])
                if terms[a] is None:
                    ef = A("ef%d" % h, 512 * a, 512 * (a + ne))
                    scan(ef, A(wd, 512 * a, 512 * (a + ne)), LANE("qe%d" % h, 512 * a, 512 * (a + ne)), OP.max, OP.subtract)
                    act(F4(k0 + 2 * a, k0 + 2 * (a + ne)), ef, FN.Abs, bias=A("cf", 10, 11))
                else:
                    E = tile()
                    for k in range(ne):
                        full = acc(A(E, 512 * k, 512 * k + 512), [(qt, A("eq", 512 * (a + k), 512 * (a + k + 1)))] + terms[a + k])
                        mm(full[:1])
                        nodes[-1]["after"] = [got[a + k]]
                        mm(full[1:])
                    act(F4(k0 + 2 * a, k0 + 2 * (a + ne)), A(E, 0, 512 * ne), FN.Abs)
                eu = [eu[0] + 1, a + ne]
                if z == "A":
                    seen[eu[0]] = len(nodes) - 1
                while su[0] < len(sg) and su[1] + int(sg[su[0]]) <= eu[1]:
                    a, ns = su[1], int(sg[su[0]])
                    mm(acc(A(Wb, 32 * a, 32 * (a + ns)), [(A("idh"), A("sth", 32 * a, 32 * (a + ns)))]
                           + [(A("bgb", 15 - x, 143 - x), F4(k0 + 2 * a, k0 + 2 * (a + ns), x)) for x in range(16)]))
                    su = [su[0] + 1, a + ns]
        ou = A("ou", k0, k0 + K)
        scan(A("sc", i0, i0 + H), A("rst%d" % (t % 2), 0, H), A(Wb, 0, H), OP.max, OP.min)
        if par["OJ"]:
            ts(A("oj", k0, k0 + K), A("sc", i0 + 15, i0 + H, 16), 4095, OP.bitwise_and)
            cp(ou, A("oj", k0, k0 + K))
        else:
            ts(ou, A("sc", i0 + 15, i0 + H, 16), 4095, OP.bitwise_and)
        if h == 0 and s == 1:
            ts(A("j15", k0, k0 + K), A("sc", i0 + 15, i0 + H, 16), 15, OP.bitwise_and)
        if s < 2:
            nm, lo = ("sela", 128 * s) if h == 0 else ("selb", 0)
            tt(A(nm, lo, lo + H), IND(A("tab", 0, top), ou), kc, OP.min)
            if h == 0 and s == 1:
                tt(A("ohn"), IND(A("tab", 0, top), ou), A("nh", 128 * t, 128 * t + 128), OP.min)
            if z in par["LIST"]:
                Wc = A(tile(), 0, H)
                mm(acc(Wc, [(A("idb"), A("tab", 0, H)), (A("boh"), A(nm, lo, lo + H))]))
                scan(A("vs", i0, i0 + H), A("cut", 0, H), Wc, OP.min, OP.max)
                ts(A("vl", 8 * s + 2 * k0, 8 * s + 2 * k0 + K), A("vs", i0 + 15, i0 + H, 16), 32768.0 - 4096.0, OP.add)
            else:
                Wc = A(tile(), 0, K)
                mm(acc(Wc, [(A("bgh", 15 - x, 143 - x), A(nm, lo + x, lo + H, 16)) for x in range(16)]))
                ts(A("vl", 8 * s + 2 * k0, 8 * s + 2 * k0 + K), Wc, 2.0 ** -12, OP.mult, 32768.0, OP.add)
            act(A(wn, Y, top, 16), IND(A(wd, 0, top), ou), FN.Abs)
        else:
            o = A("ps", L * t + i0, L * t + i0 + H)
            act(o, IND(A(wd, 0, top), ou), FN.Abs)
            if h == 0 and par["OH"] == "S":
                act(A("oh", 128, 128 + H), IND(A("tab", 0, top), ou), FN.Relu, 1.0 / 4096)
            elif h == 0:
                ts(A("oh", 128, 128 + H), IND(A("tab", 0, top), ou), 0.0, OP.is_gt)
            dst = A("pl", L * t + i0, L * t + i0 + H)
            sem = T.sem["ap%d" % (2 * t + h)]
            a = node("G", lambda: g.remote_dma(dst[0], o[0], sem, T.sem.ls, pid1, rid1, mask1), [o], [], 1200, remote=1)
            sent[0] += ne1
            node("R", None, [], [dst], 0, sem=sem, cnt=ne_in, after=[a], lat=3500)
            if t == NT - 1:
                dma("Y", T.yp[:, i0:i0 + H], dst[0], [dst], [], 2500)

    def early(t):
        base = B + 256 * t
        X = tile()
        mm(acc(A(X, 0, 128), [(A("la"), A("sela", 0, 128)), (A("lb"), A("sela", 128, 256))]))
        ts(A("npre"), A(X, 0, 128), A("dum", 7, 8), OP.is_equal, 3600.0, OP.mult)
        X = tile()
        for e in range(2):
            mm(acc(A(X, e, 256, 2), [(A("boh"), A("sela", 128 * e, 128 * e + 128)), (A("boh"), A("npre"))]))
        if par["UH"] == "S":
            act(A("uh"), A(X, 0, 256), FN.Identity, bias=A("dum", 8, 9))
        else:
            ts(A("uh"), A(X, 0, 256), 30720.0, OP.add)
        ts(A("ab"), A("vl", 0, 16), -2048.0, OP.add)
        for m in range(8):
            for e in range(2):
                at = 2 * (BLK[8] * e + BLK[m])
                ts(A("eqw", at, at + 32 * m + 32), A("uh", 0, 32 * m + 32), A("ab", 8 * e + m, 8 * e + m + 1), OP.is_equal)
        tt(A("pre", 0, 8), A("ab", 0, 8), A("ab", 8, 16), OP.not_equal)
        ts(A("pre", 8, 16), A("j15"), 15.0, OP.is_lt, A("rst%d" % (t % 2), 0, 1), OP.mult)
        tt(A("pre", 16, 24), A("pre", 0, 8), A("pre", 8, 16), OP.mult)
        if t < NT - 1:
            for e in range(2):
                act(A("key", base + e, base + 256, 2), IND(A("key", 0, base), A("vl", 8 * e, 8 * e + 8)), FN.Copy)
        act(A("oh", 0, 128), A("sela", 128, 256), FN.Sign, bias=up)
        X = tile()
        mm(acc(A(X, 0, 128), [(A("idh"), A("ka", 0, 128)), (A("ngt"), A("oh", 0, 128))]))
        mm([(A(X, 128, 256), A("shh"), A("ohn"), True, False), (A(X, 128, 256), A("nsh"), A("tab", Y, Y + 128), False, False),
            (A(X, 129, 256, 2), A("ns4"), A("oh", 1, 128, 2), False, True)])
        act(A("t1", 0, 128), A(X, 0, 128), FN.Relu, bias=up)
        tt(A("t1", 0, 128), A(X, 128, 256), A("t1", 0, 128), OP.add)

    def late(t):
        base = B + 256 * t
        F = tile()
        o = 512 - BLK[7]

        def blk(m, a=0, b=None):
            return A(F, o + BLK[m] + a, o + BLK[m] + (16 * m + 16 if b is None else b))
        parts = ((0, BLK[7]), (BLK[7], BLK[8]))
        mm([(A(F, o + a, o + b), A("idb"), A("fix", a, b), True, False) for a, b in parts])
        nodes[-1]["after"] = [seen[par["FAT"]]]
        for e in range(2):
            for f in range(2):
                mm([(A(F, o + a, o + b), A("prs"), A("eqw", 2 * (BLK[8] * e + a) + f, 2 * (BLK[8] * e + b), 2), False, False) for a, b in parts])
        tt(A("cand"), A("sc", 15, 128, 16), A("pre", 16, 24), OP.is_ge)
        mm([(blk(m, 16 * m + 16, 16 * m + 17), A("prn"), A("cand", m, m + 1), False, False) for m in range(8)])
        mm([(blk(m), A("bup"), A("oh", 128, 144 + 16 * m), False, m >= 6) for m in range(8)])
        scan(A("bs"), A("lid", 0, BLK[8]), A(F, o, o + BLK[8]), OP.min, OP.max, -BIG)
        tt(A("og2"), IND(A("bs"), A("end", 0, 1)), A("ab"), OP.max)
        ts(A("so"), A("og2"), 2048.0, OP.add)
        X = tile()
        mm(acc(A(X, 0, 128), [(A("idh"), A("ka", 128, 256)), (A("ngt"), A("oh", 128, 256))]))
        act(A("t1", 128, 256), A(X, 0, 128), FN.Relu, bias=up)
        tb = rows[t + 1]
        cp(IND(A(tb), A("so")), A("t1"))
        ts(A("cw", 0, 8), A("og2", 0, 8), float(W - 2048), OP.is_ge, 4096.0, OP.mult)
        tt(A("cwx"), IND(A("cw", 0, 8), A("rep")), A("tab", 0, 128), OP.min)
        X = tile()
        mm([(A(X, 0, 256), A("idh"), A("ka"), True, False), (A(X, 0, 128), A("nih"), A("sela", 128, 256), False, False),
            (A(X, 0, 128), A("idh"), A("ohn"), False, False), (A(X, 0, 128), A("nlt"), A("oh", 0, 128), False, False),
            (A(X, 128, 256), A("nle"), A("oh", 128, 256), False, False)])
        nodes[-1]["after"] = [len(nodes) - 2]
        mm([(A(X, 128 * e, 128 * e + 128), A("nbo"), A("cwx"), False, e == 1) for e in range(2)])
        for e in range(2):
            act(A(tb, base + e, base + 256, 2), A(X, 128 * e, 128 * e + 128), FN.Relu, bias=A("dum", 11, 12))
        if t < NT - 1:
            X = tile()
            mm([(A(X, 0, 8), A("ones"), A("cw", 0, 8), True, True)])
            act(A("fl", 0, 8), A(X, 0, 8), FN.Identity, -1.0 / 4096, acc=A("zc", 0, 1), bias=A("dum", 12, 13))
            cp(A("zi", 0, 1), A("zc", 0, 1))
            ts(A("zk", 0, 1), A("zi", 0, 1), 63, OP.bitwise_and)
            ts(A("za", 0, 1), A("zk", 0, 1), 4096.0, OP.mult)
            ts(A("rst%d" % ((t + 1) % 2), 0, 128, 16), A("rb"), A("za", 0, 1), OP.add)
        else:
            dma("Y", T.yc[:, 0:base], T[tb][:, 0:base], [A(tb, 0, base)], [], 9000)
            dma("S", T.yc[:, base:W], T[tb][:, base:W], [A(tb, base, W)], [], 3000)

    def copy_rows(t):
        top = B + 256 * t
        a, b = rows[t], rows[t + 1]
        dma("Y", T[b][:, 0:top], T[a][:, 0:top], [A(a, 0, top)], [A(b, 0, top)], 9000)
        cp(A(b, 0, 1), A("ch0", 0, 1))

    for t in range(NT):
        for w in par["ORDER"][t].split():
            if w[0] in STREAM:
                step(t, int(w[1]), w[0], {"": "all", "k": "kids", "r": "rest"}[w[2:]])
            else:
                {"c": constants, "e": early, "l": late, "o": copy_rows}[w](t)
    return nodes, sent[0]


def depend(nodes):
    hist = {}
    deps = []
    for i, d in enumerate(nodes):
        dd = {}
        for regs, w in ((d["rd"], False), (d["wr"], True)):
            for nm, lo, hi in regs:
                ps = isps(nm)
                for j, lo2, hi2, w2 in hist.get(nm, []):
                    same = nodes[j]["eng"] == d["eng"] and "sem" not in nodes[j]
                    if ps and not same:
                        dd[j] = True
                    elif ps:
                        dd[j] = dd.get(j, False) or (d["eng"] != "P" and (w2 or w) and lo < hi2 and lo2 < hi)
                    elif lo < hi2 and lo2 < hi and (w or w2):
                        dd[j] = True
        for j in d.get("after", []):
            dd[j] = False
        for j in d.get("behind", []):
            dd[j] = True
        for regs, w in ((d["rd"], False), (d["wr"], True)):
            for nm, lo, hi in sorted(set(regs)):
                h = hist.setdefault(nm, [])
                if isps(nm):
                    h[:] = [e for e in h if nodes[e[0]]["eng"] == d["eng"]]
                elif w:
                    h[:] = [e for e in h if not (lo <= e[1] and e[2] <= hi) or e[0] == i]
                h.append((i, lo, hi, w))
        dd.pop(i, None)
        deps.append(dd)
    return deps


def gaps(nodes, deps, par):
    return [[(j, nodes[j].get("lat", 0) + (par["LAT"] if w else 0)) for j, w in dd.items()] for dd in deps]


def place(nodes, seq, before, lat):
    busy = {e: [] for e in "VSPGYR"}
    start = [0.0] * len(nodes)
    for i in seq:
        c = nodes[i]["cost"]
        t0 = max([0.0] + [start[j] + nodes[j]["cost"] + x for j, x in before[i]])
        iv = busy[nodes[i]["eng"]]
        k = len(iv)
        while k > 0 and iv[k - 1][1] > t0:
            k -= 1
        while k < len(iv) and iv[k][0] < t0 + c:
            t0 = max(t0, iv[k][1])
            k += 1
        iv.insert(k, (t0, t0 + c))
        start[i] = t0
    return start, max(start[i] + nodes[i]["cost"] + lat[i] for i in seq)


def ordered(n, deps, key):
    seq, seen = [], set()
    for r in sorted(range(n), key=lambda i: (key[i], i)):
        stack = [r]
        while stack:
            i = stack[-1]
            todo = [j for j in deps[i] if j not in seen]
            if i in seen:
                stack.pop()
            elif todo:
                stack.append(min(todo, key=lambda j: (key[j], j)))
            else:
                seen.add(i)
                seq.append(i)
                stack.pop()
    return seq


def pack(nodes, deps, key, par):
    n = len(nodes)
    lat = [d.get("lat", 0) for d in nodes]
    before = gaps(nodes, deps, par)
    after = [[] for _ in range(n)]
    for i in range(n):
        for j, x in before[i]:
            after[j].append((i, x))
    for i in range(n):
        if not after[i]:
            after[i].append((n, lat[i]))
    ext = nodes + [{"eng": "R", "cost": 0}]
    seq = ordered(n, deps, key)
    best = None
    for _ in range(par["ROUNDS"]):
        start, end = place(nodes, seq, before, lat)
        if best is None or end < best[1]:
            best = (start, end)
        pos = {i: k for k, i in enumerate(seq)}
        rev = sorted(range(n), key=lambda i: (-start[i] - nodes[i]["cost"], -pos[i]))
        back, _e = place(ext, [n] + rev, after + [[]], lat + [0])
        pos = {i: k for k, i in enumerate(rev)}
        seq = sorted(range(n), key=lambda i: (-back[i] - nodes[i]["cost"], -pos[i]))
    return best


def banks(nodes, base, start, par):
    deps = [dict(d) for d in base]
    users = {}
    for i, d in enumerate(nodes):
        for nm in sorted(set(r[0] for r in d["rd"] + d["wr"] if isps(r[0]))):
            users.setdefault(nm.split("/")[0], {}).setdefault(int(nm.split("/")[1]), []).append(i)
    held = [[] for _ in range(8)]
    phys = {}
    kept = par["KEPT"]

    def needs(js, first):
        seen, stack = set(), list(js)
        since = min(start[f] for f in first) - 20000
        while stack:
            j = stack.pop()
            if j in first:
                return True
            if j not in seen and start[j] >= since:
                seen.add(j)
                stack.extend(deps[j])
        return False

    for nm in sorted(users, key=lambda nm: min((start[u[0]], u[0]) for u in users[nm].values())):
        n = len(users[nm])
        first = set(u[0] for u in users[nm].values())
        t0 = min(start[f] for f in first)
        opts = []
        for b in ([7 - int(nm[2:])] if nm[1] == "f" else range(8 - kept, 8, n) if nm[1] == "k" else range(0, 9 - kept - n, n)):
            old = [j for k in range(n) for j in held[b + k]]
            end = max([0.0] + [start[j] + nodes[j]["cost"] for j in old])
            opts.append((max(end, t0 - 3000), b, old))
        b = next(o[1] for o in sorted(opts) if not needs(o[2], first))
        phys[nm] = b
        for k in range(n):
            i = users[nm][k][0]
            for j in held[b + k]:
                deps[i][j] = deps[i].get(j, False) or not (nodes[i]["eng"] == "P" and nodes[j]["eng"] == "P")
            held[b + k] = users[nm][k]
    return deps, phys


def improve(nodes, deps, start, par, rng):
    n = len(nodes)
    cost = [d["cost"] for d in nodes]
    lat = [d.get("lat", 0) for d in nodes]
    eng = [d["eng"] for d in nodes]
    pre = [[(j, cost[j] + x) for j, x in b] for b in gaps(nodes, deps, par)]
    suc = [[] for _ in range(n)]
    for i in range(n):
        for j, x in pre[i]:
            suc[j].append((i, x))
    seq = sorted(range(n), key=lambda i: (start[i], i))
    up, dn = [-1] * n, [-1] * n
    last = {}
    for i in seq:
        if eng[i] != "R":
            j = last.get(eng[i], -1)
            up[i] = j
            if j >= 0:
                dn[j] = i
            last[eng[i]] = i
    r, q = [0.0] * n, [0.0] * n

    def head(i, t):
        for j, x in pre[i]:
            if r[j] + x > t:
                t = r[j] + x
        return t

    def tail(i, t):
        for j, x in suc[i]:
            if q[j] + x > t:
                t = q[j] + x
        return t

    def heads(part):
        for i in part:
            j = up[i]
            r[i] = head(i, r[j] + cost[j] if j >= 0 else 0.0)

    def tails(part):
        for i in reversed(part):
            j = dn[i]
            q[i] = tail(i, cost[i] + (max(q[j], lat[i]) if j >= 0 else lat[i]))

    heads(seq)
    tails(seq)
    size = par["WINDOW"]
    for _ in range(par["SWEEPS"]):
        p0 = -int(rng.integers(size // 2))
        while p0 < n:
            lo, hi = max(p0, 0), min(p0 + size, n)
            part = seq[lo:hi]
            inside = set(part)
            now = best = max(r[i] + q[i] for i in part)
            keep = (part[:], [(i, up[i], dn[i]) for i in part])
            tabu = {}
            stale = 0
            for it in range(par["MOVES"]):
                cand = []
                for v in part:
                    u = up[v]
                    if r[v] + q[v] > now - 1e-6 and u in inside and r[u] + cost[u] > r[v] - 1e-6 and u not in deps[v]:
                        a, b = up[u], dn[v]
                        rv = head(v, r[a] + cost[a] if a >= 0 else 0.0)
                        ru = head(u, rv + cost[v])
                        qu = tail(u, cost[u] + (q[b] if b >= 0 else lat[u]))
                        qv = tail(v, cost[v] + qu)
                        est = max(rv + qv, ru + qu)
                        if tabu.get((v, u), -1) < it or est < best - 1e-6:
                            cand.append((est + par["NOISE"] * rng.random(), u, v))
                if not cand or stale > par["STALE"]:
                    break
                _e, u, v = min(cand)
                a, b = up[u], dn[v]
                up[v], dn[v], up[u], dn[u] = a, u, v, b
                if a >= 0:
                    dn[a] = v
                if b >= 0:
                    up[b] = u
                tabu[u, v] = it + 6 + int(rng.integers(8))
                a, b = part.index(u), part.index(v)
                mid = part[a + 1:b]
                dep = {u}
                for i in mid:
                    if up[i] in dep or any(j in dep for j in deps[i]):
                        dep.add(i)
                part[a:b + 1] = [i for i in mid if i not in dep] + [v, u] + [i for i in mid if i in dep]
                heads(part[a:])
                tails(part[:b + 1])
                now = max(r[i] + q[i] for i in part)
                stale += 1
                if now < best - 1e-6:
                    best, stale = now, 0
                    keep = (part[:], [(i, up[i], dn[i]) for i in part])
            for i, a, b in keep[1]:
                up[i], dn[i] = a, b
                if a >= 0:
                    dn[a] = i
                if b >= 0:
                    up[b] = i
            seq[lo:hi] = keep[0]
            p0 += size // 2
            heads(seq[lo:min(p0 + size, n)])
            tails(seq[lo:hi])
        heads(seq)
        seq.sort(key=lambda i: r[i])
        tails(seq)
    return r[:], max(r[i] + q[i] for i in seq)


def plan(nodes, par=None):
    par = par or PAR
    n = len(nodes)
    base = depend(nodes)
    rng = numpy.random.default_rng(par["SEED"])
    start, _e = pack(nodes, base, list(range(n)), par)
    start, _e = improve(nodes, base, start, par, rng)
    best = None
    for _ in range(par["PASSES"]):
        deps, phys = banks(nodes, base, start, par)
        start, end = place(nodes, ordered(n, deps, start), gaps(nodes, deps, par), [d.get("lat", 0) for d in nodes])
        start, end = improve(nodes, deps, start, par, rng)
        if best is None or end < best[0]:
            best = (end, start, deps, phys)
    end, start, deps, phys = best
    for i in range(n):
        if "load" in nodes[i]:
            start[i] = i - n
    order = {e: sorted((i for i in range(n) if nodes[i]["eng"] == e), key=lambda i: (start[i], i)) for e in "VSPGYR"}
    return deps, order, [start[i] + nodes[i]["cost"] + nodes[i].get("lat", 0) for i in range(n)], phys


def rank_program(g, core, T, topo):
    rank = T.rank_of(core)
    if rank is None:
        return
    if not PLAN:
        PLAN.append(plan(build(g, core, T, topo, rank, {})[0]))
    deps, order, fin, phys = PLAN[0]
    nodes, sent = build(g, core, T, topo, rank, phys)
    n = len(nodes)
    queue = {"V": g.vector, "S": g.scalar, "P": g.tensor, "G": g, "Y": g.sync}
    esem = {"V": T.sem.sV, "S": T.sem.sS, "P": T.sem.sP, "G": T.sem.sG}
    pos = {i: k for e in order for k, i in enumerate(order[e])}
    lane = [("n%d" % i if "sem" in d else d["eng"]) for i, d in enumerate(nodes)]
    known = {e: {} for e in order}
    behind, waits = {}, {}
    for i in sorted(range(n), key=lambda i: (fin[i] - nodes[i].get("lat", 0) - nodes[i]["cost"], i)):
        kn = known[nodes[i]["eng"]]
        waits[i] = []
        if nodes[i]["eng"] != "R":
            for j in sorted((j for j, w in deps[i].items() if w), key=lambda j: -fin[j]):
                if kn.get(lane[j], -1) < pos[j]:
                    waits[i].append(j)
                    kn[lane[j]] = pos[j]
                    for k, p in behind[j].items():
                        kn[k] = max(kn.get(k, -1), p)
            behind[i] = dict(kn)
        else:
            behind[i] = {}
    need = set(j for i in waits for j in waits[i])
    mark = {}
    for e in esem:
        c = 0
        for i in order[e]:
            if "sem" not in nodes[i] and i in need:
                c += 1
                mark[i] = (esem[e], c)
    for i, d in enumerate(nodes):
        if "sem" in d:
            mark[i] = (d["sem"], d["cnt"])
    for e in queue:
        for i in order[e]:
            for j in waits[i]:
                queue[e].wait_ge(*mark[j])
            r = nodes[i]["emit"]()
            if i in mark and "sem" not in nodes[i]:
                r.then_inc(mark[i][0], 1)
    for i, d in enumerate(nodes):
        if "sem" in d and i not in need:
            g.wait_ge(d["sem"], d["cnt"])
    g.wait_ge(T.sem.ls, sent)
